import numpy as np, ml_dtypes
CORES = [35,38,43,46]
N = 4
import mx_ref
BF = ml_dtypes.bfloat16
def entries(a):
    return np.ascontiguousarray(a.T).reshape(-1)
def table(e):
    return np.ascontiguousarray(np.reshape(e, (-1, 16)).T).astype(np.int32)
def gcols(t, e):
    v = np.concatenate([t.reshape(8, 16, -1, 4), np.zeros((8, 16, 1, 4), BF)], axis=2)
    return np.ascontiguousarray(np.stack([v[g][:, e[g]] for g in range(8)])).reshape(128, -1)
def tile(rs):
    return np.stack(rs, axis=2).reshape(128, -1).astype(BF)
def pick(q, e):
    c = np.concatenate([q[0].reshape(128, -1, 4), np.zeros((128, 1, 4), np.uint8)], axis=1); s = np.concatenate([q[1], np.ones((16, 1), np.uint8)], axis=1)
    return (np.ascontiguousarray(c[:, e].reshape(128, -1)), np.ascontiguousarray(s[:, e]))
def join(*qs):
    return (np.concatenate([q[0] for q in qs], axis=1), np.concatenate([q[1] for q in qs], axis=1))
def put(q, e, v):
    c, s = q[0].reshape(128, -1, 4).copy(), q[1].copy(); c[:, e] = v[0].reshape(128, -1, 4); s[:, e] = v[1]
    return (c.reshape(128, -1), s)
def pk(c, s):
    return (np.ascontiguousarray(c), mx_ref.live(s))
def emit(q):
    return q[0], q[1]
def packed(v, rng):
    q = [mx_ref.quantize(np.ascontiguousarray(v[r])) for r in range(N)]
    return np.stack([a for a, b in q]), np.stack([mx_ref.plane(b, rng) for a, b in q])
def values_of_codes():
    e, c = np.zeros((128, 128, 4), np.float32), np.zeros((128, 2, 4), np.uint8)
    e[np.arange(128), np.arange(128), 0] = 1
    c[:127, :, 0] = np.arange(256).reshape(2, 128).T[:127]
    return mx_ref.matmul(mx_ref.quantize(e.reshape(128, 512).astype(BF)), (c.reshape(128, 8), np.full((16, 2), 127, np.uint8))).T.reshape(-1).astype(np.float64)
CODE_VALUE, SCALE_VALUE = values_of_codes(), 2.0 ** (np.arange(256) - 127.0)
def decode(q):
    return (CODE_VALUE[q[0]].reshape(16, 8, -1, 4) * SCALE_VALUE[q[1]][:, None, :, None] + 0.0).reshape(128, -1).astype(np.float32)
def f(rng, *shape):
    return mx_ref.flush((rng.standard_normal(shape, dtype=np.float32) * np.exp2(rng.integers(-2, 3, shape[:-1] + (1,)))).astype(BF))
def wide(rng, *shape, cols=0):
    v = rng.standard_normal(shape, dtype=np.float32) * np.exp2(rng.integers(-12, 13, shape)).astype(np.float32)
    if cols: v *= np.repeat(np.exp2(rng.integers(-cols, cols + 1, shape[:-2] + (1, shape[-1] // 4))) * (rng.random(shape[:-2] + (1, shape[-1] // 4)) > 0.0625), 4, axis=-1).astype(np.float32)
    return mx_ref.flush(v.astype(BF))
C, K = 384, 160
PARTNER = [1, 2, 3]
LOCAL = np.arange(C) % 32
ROOT = np.arange(C) - LOCAL
PLACE = np.arange(32)
def big(v):
    v = v.astype(np.float32)
    v[np.abs(v) < np.float32(2.0 ** -16)] = 0
    return v.astype(BF)
def numbers_of(rng):
    return {"x": big(f(rng, N, 128, 4 * C)), "u": np.array(f(rng, N, 128, 512)), "v": np.array(f(rng, N, 128, 512))}
def parents(rng):
    return {k: np.stack([table(ROOT + rng.integers(0, np.maximum(LOCAL, 1), C)) for r in range(N)]) for k in ("p0", "p1")}
def weights(rng, still=[]):
    w = np.array(big(f(rng, N, 128, 2048))).reshape(N, 128, 4, 128, 4)
    for i in still:
        w[:, i] = 0
        w[:, :, :, i] = 0
    c, p = packed(w.reshape(N, 128, 2048), rng)
    return {"wc": c, "ws": p}
def setup_inputs(rng):
    return {**numbers_of(rng), **parents(rng), **weights(rng)}
def setup_inputs_ties(rng):
    d = numbers_of(rng)
    x = d["x"].reshape(N, 128, C, 4)
    x[:, ::64] = 0
    x[:, ::64, :, 0] = rng.integers(0, 3, (N, 2, C)).astype(np.float32).astype(BF)
    u = d["u"].reshape(N, 128, 128, 4)
    u[:, :, ::64] = 0
    o = rng.permutation(N)
    for r in range(N):
        for h in (0, 64): u[r, h, h, 0] = 0.0 if r == o[0] else -1.0 if r == o[1] else 1.0
    return {"x": x.reshape(N, 128, 4 * C), "u": u.reshape(N, 128, 512), "v": d["v"], **parents(rng), **weights(rng, [0, 64])}
def setup_inputs_near(rng):
    d = numbers_of(rng)
    x = d["x"].astype(np.float32).reshape(N, 128, C, 4)
    u = d["u"].reshape(N, 128, 128, 4)
    u[:, :, ::64] = 0
    o = rng.permutation(N) % 4
    for r in range(N):
        k = 2.0 ** -30 if o[r] > 0 else 1.0
        for h in (0, 64):
            x[r, h:h + 16] = 0
            sign = np.repeat(rng.permutation(C // 32) % 2 * 2.0 - 1.0, 32)
            far = 32 * np.arange(C // 32) + rng.integers(0, 32, C // 32)
            s = rng.integers(0, 16, C)
            if o[r] < 3:
                x[r, h + 8] = ((s[:, None] >> np.arange(4)) & 1) * np.exp2(np.arange(4) - 23.0)
                u[r, h + 8, h] = k
            if o[r] < 2:
                x[r, h, :, 0] = sign
                x[r, h + 11, :, 0] = 2.0 ** -10
                u[r, h, h, 0] = k
                u[r, h + 11, h, 0] = k
            if o[r] == 2:
                x[r, h, far, 0] = sign[far] * 2.0 ** 29
                u[r, h, h, 0] = 1.0
            if o[r] == 3:
                odd = np.arange(C) // 32 % 2
                j = rng.integers(0, 3, C)
                x[r, h + 10, :, 0] = (1 - odd) * np.array([1.0, 0.0, 1.125])[j] * 2.0 ** -29
                x[r, h + 12, :, 0] = (1 - odd) * (j == 1) * 2.0 ** -29
                u[r, h + 10, h, 0] = 1.125 * k
                u[r, h + 12, h, 0] = 1.25 * k
                x[r, h, :, 0] = odd * 1.96875
                x[r, h + 1, :, 0] = odd * rng.integers(3, 5, C) * np.exp2(np.arange(C) // 64 % 4 - 16.0)
                u[r, h + 1, h, 0] = k
    still = [h + i for h in (0, 64) for i in range(16)]
    return {"x": x.reshape(N, 128, 4 * C).astype(BF), "u": u.reshape(N, 128, 512), "v": d["v"], **parents(rng), **weights(rng, still)}
def setup_inputs_huge(rng):
    d = numbers_of(rng)
    o = rng.permutation(N) % 2
    x = (0.5 + 0.12 * rng.random((N, 128, C, 4))) * 2.0 ** 30
    for r in range(N):
        if o[r] == 0: c = np.repeat(rng.permutation(C // 32) % 2 * 2.0 - 1.0, 32)
        else: c = rng.permutation(C) % 2 * 2.0 - 1.0
        x[r] *= c[None, :, None]
    u = d["u"].reshape(N, 128, 128, 4)
    a = 2.0 ** 30 * (1.0 - 0.1 * rng.random((N, 128, 2, 4))) * rng.choice([-1.0, 1.0], (N, 1, 2, 1))
    u[:, :, ::64] = a.astype(np.float32).astype(BF)
    w = np.zeros((N, 128, 4, 128, 4), np.float32)
    i = np.arange(128)
    for b in range(4): w[:, i, b, i, b] = -2
    c, p = packed(w.reshape(N, 128, 2048).astype(BF), rng)
    return {"x": x.astype(np.float32).reshape(N, 128, 4 * C).astype(BF), "u": u.reshape(N, 128, 512), "v": d["v"], **parents(rng), "wc": c, "ws": p}
def setup_inputs_late(rng):
    d = numbers_of(rng)
    x = d["x"].astype(np.float32).reshape(N, 8, 16, C, 4)
    odd = 1.0 + (2.0 * rng.integers(0, 64, (N, 8, 8, C, 4)) + 1.0) * 2.0 ** -7
    x[:, :, 8:] = odd * np.exp2(rng.integers(-14, -7, (N, 8, 8, C, 4))) * rng.choice([-1.0, 1.0], (N, 8, 8, C, 4))
    x[:, :, 8, :, 0] = 1.96875 * rng.choice([-1.0, 1.0], (N, 8, C))
    x[:, ::4, 0] = 0
    u = d["u"].reshape(N, 128, 128, 4)
    u[:, :, ::64] = 0
    for h in (0, 64): u[:, h, h, 0] = 1.0
    before = np.maximum(LOCAL - 1, 0)
    a, b = [], []
    for r in range(N):
        k = np.repeat(rng.permutation(C // 32) % 4, 32)
        a.append(table(ROOT + np.where(k == 1, 0, np.where(k == 3, before // 2, before))))
        b.append(table(ROOT + np.where((k == 1) | (k == 2), 0, before)))
    return {"x": x.reshape(N, 128, 4 * C).astype(BF), "u": u.reshape(N, 128, 512), "v": d["v"], "p0": np.stack(a), "p1": np.stack(b), **weights(rng)}
def setup_inputs_spread(rng):
    d = setup_inputs(rng)
    d["x"] = big(wide(rng, N, 128, 4 * C, cols=6))
    return d
def check_inputs(d):
    b = []
    for k in ("x", "u", "v"):
        a = np.abs(d[k].astype(np.float32))
        if not (np.isfinite(a).all() and ((a == 0) | (a >= 2.0 ** -30) & (a <= 2.0 ** 30)).all()): b.append("a value of " + k)
    none, least, most = [emit(mx_ref.quantize(np.full((128, 16), k, np.float32).astype(BF)))[1][0, 0] for k in (0.0, 2.0 ** -30, 2.0 ** 30)]
    for r in range(N):
        for k in ("p0", "p1"):
            e = entries(d[k][r])
            if not ((e >= ROOT) & (e < ROOT + np.maximum(LOCAL, 1))).all(): b.append("an entry of " + k)
        if ((d["wc"][r] == 0x7F) | (d["wc"][r] == 0xFF)).any(): b.append("wc: a code that is no number")
        s = mx_ref.live(d["ws"][r])
        if ((s != none) & ((s < least) | (s > most))).any(): b.append("ws: a scale out of range")
    return b
def split(s, a, b):
    a, b = np.stack([a, a], axis=1), np.stack([b, b], axis=1)
    up = np.where(np.take_along_axis(s, a, axis=2) >= np.take_along_axis(s, b, axis=2), a, b).reshape(-1, 32) % 32
    n = len(up)
    above = np.zeros((n, 32, 32), bool)
    for j in range(32):
        if j > 0: above[:, :, j] = above[np.arange(n), :, up[:, j]]
        above[:, j, j] = True
    left, top = np.ones((n, 32), bool), np.zeros((n, 32), np.int64)
    c, w = [], []
    for l in range(4):
        one = (top[:, :, None] == top[:, None]) & left[:, :, None] & left[:, None]
        size = np.sum(above & one, axis=2)
        half = 2 * size >= np.sum(one, axis=2)
        best = np.max(np.where(one & half[:, None], PLACE, -1), axis=2)
        c.append(np.where(left, best, PLACE))
        w.append(size)
        left = left & (best != PLACE)
        cut = ~np.take_along_axis(left, up, axis=1)
        cut[:, 0] = True
        top = np.max(np.where(above & cut[:, :, None], PLACE[:, None], 0), axis=1)
    c, w = [np.stack(k, axis=1).reshape(N, 2, -1, 4, 32).transpose(0, 1, 3, 2, 4).reshape(N, 8, C) for k in (c, w)]
    return c + ROOT, np.argsort(-w, axis=2, kind="stable")
def reference(x, u, v, p0, p1, wc, ws):
    qu = [mx_ref.quantize(u[r]) for r in range(N)]
    lay = [pk(wc[r], ws[r]) for r in range(N)]
    a, b = np.stack([entries(p0[r]) for r in range(N)]), np.stack([entries(p1[r]) for r in range(N)])
    now = [x[r] for r in range(N)]
    for m in PARTNER:
        q = [mx_ref.quantize(now[r]) for r in range(N)]
        own = [decode(q[r]) for r in range(N)]
        s = np.stack([mx_ref.matmul(qu[r], q[r])[::64] for r in range(N)]) + np.float32(0.0)
        c, o = split(s, a, b)
        mosaic = [gcols(own[r].astype(BF), c[r]) for r in range(N)]
        sent = [mx_ref.quantize(gcols(mosaic[r], o[r][:, :K])) for r in range(N)]
        for r in range(N):
            e = np.argsort(o[r], axis=1)
            e = np.where(e < K, e, K + np.arange(C))
            mate = gcols(np.concatenate([decode(sent[r ^ m]).astype(BF), mosaic[r]], axis=1), e).astype(np.float32)
            z = mx_ref.quantize(((mosaic[r].astype(np.float32) + mate) * np.float32(0.5)).astype(BF))
            now[r] = tile([mx_ref.matmul(pick(lay[r], np.arange(128 * k, 128 * k + 128)), z) * np.float32(0.03125) + own[r][:, k::4] for k in range(4)])
    y, cl = np.zeros((N, 128, C), np.float32), np.zeros((N, 8, C), np.float32)
    oc, osc = np.zeros((N, 128, 4 * C), np.uint8), np.zeros((N, 16, C), np.uint8)
    for r in range(N):
        q = mx_ref.quantize(now[r])
        y[r] = mx_ref.matmul(mx_ref.quantize(v[r]), q)
        cl[r] = c[r]
        oc[r], osc[r] = emit(q)
    return {"y": y, "cl": cl, "oc": oc, "osc": osc}

@@ -1,0 +1,621 @@
+from concourse.mybir import dt, AluOpType, ActivationFunctionType
+
+C, K, ROUNDS = 384, 160, (1, 2, 3)
+HC = C // 2
+F32, BF, HF, I32, U16, MX, U8 = "float32", "bfloat16", "float16", "int32", "uint16", "float8_e4m3fn_x4", "uint8"
+MAGIC = 12582912.0
+BIG = 1048576.0
+SMALL = 262144.0
+WIN = C + K
+BASE = 1024.0
+
+_SB = {
+    "xt": (4 * C, BF), "xn": (4 * C, BF), "ut": (512, BF), "vt": (512, BF), "eye": (528, BF),
+    "qx": (C, MX), "sx": (C, U8), "qu": (128, MX), "su": (128, U8), "qup": (128, MX), "sup": (128, U8),
+    "qv": (128, MX), "sv": (128, U8), "qw": (512, MX), "sw": (512, U8), "qe": (512, MX), "se": (512, U8),
+    "qz": (C, MX), "sz": (C, U8), "tt": (4 * C, BF), "zt": (4 * C, BF),
+    "win": (4 * WIN, F32), "gall": (4 * C, F32), "ee": (4 * K, F32), "yo": (C, F32), "clo": (C, F32),
+    "pr": (48, I32), "pi": (8, I32), "pj": (16, I32), "fio": (192, F32), "p0f": (96, F32),
+    "dm": (K, F32), "eqm": (K, F32), "eqb": (K, F32), "gtm": (K, F32), "mw": (K, F32), "mwa": (96, F32), "m2": (192, F32),
+    "cd0": (192, F32), "cd1": (192, F32), "eqc": (96, F32), "tmp": (192, F32), "tmp2": (192, F32), "tmp3": (288, F32), "tmp4": (192, F32),
+    "m32": (192, BF), "m16": (C, BF), "mcl": (C, BF), "ones": (C, BF),
+    "ssb": (192, F32), "sb1": (96, F32), "sca": (192, F32),
+    "w0": (192, F32), "wa": (192, F32), "wb": (192, F32), "wc4": (192, F32), "wd": (192, F32), "x3": (96, F32),
+    "wf": (96, F32), "wg": (96, F32), "wft": (96, F32),
+    "bits": (96, F32), "bitt": (96, F32), "b2": (96, BF), "at": (192, BF), "am": (192, BF), "ua": (192, BF), "ws0": (192, BF),
+    "pd": (192, HF), "kd": (192, HF), "bs": (192, HF), "pfree": (192, HF), "y1": (192, HF), "y1t": (192, HF), "ks": (192, HF),
+    "y2": (192, HF), "y2t": (192, HF), "rs2": (192, HF),
+    "sd": (C, BF), "sbs": (C, BF), "sf": (C, BF), "eq1": (C, BF), "eqt": (C, BF), "sgn": (C, BF),
+    "p2": (C, HF), "p2t": (C, HF), "rs": (C, HF),
+    "cd": (C, BF), "cbs": (C, BF), "cf": (C, BF), "cs": (C, F32), "csw": (K, F32), "zz": (320, F32),
+}
+for _t in range(3):
+    _SB["qt%d" % _t] = (C, MX)
+    _SB["st%d" % _t] = (C, U8)
+    _SB["ql%d" % _t] = (C, MX)
+    _SB["sl%d" % _t] = (C, U8)
+    _SB["lo%d" % _t] = (10, U16)
+    _SB["li%d" % _t] = (10, U16)
+_PART = {}
+for _pool, _d, _names in (
+        ("fpool", F32, {"pf": 24, "aux": 16, "lpf": 32, "p1w": 8, "p1c": 8, "o1f": 8, "u1": 8, "up1": 8, "gg": 32, "w2": 24, "call": 24,
+                        "sm": 64, "cnt": 8, "rr": 64, "t1": 64, "t2": 64, "t3": 64, "cg": 96, "colc": 24, "z1": 64, "z2": 64, "z3": 64}),
+        ("upool", U16, {"uoff": 8, "sel": 8, "lp": 32, "o1": 8, "o4": 8, "o16": 8, "swp": 4, "opl": 24, "ozl": 24})):
+    _at = 0
+    for _k, _n in _names.items():
+        _PART[_k] = (_pool, _at, _n)
+        _at += (_n + 7) // 8 * 8
+    _SB[_pool] = (_at, _d)
+SCRATCH = {k: ("sbuf", [128, n], d) for k, (n, d) in _SB.items()}
+SCRATCH["ps"] = ("psum", [128, 4096], F32)
+NDMA = 20
+SEMAPHORES = ["cV", "cS", "cP", "cG", "sent"] + ["d%d" % k for k in range(NDMA)] + ["big%d" % t for t in range(3)] + ["lst%d" % t for t in range(3)]
+
+A = AluOpType
+FN = ActivationFunctionType
+
+
+def v(name, c0=0, c1=None, step=1, p0=0, p1=128):
+    name, at, n = _PART[name] if name in _PART else (name, 0, _SB[name][0])
+    return (name, p0, p1, at + c0, at + (n if c1 is None else c1), step)
+
+
+def ind(win, off):
+    return ("@", win, off)
+
+
+def col(name, c):
+    return v(name, c, c + 1)
+
+
+def _meet(a, b):
+    if a[0] == "ps":
+        return a[3] // 512 == b[3] // 512
+    if a[2] <= b[1] or b[2] <= a[1] or a[4] <= b[3] or b[4] <= a[3]:
+        return False
+    if a[5] == b[5] and a[5] > 1 and (a[3] - b[3]) % a[5]:
+        return False
+    return True
+
+
+def rank_program(g, core, T, topo):
+    rank = T.rank_of(core)
+    if rank is None:
+        return
+    ops = []
+
+    def real(a, cast=None):
+        if a[0] == "@":
+            return real(a[1], cast).indirect(real(a[2]))
+        name, p0, p1, c0, c1, step = a
+        r = T[name][p0:p1, c0:c1] if step == 1 else T[name][p0:p1, c0:c1:step]
+        return r.bitcast(cast) if cast is not None else r
+
+    def parts(a):
+        if isinstance(a, tuple):
+            return [a[1], a[2]] if a[0] == "@" else [a]
+        return []
+
+    def arg(a):
+        return real(a) if isinstance(a, tuple) else a
+
+    def add(q, call, ins, outs, waits=(), kind="c"):
+        r, w = [], []
+        for a in ins:
+            r += parts(a)
+        for a in outs:
+            if a[0] == "@":
+                w.append(a[1])
+                r.append(a[2])
+            else:
+                w.append(a)
+        ops.append((q, call, r, w, list(waits), kind))
+
+    def copy(o, i):
+        add("V", lambda: g.vector.tensor_copy(real(o), real(i)), [i], [o])
+
+    def pick(o, i):
+        add("V", lambda: g.vector.tensor_copy(real(o, dt.uint32), real(i, dt.uint32)), [i], [o])
+
+    def tt(o, a, b, op, waits=()):
+        add("V", lambda: g.vector.tensor_tensor(real(o), real(a), real(b), op), [a, b], [o], waits)
+
+    def ts(o, a, s1, op0, s2=None, op1=None):
+        if op1 is None:
+            add("V", lambda: g.vector.tensor_scalar(real(o), real(a), arg(s1), None, op0), [a, s1], [o])
+        else:
+            add("V", lambda: g.vector.tensor_scalar(real(o), real(a), arg(s1), arg(s2), op0, op1), [a, s1, s2], [o])
+
+    def scan(o, d0, d1, op0, op1, init=0.0):
+        add("V", lambda: g.vector.tensor_tensor_scan(real(o), real(d0), real(d1), arg(init), op0, op1), [d0, d1, init], [o])
+
+    def turn(o, i):
+        add("V", lambda: g.vector.transpose(real(o), real(i)), [i], [o])
+
+    def fill(o, c):
+        add("V", lambda: g.vector.memset(real(o), c), [], [o])
+
+    def quant(q, s, i):
+        add("V", lambda: g.vector.quantize_mx(real(q), real(s), real(i)), [i], [q, s])
+
+    def act(o, i, scale=1.0, bias=0.0, func=None, acc=None):
+        f = func if func is not None else (FN.Copy if not isinstance(bias, tuple) and bias == 0.0 else FN.Identity)
+        if acc is None:
+            add("S", lambda: g.scalar.activation(real(o), real(i), f, bias=arg(bias), scale=arg(scale)), [i, scale, bias], [o])
+        else:
+            add("S", lambda: g.scalar.activation(real(o), real(i), f, bias=arg(bias), scale=arg(scale), accum_out=real(acc)), [i, scale, bias], [o, acc])
+
+    def zero(o, n):
+        act(o, v("ones", 0, n), 0.0)
+
+    def mm(o, l, b, rq, rs, start=True, stop=True, waits=()):
+        lq, ls = v("q" + l, 128 * b, 128 * b + 128), v("s" + l, 128 * b, 128 * b + 128)
+        add("P", lambda: g.tensor.matmul_mx(real(o), real(lq), real(ls), real(rq), real(rs), start, stop), [lq, ls, rq, rs], [o], waits)
+
+    def iota(o, pattern, base, cm):
+        if _SB[o[0]][1] == I32:
+            add("G", lambda: g.iota(real(o), pattern, base, cm), [], [o])
+        else:
+            add("G", lambda: g.iota(real(o), pattern, base, cm, allow_small_or_imprecise_dtypes=True), [], [o])
+
+    def select(o, i, pattern, op, base, cm):
+        add("G", lambda: g.affine_select(real(o), real(i), pattern, op, 0.0, base, cm), [i], [o])
+
+    def dma(q, mk_out, mk_in, ins, outs):
+        e = g.sync if q == "Y" else g.scalar
+        add(q, lambda: e.dma_start(mk_out(), mk_in()), ins, outs, (), "d")
+
+    sent = [0]
+
+    def send(o, i, peer, sem, cast=None):
+        rid, pid, _ = topo.addr(peer)
+        m = topo.mask(core, peer)
+        sent[0] += len(topo.engines(core, peer))
+        add("G", lambda: g.remote_dma(real(o, cast), real(i, cast), T.sem[sem], T.sem.sent, pid, rid, m), [i], [], (), "r")
+
+    def bank(b, n=C, p0=0, p1=128):
+        return ("ps", p0, p1, 512 * b, 512 * b + n, 1)
+
+    def quad(name, q, c0, c1, step=1):
+        return v(name, c0, c1, step, 32 * q, 32 * q + 32)
+
+    def half(name, k):
+        return v(name, HC * k, HC * k + HC)
+
+    def quant_half(q, s, i, k):
+        quant(half(q, k), half(s, k), v(i, 4 * HC * k, 4 * HC * (k + 1)))
+
+    def odd(name):
+        return v(name, 1, None, 2)
+
+    def even(name):
+        return v(name, 0, None, 2)
+
+    for k in range(2):
+        dma("Y", lambda k=k: T.pr[16 * k:16 * k + 16, 0:24], lambda: T.p0[:], [], [v("pr", 0, 24, 1, 16 * k, 16 * k + 16)])
+        dma("S", lambda k=k: T.pr[16 * k:16 * k + 16, 24:48], lambda: T.p1[:], [], [v("pr", 24, 48, 1, 16 * k, 16 * k + 16)])
+    dma("S", lambda: T.ut[:], lambda: T.u[:], [], [v("ut")])
+    for k in range(2):
+        dma("Y", lambda k=k: T.xt[:, 4 * HC * k:4 * HC * (k + 1)], lambda k=k: T.x[:, 4 * HC * k:4 * HC * (k + 1)], [], [v("xt", 4 * HC * k, 4 * HC * (k + 1))])
+    dma("Y", lambda: T.qw[:].bitcast(dt.uint8), lambda: T.wc[:], [], [v("qw")])
+    dma("Y", lambda: T.sw[:], lambda: T.ws[:], [], [v("sw")])
+    dma("Y", lambda: T.vt[:], lambda: T.v[:], [], [v("vt")])
+
+    fill(v("ones"), 1.0)
+    fill(v("eye"), 32.0)
+    iota(col("pi", 0), [[0, 1]], 0, 1)
+    iota(v("pj", 0, 8), [[0, 2], [64, 2], [0, 2]], 0, 0)
+    iota(v("dm"), [[0, K // 16], [1, 16]], 0, 0)
+    iota(v("tmp", 0, 96), [[0, 3], [1, 32]], 0, 0)
+    iota(v("tmp", 96, 192), [[64, 3], [1, 32]], 0, 0)
+    iota(v("p1c", 0, 6), [[32, 3], [0, 2]], 0, 0)
+    iota(v("fio"), [[1, 192]], 0, 0)
+    select(v("eye"), v("eye"), [[-1, 528]], A.is_equal, 3, 4)
+    select(v("m32"), v("ones", 0, 192), [[0, 6], [1, 32]], A.is_gt, 0, 0)
+    iota(v("pj", 8, 12), [[16, 2], [32, 2]], 0, 0)
+    iota(v("colc"), [[0, 2], [32, 6], [0, 2]], -HC, 0)
+    select(v("mcl"), v("ones"), [[0, 12], [1, 32]], A.is_gt, 0, 0)
+    select(v("m16"), v("ones"), [[0, 24], [1, 16]], A.is_gt, 0, 0)
+    for name in ("cd0", "wa", "wb"):
+        zero(v(name), 192)
+    for k, (c, op) in enumerate(((15, A.bitwise_and), (31, A.bitwise_and), (6, A.logical_shift_right), (16, A.bitwise_and),
+                                 (1, A.bitwise_and), (14, A.bitwise_and), (63, A.bitwise_and))):
+        ts(col("pi", k + 1), col("pi", 0), c, op)
+    copy(v("uoff"), v("pj", 0, 8))
+    copy(v("pf", 0, 8), v("pi", 0, 8))
+    PR, PI, PQ, PSB, PX, P2B, P64 = [col("pf", k) for k in range(1, 8)]
+    R2, R21, I1, SB32, PCL, PNB, Q192, ROOT, I162, NI162, NI2 = [col("pf", k) for k in range(8, 19)]
+    ts(col("aux", 0), P2B, 4.0, A.min, 2.0, A.mult)
+    ts(col("aux", 1), PQ, 12.0, A.mult, PX, A.add)
+    ts(Q192, PQ, -192.0, A.mult)
+    ts(col("aux", 2), PSB, 0.125, A.mult, col("aux", 0), A.add)
+    act(R2, PR, 2.0)
+    act(R21, PR, 2.0, 1.0)
+    act(SB32, PSB, 2.0)
+    ts(v("eqm"), v("dm"), PR, A.is_equal)
+    ts(col("sel", 0), col("aux", 1), col("aux", 2), A.add)
+    ts(v("gtm"), v("dm"), PR, A.is_gt)
+    act(v("eqb"), v("eqm"), BIG)
+    ts(v("tmp2", 0, 96), v("tmp", 0, 96), R2, A.is_equal, 1.0 / 16, A.mult)
+    ts(v("tmp2", 96, 192), v("tmp", 0, 96), R21, A.is_equal, 2.0 / 16, A.mult)
+    act(v("tmp3", 0, 96), v("tmp", 96, 192), 1.0, SB32)
+    for name in ("eqb", "gtm"):
+        act(v(name, 15, None, 16), v(name, 15, None, 16), 1.0 / BIG / SMALL)
+    act(v("eqc"), v("eqb", 0, 96), -2.0)
+    fill(v("tmp2", 0, 96, 32), 0.0)
+    copy(v("pr", 0, 48, 1, 32, 64), v("pr", 0, 48, 1, 0, 32))
+    tt(v("tmp3", 96, 192), v("tmp3", 0, 96), v("tmp2", 96, 192), A.add)
+    copy(v("pr", 0, 48, 1, 64, 128), v("pr", 0, 48, 1, 0, 64))
+    tt(v("tmp3", 192, 288), v("tmp3", 96, 192), v("tmp2", 0, 96), A.add)
+    for k in range(2):
+        ts(v("lpf", 16 * k, 16 * k + 16), ind(v("pr", 24 * k, 24 * k + 24), col("sel", 0)), Q192, A.add)
+    quant(v("qu"), v("su"), v("ut"))
+    copy(v("lp"), v("lpf"))
+    pick(v("qup"), ind(v("qu"), v("uoff")))
+    copy(v("sup"), ind(v("su"), v("uoff")))
+    LP0, LP1 = v("lp", 0, 6), v("lp", 16, 22)
+    act(v("p0f"), ind(v("fio"), LP0))
+    ts(v("p1c", 0, 6), v("p1c", 0, 6), SB32, A.add, -0.625, A.add)
+    quant_half("qx", "sx", "xt", 0)
+    tt(v("tmp4", 96, 192), ind(v("fio"), LP1), v("tmp3", 192, 288), A.subtract)
+    quant_half("qx", "sx", "xt", 1)
+
+    def scores(k):
+        mm(bank(k, HC), "up", 0, half("qx", k), half("sx", k))
+
+    for k in range(2):
+        scores(k)
+    tt(v("tmp4", 0, 96), ind(v("fio"), LP1), v("p0f"), A.subtract)
+    act(odd("cd1"), v("tmp4", 96, 192), -16.0)
+    act(v("ssb", 0, HC, 1, 0, 64), bank(0, HC, 0, 64))
+    act(even("cd1"), v("tmp4", 0, 96), 16.0)
+    tt(v("p1w", 0, 6), v("lpf", 16, 22), v("p1c", 0, 6), A.subtract)
+    tt(v("tmp2", 0, 96), v("tmp4", 0, 96), v("eqc"), A.mult)
+    act(v("p1w", 0, 6), v("p1w", 0, 6), 2.0 / SMALL)
+
+    def early_constants():
+        for name in ("wc4", "wd"):
+            act(even(name), v("fio", 0, 96), -16.0, -8 * 1.45)
+        act(I1, PI, 1.0, 1.0)
+        act(I162, PI, 16.0, 2.0)
+        act(NI162, PI, -16.0, -2.0)
+        act(NI2, PI, -2.0)
+        ts(even("m2"), v("dm", 0, 96), PR, A.is_ge)
+        tt(odd("m2"), v("gtm", 0, 96), v("eqb", 0, 96), A.subtract)
+        ts(ROOT, PR, 0.0, A.is_equal)
+
+    def late_constants():
+        zero(v("sd"), C)
+        zero(v("cd"), C)
+        zero(v("rr"), 64)
+        zero(v("zz", 0, 64), 64)
+        ts(col("aux", 3), P64, 32.0, A.is_ge, 16.0, A.mult)
+        ts(col("aux", 4), P64, 49.0, A.is_ge, 5.0, A.mult)
+        ts(col("aux", 5), P64, 55.0, A.is_ge, 10.0, A.mult)
+        for h in range(2):
+            fill(quad("mcl", 2 * h + 1, 17, C, 32), 0.0)
+            fill(quad("mcl", 2 * h + 1, 23, C, 32), 0.0)
+        ts(col("aux", 6), P64, col("aux", 3), A.subtract, col("aux", 4), A.subtract)
+        act(col("aux", 7), col("aux", 5), 1.0 / 32, 1.0)
+        ts(v("colc"), v("colc"), Q192, A.subtract, PI, A.add)
+        ts(v("swp"), v("pj", 8, 12), PR, A.add)
+        tt(v("mw"), v("eqb"), v("gtm"), A.add)
+        act(PCL, col("aux", 6), -1.0 / 32, col("aux", 7))
+        act(PNB, PCL, -1.0, -1.0 / 64)
+
+    def lv(name, l):
+        return v(name, 12 * (l // 2) + l % 2, 12 * (l // 2) + 12, 2)
+
+    def lvc(name, l, s):
+        return col(name, 12 * (l // 2) + l % 2 + 2 * s)
+
+    def sm(k):
+        return v("sm", 8 * k, 8 * k + 6)
+
+    def gv(l):
+        return v("gg", 8 * l, 8 * l + 6)
+
+    def slot(name, s):
+        return v(name, 32 * s, 32 * s + 32)
+
+    def spread(l):
+        c0, c1, off = lv("w2", l)[3], lv("w2", l)[4], (0, 0, 23, 17)[l]
+        for h in range(2):
+            for qs in range(2):
+                act(quad("sd", 2 * h + (l > 0), 192 * qs + off, 192 * qs + 192, 32), quad("fpool", 2 * qs + h, c0, c1, 2))
+
+    END = v("ks", 31, None, 32)
+    PP = v("pd", 0, None, 32)
+
+    def same_piece(l):
+        ts(sm(1), PP, MAGIC, A.add, MAGIC, A.subtract)
+        scan(v("bs"), v("m32"), v("pd"), A.mult, A.add)
+        tt(sm(2), lv("w2", l), sm(1), A.add)
+        turn(v("pfree"), v("bs"))
+        tt(sm(3), sm(2), PP, A.min)
+        if l < 3:
+            tt(sm(0), sm(2), PP, A.is_ge)
+
+    def heavy(l):
+        for s in range(6):
+            ts(slot("y1", s), slot("pfree", s), col("sm", 24 + s), A.is_equal, col("gg", 8 * l + s), A.mult)
+
+    for t, mask in enumerate(ROUNDS):
+        peer = T.cores[rank ^ mask]
+        ne = len(topo.engines(peer, core))
+        qt, st, ql, sl, lo, li = ["%s%d" % (n, t) for n in ("qt", "st", "ql", "sl", "lo", "li")]
+
+        def unpack(b):
+            mm(bank(4 + b), "e", b, v("qx"), v("sx"))
+
+        def tile_t(b):
+            act(v("tt", b, None, 4), bank(4 + b), 1.0 / 32)
+
+        def quant_t(k):
+            quant(v(qt, 128 * k, 128 * k + 128), v(st, 128 * k, 128 * k + 128), v("tt", 512 * k, 512 * k + 512))
+
+        def send_t():
+            send(v(ql), v(qt), peer, "big%d" % t, dt.uint8)
+            send(v(sl), v(st), peer, "big%d" % t)
+
+        copy(v("ssb", 0, HC, 1, 64, 128), bank(1, HC, 64, 128))
+        if t:
+            for b in range(4):
+                unpack(b)
+            tile_t(0)
+            tile_t(1)
+        else:
+            tt(v("mwa"), v("tmp2", 0, 96), v("gtm", 0, 96), A.add)
+        copy(v("sb1"), ind(v("ssb"), LP1))
+        tt(odd("cd0"), ind(v("ssb"), LP0), v("sb1"), A.is_ge)
+        scan(v("w0"), v("cd0"), v("cd1"), A.mult, A.add)
+        scan(v("sca", 0, 96), odd("cd0"), v("mwa"), A.add, A.mult)
+        act(v("wf"), odd("w0"))
+        tt(v("o1f", 0, 6), v("sca", 15, 96, 16), v("p1w", 0, 6), A.add)
+        ts(v("o1", 0, 6), v("o1f", 0, 6), SMALL, A.mult)
+        if t:
+            tile_t(2)
+            tile_t(3)
+        else:
+            early_constants()
+        for src, base, off, last, nxt in (("w0", "wf", "o1", "wc4", "o4"), ("wc4", "wg", "o4", "wd", "o16")):
+            for k, dst in enumerate(("wa", "wb", last)):
+                tt(odd(dst), ind(v(src), v(off, 0, 6)), v(base), A.add)
+                src = dst
+                if t == 0 and k < 2:
+                    b = k + 2 * (last == "wd")
+                    quant(v("qe", 128 * b, 128 * b + 128), v("se", 128 * b, 128 * b + 128), v("eye", 3 - b, 515 - b))
+                    unpack(b)
+                if t and last == "wd":
+                    quant_t(k)
+            if last == "wd":
+                act(v("x3"), odd("wd"), 1.0, ROOT)
+                if t:
+                    send_t()
+            else:
+                act(v("wg"), odd("wc4"))
+            scan(v("sca"), v(last), v("m2"), A.add, A.mult)
+            if last == "wc4":
+                turn(v("wft"), v("wf"))
+            ts(v(nxt, 0, 6), v("sca", 31, None, 32), SMALL / 8, A.mult)
+            if last == "wc4":
+                act(v("u1", 0, 6), v("wft", 0, None, 16), -1.0 / 16, MAGIC)
+                if t == 0:
+                    tile_t(0)
+                    tile_t(1)
+        tt(v("bits"), ind(v("wd"), v("o16", 0, 6)), v("x3"), A.add)
+        ts(v("up1", 0, 6), v("u1", 0, 6), MAGIC, A.subtract, I1, A.add)
+        turn(v("bitt"), v("bits"))
+        act(v("b2"), v("bitt"), 1.0, NI162, FN.Abs)
+        ts(odd("at"), v("bitt"), I162, A.is_ge)
+        if t == 0:
+            for name in ("pd", "kd"):
+                ts(v(name), v("ones", 0, 192), 0.0, A.mult)
+        ts(even("at"), v("b2"), 1.0, A.is_equal)
+        turn(v("am"), v("at"))
+        for s in range(6):
+            act(slot("ua", s), slot("am", s), col("up1", s), -1.0)
+        scan(v("ws0"), v("m32"), v("am"), A.mult, A.add)
+        W0 = v("ws0", 31, None, 32)
+        ts(gv(0), W0, 1.0 / 64, A.mult, PI, A.add)
+        ts(sm(0), W0, 16.0, A.is_ge)
+        act(lv("w2", 0), W0, 1.0 / 32)
+        tt(v("kd", 0, None, 32), sm(0), gv(0), A.mult)
+        ts(PP, W0, 0.0, A.mult, 0.5, A.add)
+        scan(v("y1"), v("m32"), v("kd"), A.mult, A.add)
+        if t == 0:
+            tile_t(2)
+            tile_t(3)
+            late_constants()
+        spread(0)
+        for b in range(4):
+            act(v("win", WIN * b, WIN * b + C), bank(4 + b), 1.0 / 16)
+        for l in range(3):
+            if l:
+                same_piece(l)
+                heavy(l)
+            turn(v("y1t"), v("y1"))
+            scan(v("ks"), v("m32"), v("y1t"), A.mult, A.max)
+            ts(lv("call", l), END, MAGIC, A.add, MAGIC, A.subtract)
+            for s in range(6):
+                ts(slot("y2", s), slot("ua", s), lvc("call", l, s), A.is_equal, col("gg", 8 * l + s), A.mult)
+            tt(sm(4), END, lv("call", l), A.subtract)
+            turn(v("y2t"), v("y2"))
+            tt(sm(5), sm(4), sm(0), A.mult)
+            tt(sm(6), PP, sm(4), A.subtract)
+            scan(v("rs2"), v("m32"), v("y2t"), A.mult, A.max)
+            tt(gv(l + 1), gv(l), sm(5), A.subtract)
+            tt(PP, v("rs2", 31, None, 32), sm(6), A.max)
+            act(lv("w2", l + 1), gv(l + 1), 2.0, NI2)
+            spread(l + 1)
+            if t == 0 and l == 0:
+                for k in range(3):
+                    quant_t(k)
+                send_t()
+        same_piece(3)
+        scan(v("sbs"), v("mcl"), v("sd"), A.mult, A.add)
+        turn(v("sf"), v("sbs"))
+        act(v("sgn"), v("sf"), 1.0, PNB, FN.Sign, col("cnt", 0))
+        act(col("cnt", 1), col("cnt", 0), 0.5, BASE + C / 2)
+        heavy(3)
+        ts(v("eq1"), v("sf"), PCL, A.is_equal, 1.0, A.add)
+        turn(v("y1t"), v("y1"))
+        turn(v("eqt"), v("eq1"))
+        scan(v("ks"), v("m32"), v("y1t"), A.mult, A.max)
+        ts(v("cg", 0, 24), v("w2"), 0.0, A.is_gt)
+        ts(lv("call", 3), END, MAGIC, A.add, MAGIC, A.subtract)
+        scan(v("p2"), v("eq1"), v("ones"), A.add, A.subtract, col("cnt", 1))
+        ts(v("cg", 24, 48), v("call"), PI, A.subtract)
+        turn(v("p2t"), v("p2"))
+        tt(v("cg", 48, 72), v("cg", 0, 24), v("cg", 24, 48), A.mult)
+        scan(v("rs"), v("eqt"), v("p2t"), A.mult, A.min, BASE)
+        tt(v("cg", 72, 96), v("cg", 48, 72), v("colc"), A.add)
+        for h in range(2):
+            for qq in range(2):
+                for qs in range(2):
+                    act(quad("cd", 2 * h + qq, 192 * qs, 192 * qs + 192, 16), quad("cg", 2 * qs + h, 72 + 12 * qq, 84 + 12 * qq))
+        copy(v("rr", 0, 12), v("rs", 31, C, 32))
+        for h in range(2):
+            copy(quad("rr", 2 * h, 32, 44), quad("rs", 2 * h + 1, 16, C, 32))
+            copy(quad("rr", 2 * h + 1, 32, 44), quad("rs", 2 * h + 1, 21, C, 32))
+        turn(v("t1"), v("rr"))
+        copy(v("t2"), ind(v("t1"), v("swp")))
+        turn(v("t3"), v("t2"))
+        scan(v("cbs"), v("m16"), v("cd"), A.mult, A.add)
+        ts(v("opl", 0, None, 2), v("t3", 0, 12), -BASE - 0.75, A.add)
+        turn(v("cf"), v("cbs"))
+        ts(v("opl", 1, None, 2), v("t3", 32, 44), -BASE - 0.75, A.add)
+        for b in range(4):
+            mm(bank(b), "e", b, v(ql), v(sl), waits=[("big%d" % t, 2 * ne)] if b == 0 else ())
+            act(v("gall", C * b, C * b + C), bank(b), 1.0 / 32)
+        for k in (1, 0):
+            for b in range(4):
+                mm(bank(4 * k + b, HC), "e", b, half("qx", k), half("sx", k), True, False)
+        copy(ind(v("cs"), v("opl")), v("cf"))
+        scan(v("csw"), v("cs", 0, K), v("mw"), A.add, A.mult)
+        ts(v(lo), v("csw", 15, None, 16), SMALL, A.mult, HC + 0.25, A.add)
+        send(v(li), v(lo), peer, "lst%d" % t)
+        for b in range(4):
+            act(v("ee", K * b, K * b + K), ind(v("win", WIN * b, WIN * b + C), v(lo)), 0.5)
+        for a in range(2):
+            copy(v("zz", 32 * a, 32 * a + 12), v("cd", 16 * a, None, 32))
+        ts(v("zz", 128, 192), v("rr"), C - HC - BASE - 1.0, A.add)
+        ts(v("zz", 64, 128), v("rr"), BASE + K + 0.5, A.is_lt)
+        tt(v("zz", 192, 256), v("zz", 128, 192), v("zz", 0, 64), A.subtract)
+        tt(v("zz", 256, 320), v("zz", 192, 256), v("zz", 64, 128), A.mult)
+        tt(v("zz", 128, 192), v("zz", 256, 320), v("zz", 0, 64), A.add)
+        turn(v("z1"), v("zz", 128, 192))
+        copy(v("z2"), ind(v("z1"), v("swp")))
+        turn(v("z3"), v("z2"))
+        for hi in range(2):
+            ts(v("ozl", hi, None, 2), v("z3", 32 * hi, 32 * hi + 12), HC + 0.25, A.add)
+        if t == 2:
+            ts(v("clo"), v("cf"), float(HC), A.add)
+            dma("Y", lambda: T.cl[:], lambda: T.clo[0:128:16, :], [v("clo")], [])
+            quant(v("qv"), v("sv"), v("vt"))
+
+        def zpart(b, k, eng):
+            o = v("zt", 4 * HC * k + b, 4 * HC * (k + 1), 4)
+            i = ind(v("win", WIN * b, WIN * b + WIN), v("ozl", 12 * k, 12 * k + 12))
+            if eng == "V":
+                ts(o, i, 0.5, A.mult)
+            else:
+                act(o, i, 0.5)
+
+        def xpart(b, k, eng):
+            o = v("xn", 4 * HC * k + b, 4 * HC * (k + 1), 4)
+            if eng == "V":
+                ts(o, bank(4 * k + b, HC), 1.0 / 32, A.mult)
+            else:
+                act(o, bank(4 * k + b, HC), 1.0 / 32)
+
+        def layer(k):
+            quant_half("qz", "sz", "zt", k)
+            for b in range(4):
+                mm(bank(4 * k + b, HC), "w", b, half("qz", k), half("sz", k), False, True)
+
+        def after(k):
+            quant_half("qx", "sx", "xn", k)
+            if t < 2:
+                scores(k)
+            else:
+                mm(bank(k, HC), "v", 0, half("qx", k), half("sx", k))
+                dma("Y", lambda: T.oc[:, 4 * HC * k:4 * HC * (k + 1)], lambda: T.qx[:, HC * k:HC * (k + 1)].bitcast(dt.uint8), [half("qx", k)], [])
+
+        for b in range(4):
+            tt(v("win", WIN * b + C, WIN * b + WIN), ind(v("gall", C * b, C * b + C), v(li)), v("ee", K * b, K * b + K), A.add,
+               waits=[("lst%d" % t, ne)] if b == 0 else ())
+        for b in range(3):
+            zpart(b, 0, "S")
+        zpart(3, 0, "V")
+        layer(0)
+        for b in range(3):
+            zpart(b, 1, "S")
+        zpart(3, 1, "V")
+        xpart(0, 0, "V")
+        xpart(1, 0, "V")
+        layer(1)
+        xpart(2, 0, "S")
+        xpart(3, 0, "S")
+        after(0)
+        xpart(0, 1, "S")
+        xpart(1, 1, "V")
+        xpart(2, 1, "S")
+        xpart(3, 1, "V")
+        if t < 2:
+            act(v("ssb", 0, HC, 1, 0, 64), bank(0, HC, 0, 64))
+        else:
+            act(half("yo", 0), bank(0, HC))
+            dma("S", lambda: T.y[:, 0:HC], lambda: T.yo[:, 0:HC], [half("yo", 0)], [])
+        after(1)
+
+    copy(half("yo", 1), bank(1, HC))
+    for k in range(4):
+        dma("S" if k % 2 else "Y", lambda k=k: T.osc[4 * k:4 * k + 4, :], lambda k=k: T.sx[32 * k:32 * k + 4, :], [v("sx")], [])
+    dma("Y", lambda: T.y[:, HC:C], lambda: T.yo[:, HC:C], [half("yo", 1)], [])
+
+    used = {}
+    seen = {}
+    need = set()
+    deps = []
+    for n, (q, call, r, w, waits, kind) in enumerate(ops):
+        hits = set()
+        for mine, writes in ((r, False), (w, True)):
+            for a in mine:
+                for m, b, wrote in used.get(a[0], ()):
+                    q2 = ops[m][0]
+                    if (writes or wrote or (a[0] == "ps" and q2 != q)) and not (q == "P" and q2 == "P") and _meet(a, b):
+                        hits.add(m)
+        keep = []
+        for m in sorted(hits, reverse=True):
+            key = (q, ops[m][0]) if ops[m][5] == "c" else (q, m)
+            if seen.get(key, -1) < m:
+                seen[key] = m
+                keep.append(m)
+                need.add(m)
+        deps.append(keep)
+        if kind != "r":
+            for mine, writes in ((r, False), (w, True)):
+                for a in mine:
+                    used.setdefault(a[0], []).append((n, a, writes))
+    queue = {"V": g.vector, "S": g.scalar, "P": g.tensor, "G": g, "Y": g.sync}
+    count = {"V": 0, "S": 0, "P": 0, "G": 0}
+    mark = {}
+    ndma = 0
+    for n, (q, call, r, w, waits, kind) in enumerate(ops):
+        for m in deps[n]:
+            queue[q].wait_ge(T.sem[mark[m][0]], mark[m][1])
+        for s, val in waits:
+            queue[q].wait_ge(T.sem[s], val)
+        done = call()
+        if kind == "d":
+            mark[n] = ("d%d" % ndma, 16)
+            ndma += 1
+            done.then_inc(T.sem[mark[n][0]], 16)
+        elif kind == "c" and n in need:
+            count[q] += 1
+            mark[n] = ("c" + q, count[q])
+            done.then_inc(T.sem["c" + q], 1)
+    for k in range(ndma):
+        g.sync.wait_ge(T.sem["d%d" % k], 16)
+    g.wait_ge(T.sem.sent, sent[0])

@@ -8,6 +8,7 @@ BIG = 1048576.0
 SMALL = 262144.0
 WIN = C + K
 BASE = 1024.0
+CY, WAKE, LOAD, LIST, TILE = 0.95, 170.0, 2500.0, 2600.0, 6000.0
 
 _SB = {
     "xt": (4 * C, BF), "xn": (4 * C, BF), "ut": (512, BF), "vt": (512, BF), "eye": (528, BF),
@@ -15,19 +16,20 @@ _SB = {
     "qv": (128, MX), "sv": (128, U8), "qw": (512, MX), "sw": (512, U8), "qe": (512, MX), "se": (512, U8),
     "qz": (C, MX), "sz": (C, U8), "tt": (4 * C, BF), "zt": (4 * C, BF),
     "win": (4 * WIN, F32), "gall": (4 * C, F32), "ee": (4 * K, F32), "yo": (C, F32), "clo": (C, F32),
-    "pr": (48, I32), "pi": (8, I32), "pj": (16, I32), "fio": (192, F32), "p0f": (96, F32),
+    "pr": (48, I32), "pi": (8, I32), "pj": (16, I32), "top": (8, I32), "fio": (192, F32), "p0f": (96, F32),
     "dm": (K, F32), "eqm": (K, F32), "eqb": (K, F32), "gtm": (K, F32), "mw": (K, F32), "mwa": (96, F32), "m2": (192, F32),
-    "cd0": (192, F32), "cd1": (192, F32), "eqc": (96, F32), "tmp": (192, F32), "tmp2": (192, F32), "tmp3": (288, F32), "tmp4": (192, F32),
+    "cd0": (192, F32), "cd1": (192, F32), "eqc": (96, F32), "tmp": (192, F32), "tmp2": (288, F32), "tmp3": (288, F32), "tmp4": (192, F32),
     "m32": (192, BF), "m16": (C, BF), "mcl": (C, BF), "ones": (C, BF),
     "ssb": (192, F32), "sb1": (96, F32), "sca": (192, F32),
     "w0": (192, F32), "wa": (192, F32), "wb": (192, F32), "wc4": (192, F32), "wd": (192, F32), "x3": (96, F32),
     "wf": (96, F32), "wg": (96, F32), "wft": (96, F32),
     "bits": (96, F32), "bitt": (96, F32), "b2": (96, BF), "at": (192, BF), "am": (192, BF), "ua": (192, BF), "ws0": (192, BF),
+    "hd": (192, BF), "h1": (192, BF), "h2": (192, BF), "h3": (192, F32),
     "pd": (192, HF), "kd": (192, HF), "bs": (192, HF), "pfree": (192, HF), "y1": (192, HF), "y1t": (192, HF), "ks": (192, HF),
     "y2": (192, HF), "y2t": (192, HF), "rs2": (192, HF),
     "sd": (C, BF), "sbs": (C, BF), "sf": (C, BF), "eq1": (C, BF), "eqt": (C, BF), "sgn": (C, BF),
-    "p2": (C, HF), "p2t": (C, HF), "rs": (C, HF),
-    "cd": (C, BF), "cbs": (C, BF), "cf": (C, BF), "cs": (C, F32), "csw": (K, F32), "zz": (320, F32),
+    "p2": (C, HF), "p2t": (C, HF), "rs": (C, F32),
+    "cd": (C, BF), "cbs": (C, BF), "cf": (C, BF), "cs": (C, F32), "csw": (K, F32), "zz": (384, F32),
 }
 for _t in range(3):
     _SB["qt%d" % _t] = (C, MX)
@@ -38,8 +40,8 @@ for _t in range(3):
     _SB["li%d" % _t] = (10, U16)
 _PART = {}
 for _pool, _d, _names in (
-        ("fpool", F32, {"pf": 24, "aux": 16, "lpf": 32, "p1w": 8, "p1c": 8, "o1f": 8, "u1": 8, "up1": 8, "gg": 32, "w2": 24, "call": 24,
-                        "sm": 64, "cnt": 8, "rr": 64, "t1": 64, "t2": 64, "t3": 64, "cg": 96, "colc": 24, "z1": 64, "z2": 64, "z3": 64}),
+        ("fpool", F32, {"pf": 24, "aux": 16, "lpf": 16, "p1w": 8, "p1c": 8, "o1f": 8, "u1": 8, "up1": 8, "gg": 24, "w2": 24, "call": 24,
+                        "sm": 64, "cnt": 8, "rr": 64, "t1": 64, "t2": 64, "t3": 64, "cg": 120, "colc": 24, "z1": 64, "z2": 64, "z3": 64}),
         ("upool", U16, {"uoff": 8, "sel": 8, "lp": 32, "o1": 8, "o4": 8, "o16": 8, "swp": 4, "opl": 24, "ozl": 24})):
     _at = 0
     for _k, _n in _names.items():
@@ -78,11 +80,26 @@ def _meet(a, b):
     return True
 
 
+def _len(a):
+    return 16 * _len(a[2]) if a[0] == "@" else (a[4] - a[3] + a[5] - 1) // a[5]
+
+
+def _ns(o, i, rate=None):
+    if o[0] == "@":
+        return 50 + 3.2 * _len(o)
+    if i[0] == "@":
+        return 55 + 1.3 * _len(i)
+    if rate is None:
+        rate = 0.5 if all(a[0] != "ps" and _SB[a[0]][1] in (BF, HF) for a in (o, i)) else 1.0
+    return max(64, rate * _len(i)) * CY
+
+
 def rank_program(g, core, T, topo):
     rank = T.rank_of(core)
     if rank is None:
         return
     ops = []
+    lands = {}
 
     def real(a, cast=None):
         if a[0] == "@":
@@ -99,7 +116,7 @@ def rank_program(g, core, T, topo):
     def arg(a):
         return real(a) if isinstance(a, tuple) else a
 
-    def add(q, call, ins, outs, waits=(), kind="c"):
+    def add(q, call, ins, outs, ns, waits=(), kind="c", behind=()):
         r, w = [], []
         for a in ins:
             r += parts(a)
@@ -109,61 +126,63 @@ def rank_program(g, core, T, topo):
                 r.append(a[2])
             else:
                 w.append(a)
-        ops.append((q, call, r, w, list(waits), kind))
+        ops.append((q, call, r, w, list(waits), kind, ns, list(behind)))
+        return len(ops) - 1
 
     def copy(o, i):
-        add("V", lambda: g.vector.tensor_copy(real(o), real(i)), [i], [o])
+        add("V", lambda: g.vector.tensor_copy(real(o), real(i)), [i], [o], _ns(o, i))
 
     def pick(o, i):
-        add("V", lambda: g.vector.tensor_copy(real(o, dt.uint32), real(i, dt.uint32)), [i], [o])
+        add("V", lambda: g.vector.tensor_copy(real(o, dt.uint32), real(i, dt.uint32)), [i], [o], _ns(o, i))
 
-    def tt(o, a, b, op, waits=()):
-        add("V", lambda: g.vector.tensor_tensor(real(o), real(a), real(b), op), [a, b], [o], waits)
+    def tt(o, a, b, op, waits=(), behind=()):
+        add("V", lambda: g.vector.tensor_tensor(real(o), real(a), real(b), op), [a, b], [o], _ns(o, a, 2.0), waits, "c", behind)
 
     def ts(o, a, s1, op0, s2=None, op1=None):
         if op1 is None:
-            add("V", lambda: g.vector.tensor_scalar(real(o), real(a), arg(s1), None, op0), [a, s1], [o])
+            add("V", lambda: g.vector.tensor_scalar(real(o), real(a), arg(s1), None, op0), [a, s1], [o], _ns(o, a))
         else:
-            add("V", lambda: g.vector.tensor_scalar(real(o), real(a), arg(s1), arg(s2), op0, op1), [a, s1, s2], [o])
+            add("V", lambda: g.vector.tensor_scalar(real(o), real(a), arg(s1), arg(s2), op0, op1), [a, s1, s2], [o], _ns(o, a))
 
     def scan(o, d0, d1, op0, op1, init=0.0):
-        add("V", lambda: g.vector.tensor_tensor_scan(real(o), real(d0), real(d1), arg(init), op0, op1), [d0, d1, init], [o])
+        add("V", lambda: g.vector.tensor_tensor_scan(real(o), real(d0), real(d1), arg(init), op0, op1), [d0, d1, init], [o], _ns(o, d1))
 
     def turn(o, i):
-        add("V", lambda: g.vector.transpose(real(o), real(i)), [i], [o])
+        add("V", lambda: g.vector.transpose(real(o), real(i)), [i], [o], _ns(o, i))
 
     def fill(o, c):
-        add("V", lambda: g.vector.memset(real(o), c), [], [o])
+        add("V", lambda: g.vector.memset(real(o), c), [], [o], _ns(o, o))
 
     def quant(q, s, i):
-        add("V", lambda: g.vector.quantize_mx(real(q), real(s), real(i)), [i], [q, s])
+        add("V", lambda: g.vector.quantize_mx(real(q), real(s), real(i)), [i], [q, s], 15 + 0.25 * _len(i))
 
     def act(o, i, scale=1.0, bias=0.0, func=None, acc=None):
         f = func if func is not None else (FN.Copy if not isinstance(bias, tuple) and bias == 0.0 else FN.Identity)
         if acc is None:
-            add("S", lambda: g.scalar.activation(real(o), real(i), f, bias=arg(bias), scale=arg(scale)), [i, scale, bias], [o])
+            add("S", lambda: g.scalar.activation(real(o), real(i), f, bias=arg(bias), scale=arg(scale)), [i, scale, bias], [o], _ns(o, i, 1.0))
         else:
-            add("S", lambda: g.scalar.activation(real(o), real(i), f, bias=arg(bias), scale=arg(scale), accum_out=real(acc)), [i, scale, bias], [o, acc])
+            add("S", lambda: g.scalar.activation(real(o), real(i), f, bias=arg(bias), scale=arg(scale), accum_out=real(acc)), [i, scale, bias], [o, acc], _ns(o, i, 1.0))
 
     def zero(o, n):
         act(o, v("ones", 0, n), 0.0)
 
-    def mm(o, l, b, rq, rs, start=True, stop=True, waits=()):
+    def mm(o, l, b, rq, rs, start=True, stop=True, waits=(), behind=()):
         lq, ls = v("q" + l, 128 * b, 128 * b + 128), v("s" + l, 128 * b, 128 * b + 128)
-        add("P", lambda: g.tensor.matmul_mx(real(o), real(lq), real(ls), real(rq), real(rs), start, stop), [lq, ls, rq, rs], [o], waits)
+        add("P", lambda: g.tensor.matmul_mx(real(o), real(lq), real(ls), real(rq), real(rs), start, stop), [lq, ls, rq, rs], [o], 0.6 * (_len(rq) + 16),
+            waits, "c", behind)
 
     def iota(o, pattern, base, cm):
         if _SB[o[0]][1] == I32:
-            add("G", lambda: g.iota(real(o), pattern, base, cm), [], [o])
+            add("G", lambda: g.iota(real(o), pattern, base, cm), [], [o], 130 + 2 * CY * _len(o))
         else:
-            add("G", lambda: g.iota(real(o), pattern, base, cm, allow_small_or_imprecise_dtypes=True), [], [o])
+            add("G", lambda: g.iota(real(o), pattern, base, cm, allow_small_or_imprecise_dtypes=True), [], [o], 130 + 2 * CY * _len(o))
 
     def select(o, i, pattern, op, base, cm):
-        add("G", lambda: g.affine_select(real(o), real(i), pattern, op, 0.0, base, cm), [i], [o])
+        add("G", lambda: g.affine_select(real(o), real(i), pattern, op, 0.0, base, cm), [i], [o], 170 + 2 * CY * _len(o))
 
-    def dma(q, mk_out, mk_in, ins, outs):
+    def dma(q, mk_out, mk_in, ins, outs, ns=LOAD):
         e = g.sync if q == "Y" else g.scalar
-        add(q, lambda: e.dma_start(mk_out(), mk_in()), ins, outs, (), "d")
+        lands[add(q, lambda: e.dma_start(mk_out(), mk_in()), ins, outs, 60.0, (), "d")] = ns
 
     sent = [0]
 
@@ -171,7 +190,7 @@ def rank_program(g, core, T, topo):
         rid, pid, _ = topo.addr(peer)
         m = topo.mask(core, peer)
         sent[0] += len(topo.engines(core, peer))
-        add("G", lambda: g.remote_dma(real(o, cast), real(i, cast), T.sem[sem], T.sem.sent, pid, rid, m), [i], [], (), "r")
+        return add("G", lambda: g.remote_dma(real(o, cast), real(i, cast), T.sem[sem], T.sem.sent, pid, rid, m), [i], [], 400.0, (), "r")
 
     def bank(b, n=C, p0=0, p1=128):
         return ("ps", p0, p1, 512 * b, 512 * b + n, 1)
@@ -191,15 +210,23 @@ def rank_program(g, core, T, topo):
     def even(name):
         return v(name, 0, None, 2)
 
+    def ends(name):
+        return v(name, 31, None, 32)
+
+    def starts(name):
+        return v(name, 0, None, 32)
+
     for k in range(2):
-        dma("Y", lambda k=k: T.pr[16 * k:16 * k + 16, 0:24], lambda: T.p0[:], [], [v("pr", 0, 24, 1, 16 * k, 16 * k + 16)])
-        dma("S", lambda k=k: T.pr[16 * k:16 * k + 16, 24:48], lambda: T.p1[:], [], [v("pr", 24, 48, 1, 16 * k, 16 * k + 16)])
-    dma("S", lambda: T.ut[:], lambda: T.u[:], [], [v("ut")])
+        dma("Y", lambda k=k: T.pr[16 * k:16 * k + 16, 0:24], lambda: T.p0[:], [], [v("pr", 0, 24, 1, 16 * k, 16 * k + 16)], LOAD + 3000)
+        dma("S", lambda k=k: T.pr[16 * k:16 * k + 16, 24:48], lambda: T.p1[:], [], [v("pr", 24, 48, 1, 16 * k, 16 * k + 16)], LOAD + 3000)
+    dma("S", lambda: T.ut[:], lambda: T.u[:], [], [v("ut")], LOAD + 300)
     for k in range(2):
-        dma("Y", lambda k=k: T.xt[:, 4 * HC * k:4 * HC * (k + 1)], lambda k=k: T.x[:, 4 * HC * k:4 * HC * (k + 1)], [], [v("xt", 4 * HC * k, 4 * HC * (k + 1))])
+        dma("Y", lambda k=k: T.xt[:, 4 * HC * k:4 * HC * (k + 1)], lambda k=k: T.x[:, 4 * HC * k:4 * HC * (k + 1)], [], [v("xt", 4 * HC * k, 4 * HC * (k + 1))],
+            LOAD + 1200 + 800 * k)
     dma("Y", lambda: T.qw[:].bitcast(dt.uint8), lambda: T.wc[:], [], [v("qw")])
     dma("Y", lambda: T.sw[:], lambda: T.ws[:], [], [v("sw")])
-    dma("Y", lambda: T.vt[:], lambda: T.v[:], [], [v("vt")])
+    dma("Y", lambda: T.vt[:], lambda: T.v[:], [], [v("vt")], 10 * LOAD)
+    loads = len(ops)
 
     fill(v("ones"), 1.0)
     fill(v("eye"), 32.0)
@@ -216,7 +243,7 @@ def rank_program(g, core, T, topo):
     iota(v("colc"), [[0, 2], [32, 6], [0, 2]], -HC, 0)
     select(v("mcl"), v("ones"), [[0, 12], [1, 32]], A.is_gt, 0, 0)
     select(v("m16"), v("ones"), [[0, 24], [1, 16]], A.is_gt, 0, 0)
-    for name in ("cd0", "wa", "wb"):
+    for name in ("cd0", "wa", "wb", "hd"):
         zero(v(name), 192)
     for k, (c, op) in enumerate(((15, A.bitwise_and), (31, A.bitwise_and), (6, A.logical_shift_right), (16, A.bitwise_and),
                                  (1, A.bitwise_and), (14, A.bitwise_and), (63, A.bitwise_and))):
@@ -244,64 +271,70 @@ def rank_program(g, core, T, topo):
     act(v("eqc"), v("eqb", 0, 96), -2.0)
     fill(v("tmp2", 0, 96, 32), 0.0)
     copy(v("pr", 0, 48, 1, 32, 64), v("pr", 0, 48, 1, 0, 32))
+    copy(v("pr", 0, 48, 1, 64, 96), v("pr", 0, 48, 1, 0, 32))
+    copy(v("pr", 0, 48, 1, 96, 128), v("pr", 0, 48, 1, 0, 32))
     tt(v("tmp3", 96, 192), v("tmp3", 0, 96), v("tmp2", 96, 192), A.add)
-    copy(v("pr", 0, 48, 1, 64, 128), v("pr", 0, 48, 1, 0, 64))
     tt(v("tmp3", 192, 288), v("tmp3", 96, 192), v("tmp2", 0, 96), A.add)
     for k in range(2):
-        ts(v("lpf", 16 * k, 16 * k + 16), ind(v("pr", 24 * k, 24 * k + 24), col("sel", 0)), Q192, A.add)
+        ts(v("lp", 16 * k, 16 * k + 16), ind(v("pr", 24 * k, 24 * k + 24), col("sel", 0)), Q192, A.add)
+    ts(v("lpf"), ind(v("pr", 24, 48), col("sel", 0)), Q192, A.add)
     quant(v("qu"), v("su"), v("ut"))
-    copy(v("lp"), v("lpf"))
     pick(v("qup"), ind(v("qu"), v("uoff")))
     copy(v("sup"), ind(v("su"), v("uoff")))
     LP0, LP1 = v("lp", 0, 6), v("lp", 16, 22)
     act(v("p0f"), ind(v("fio"), LP0))
     ts(v("p1c", 0, 6), v("p1c", 0, 6), SB32, A.add, -0.625, A.add)
     quant_half("qx", "sx", "xt", 0)
-    tt(v("tmp4", 96, 192), ind(v("fio"), LP1), v("tmp3", 192, 288), A.subtract)
     quant_half("qx", "sx", "xt", 1)
+    tt(v("tmp4", 96, 192), ind(v("fio"), LP1), v("tmp3", 192, 288), A.subtract)
 
     def scores(k):
         mm(bank(k, HC), "up", 0, half("qx", k), half("sx", k))
+        if k:
+            copy(v("ssb", 0, HC, 1, 64, 128), bank(1, HC, 64, 128))
+        else:
+            act(v("ssb", 0, HC, 1, 0, 64), bank(0, HC, 0, 64))
 
     for k in range(2):
         scores(k)
     tt(v("tmp4", 0, 96), ind(v("fio"), LP1), v("p0f"), A.subtract)
     act(odd("cd1"), v("tmp4", 96, 192), -16.0)
-    act(v("ssb", 0, HC, 1, 0, 64), bank(0, HC, 0, 64))
     act(even("cd1"), v("tmp4", 0, 96), 16.0)
-    tt(v("p1w", 0, 6), v("lpf", 16, 22), v("p1c", 0, 6), A.subtract)
-    tt(v("tmp2", 0, 96), v("tmp4", 0, 96), v("eqc"), A.mult)
+    tt(v("p1w", 0, 6), v("lpf", 0, 6), v("p1c", 0, 6), A.subtract)
+    tt(v("tmp2", 192, 288), v("tmp4", 0, 96), v("eqc"), A.mult)
     act(v("p1w", 0, 6), v("p1w", 0, 6), 2.0 / SMALL)
-
-    def early_constants():
-        for name in ("wc4", "wd"):
-            act(even(name), v("fio", 0, 96), -16.0, -8 * 1.45)
-        act(I1, PI, 1.0, 1.0)
-        act(I162, PI, 16.0, 2.0)
-        act(NI162, PI, -16.0, -2.0)
-        act(NI2, PI, -2.0)
-        ts(even("m2"), v("dm", 0, 96), PR, A.is_ge)
-        tt(odd("m2"), v("gtm", 0, 96), v("eqb", 0, 96), A.subtract)
-        ts(ROOT, PR, 0.0, A.is_equal)
-
-    def late_constants():
-        zero(v("sd"), C)
-        zero(v("cd"), C)
-        zero(v("rr"), 64)
-        zero(v("zz", 0, 64), 64)
-        ts(col("aux", 3), P64, 32.0, A.is_ge, 16.0, A.mult)
-        ts(col("aux", 4), P64, 49.0, A.is_ge, 5.0, A.mult)
-        ts(col("aux", 5), P64, 55.0, A.is_ge, 10.0, A.mult)
-        for h in range(2):
-            fill(quad("mcl", 2 * h + 1, 17, C, 32), 0.0)
-            fill(quad("mcl", 2 * h + 1, 23, C, 32), 0.0)
-        ts(col("aux", 6), P64, col("aux", 3), A.subtract, col("aux", 4), A.subtract)
-        act(col("aux", 7), col("aux", 5), 1.0 / 32, 1.0)
-        ts(v("colc"), v("colc"), Q192, A.subtract, PI, A.add)
-        ts(v("swp"), v("pj", 8, 12), PR, A.add)
-        tt(v("mw"), v("eqb"), v("gtm"), A.add)
-        act(PCL, col("aux", 6), -1.0 / 32, col("aux", 7))
-        act(PNB, PCL, -1.0, -1.0 / 64)
+    tt(v("mwa"), v("tmp2", 192, 288), v("gtm", 0, 96), A.add)
+    for name in ("wc4", "wd"):
+        act(even(name), v("fio", 0, 96), -16.0, -8 * 1.45)
+    act(I1, PI, 1.0, 1.0)
+    act(I162, PI, 16.0, 2.0)
+    act(NI162, PI, -16.0, -2.0)
+    act(NI2, PI, -2.0)
+    ts(even("m2"), v("dm", 0, 96), PR, A.is_ge)
+    tt(odd("m2"), v("gtm", 0, 96), v("eqb", 0, 96), A.subtract)
+    ts(ROOT, PR, 0.0, A.is_equal)
+    for b in range(4):
+        quant(v("qe", 128 * b, 128 * b + 128), v("se", 128 * b, 128 * b + 128), v("eye", 3 - b, 515 - b))
+    for name in ("pd", "kd"):
+        ts(v(name), v("ones", 0, 192), 0.0, A.mult)
+    zero(v("sd"), C)
+    zero(v("cd"), C)
+    zero(v("rr"), 64)
+    zero(v("zz", 0, 64), 64)
+    ts(col("aux", 3), P64, 32.0, A.is_ge, 16.0, A.mult)
+    ts(col("aux", 4), P64, 49.0, A.is_ge, 5.0, A.mult)
+    ts(col("aux", 5), P64, 55.0, A.is_ge, 10.0, A.mult)
+    for h in range(2):
+        fill(quad("mcl", 2 * h + 1, 17, C, 32), 0.0)
+        fill(quad("mcl", 2 * h + 1, 23, C, 32), 0.0)
+    ts(col("aux", 6), P64, col("aux", 3), A.subtract, col("aux", 4), A.subtract)
+    act(col("aux", 7), col("aux", 5), 1.0 / 32, 1.0)
+    ts(v("colc"), v("colc"), Q192, A.subtract, PI, A.add)
+    ts(v("swp"), v("pj", 8, 12), PR, A.add)
+    tt(v("mw"), v("eqb"), v("gtm"), A.add)
+    act(PCL, col("aux", 6), -1.0 / 32, col("aux", 7))
+    act(PNB, PCL, -1.0, -1.0 / 64)
+    quant(v("qv"), v("sv"), v("vt"))
 
     def lv(name, l):
         return v(name, 12 * (l // 2) + l % 2, 12 * (l // 2) + 12, 2)
@@ -312,181 +345,134 @@ def rank_program(g, core, T, topo):
     def sm(k):
         return v("sm", 8 * k, 8 * k + 6)
 
-    def gv(l):
-        return v("gg", 8 * l, 8 * l + 6)
-
     def slot(name, s):
         return v(name, 32 * s, 32 * s + 32)
 
     def spread(l):
-        c0, c1, off = lv("w2", l)[3], lv("w2", l)[4], (0, 0, 23, 17)[l]
+        c0, c1, off = lv("gg", l)[3], lv("gg", l)[4], (0, 0, 23, 17)[l]
         for h in range(2):
             for qs in range(2):
-                act(quad("sd", 2 * h + (l > 0), 192 * qs + off, 192 * qs + 192, 32), quad("fpool", 2 * qs + h, c0, c1, 2))
+                act(quad("sd", 2 * h + (l > 0), 192 * qs + off, 192 * qs + 192, 32), quad("fpool", 2 * qs + h, c0, c1, 2), 2.0,
+                    quad("fpool", 2 * qs + h, NI2[3], NI2[4]))
 
-    END = v("ks", 31, None, 32)
-    PP = v("pd", 0, None, 32)
-
-    def same_piece(l):
-        ts(sm(1), PP, MAGIC, A.add, MAGIC, A.subtract)
-        scan(v("bs"), v("m32"), v("pd"), A.mult, A.add)
-        tt(sm(2), lv("w2", l), sm(1), A.add)
-        turn(v("pfree"), v("bs"))
-        tt(sm(3), sm(2), PP, A.min)
-        if l < 3:
-            tt(sm(0), sm(2), PP, A.is_ge)
-
-    def heavy(l):
-        for s in range(6):
-            ts(slot("y1", s), slot("pfree", s), col("sm", 24 + s), A.is_equal, col("gg", 8 * l + s), A.mult)
+    PP = starts("pd")
 
     for t, mask in enumerate(ROUNDS):
         peer = T.cores[rank ^ mask]
         ne = len(topo.engines(peer, core))
         qt, st, ql, sl, lo, li = ["%s%d" % (n, t) for n in ("qt", "st", "ql", "sl", "lo", "li")]
-
-        def unpack(b):
+        for b in range(4):
             mm(bank(4 + b), "e", b, v("qx"), v("sx"))
-
-        def tile_t(b):
             act(v("tt", b, None, 4), bank(4 + b), 1.0 / 32)
-
-        def quant_t(k):
+        for k in range(3):
             quant(v(qt, 128 * k, 128 * k + 128), v(st, 128 * k, 128 * k + 128), v("tt", 512 * k, 512 * k + 512))
-
-        def send_t():
-            send(v(ql), v(qt), peer, "big%d" % t, dt.uint8)
-            send(v(sl), v(st), peer, "big%d" % t)
-
-        copy(v("ssb", 0, HC, 1, 64, 128), bank(1, HC, 64, 128))
-        if t:
-            for b in range(4):
-                unpack(b)
-            tile_t(0)
-            tile_t(1)
-        else:
-            tt(v("mwa"), v("tmp2", 0, 96), v("gtm", 0, 96), A.add)
-        copy(v("sb1"), ind(v("ssb"), LP1))
+        send(v(ql), v(qt), peer, "big%d" % t, dt.uint8)
+        tile_sent = send(v(sl), v(st), peer, "big%d" % t)
+        for b in range(4):
+            act(v("win", WIN * b, WIN * b + C), bank(4 + b), 1.0 / 16)
+        act(v("sb1"), ind(v("ssb"), LP1))
         tt(odd("cd0"), ind(v("ssb"), LP0), v("sb1"), A.is_ge)
-        scan(v("w0"), v("cd0"), v("cd1"), A.mult, A.add)
         scan(v("sca", 0, 96), odd("cd0"), v("mwa"), A.add, A.mult)
+        scan(v("w0"), v("cd0"), v("cd1"), A.mult, A.add)
         act(v("wf"), odd("w0"))
         tt(v("o1f", 0, 6), v("sca", 15, 96, 16), v("p1w", 0, 6), A.add)
         ts(v("o1", 0, 6), v("o1f", 0, 6), SMALL, A.mult)
-        if t:
-            tile_t(2)
-            tile_t(3)
-        else:
-            early_constants()
+        turn(v("wft"), v("wf"))
+        act(v("u1", 0, 6), v("wft", 0, None, 16), -1.0 / 16, MAGIC)
+        ts(v("up1", 0, 6), v("u1", 0, 6), MAGIC, A.subtract, I1, A.add)
         for src, base, off, last, nxt in (("w0", "wf", "o1", "wc4", "o4"), ("wc4", "wg", "o4", "wd", "o16")):
-            for k, dst in enumerate(("wa", "wb", last)):
+            for dst in ("wa", "wb", last):
                 tt(odd(dst), ind(v(src), v(off, 0, 6)), v(base), A.add)
                 src = dst
-                if t == 0 and k < 2:
-                    b = k + 2 * (last == "wd")
-                    quant(v("qe", 128 * b, 128 * b + 128), v("se", 128 * b, 128 * b + 128), v("eye", 3 - b, 515 - b))
-                    unpack(b)
-                if t and last == "wd":
-                    quant_t(k)
             if last == "wd":
                 act(v("x3"), odd("wd"), 1.0, ROOT)
-                if t:
-                    send_t()
             else:
                 act(v("wg"), odd("wc4"))
             scan(v("sca"), v(last), v("m2"), A.add, A.mult)
-            if last == "wc4":
-                turn(v("wft"), v("wf"))
             ts(v(nxt, 0, 6), v("sca", 31, None, 32), SMALL / 8, A.mult)
-            if last == "wc4":
-                act(v("u1", 0, 6), v("wft", 0, None, 16), -1.0 / 16, MAGIC)
-                if t == 0:
-                    tile_t(0)
-                    tile_t(1)
         tt(v("bits"), ind(v("wd"), v("o16", 0, 6)), v("x3"), A.add)
-        ts(v("up1", 0, 6), v("u1", 0, 6), MAGIC, A.subtract, I1, A.add)
         turn(v("bitt"), v("bits"))
         act(v("b2"), v("bitt"), 1.0, NI162, FN.Abs)
         ts(odd("at"), v("bitt"), I162, A.is_ge)
-        if t == 0:
-            for name in ("pd", "kd"):
-                ts(v(name), v("ones", 0, 192), 0.0, A.mult)
         ts(even("at"), v("b2"), 1.0, A.is_equal)
         turn(v("am"), v("at"))
         for s in range(6):
             act(slot("ua", s), slot("am", s), col("up1", s), -1.0)
         scan(v("ws0"), v("m32"), v("am"), A.mult, A.add)
-        W0 = v("ws0", 31, None, 32)
-        ts(gv(0), W0, 1.0 / 64, A.mult, PI, A.add)
+        W0 = ends("ws0")
+        ts(starts("hd"), W0, 16.0, A.is_ge, PI, A.mult)
+        scan(v("h1"), v("m32"), v("hd"), A.mult, A.add)
+        turn(v("h2"), v("h1"))
+        scan(v("h3"), v("m32"), v("h2"), A.mult, A.max)
+        ts(lv("gg", 0), W0, 1.0 / 64, A.mult, PI, A.add)
         ts(sm(0), W0, 16.0, A.is_ge)
         act(lv("w2", 0), W0, 1.0 / 32)
-        tt(v("kd", 0, None, 32), sm(0), gv(0), A.mult)
+        tt(starts("kd"), sm(0), lv("gg", 0), A.mult)
         ts(PP, W0, 0.0, A.mult, 0.5, A.add)
         scan(v("y1"), v("m32"), v("kd"), A.mult, A.add)
-        if t == 0:
-            tile_t(2)
-            tile_t(3)
-            late_constants()
+        act(lv("call", 0), ends("h3"))
         spread(0)
-        for b in range(4):
-            act(v("win", WIN * b, WIN * b + C), bank(4 + b), 1.0 / 16)
-        for l in range(3):
+        for l in range(4):
             if l:
-                same_piece(l)
-                heavy(l)
-            turn(v("y1t"), v("y1"))
-            scan(v("ks"), v("m32"), v("y1t"), A.mult, A.max)
-            ts(lv("call", l), END, MAGIC, A.add, MAGIC, A.subtract)
+                scan(v("bs"), v("m32"), v("pd"), A.mult, A.add)
+                tt(sm(2), lv("w2", l), v("top", 0, 6), A.add)
+                turn(v("pfree"), v("bs"))
+                tt(sm(3), sm(2), PP, A.min)
+                if l < 3:
+                    tt(sm(0), sm(2), PP, A.is_ge)
+                for s in range(6):
+                    ts(slot("y1", s), slot("pfree", s), col("sm", 24 + s), A.is_equal, lvc("gg", l, s), A.mult)
+            for c in (0, 96):
+                turn(v("y1t", c, c + 96), v("y1", c, c + 96))
+                scan(v("ks", c, c + 96), v("m32", c, c + 96), v("y1t", c, c + 96), A.mult, A.max)
+                if l:
+                    c0 = 12 * (l // 2) + l % 2 + c // 16
+                    ts(v("call", c0, c0 + 5, 2), v("ks", c + 31, c + 96, 32), MAGIC, A.add, MAGIC, A.subtract)
+            if l == 3:
+                break
             for s in range(6):
-                ts(slot("y2", s), slot("ua", s), lvc("call", l, s), A.is_equal, col("gg", 8 * l + s), A.mult)
-            tt(sm(4), END, lv("call", l), A.subtract)
+                ts(slot("y2", s), slot("ua", s), lvc("call", l, s) if l else col("h3", 32 * s + 31), A.is_equal, lvc("gg", l, s), A.mult)
+            tt(sm(4), ends("ks"), lv("call", l) if l else ends("h3"), A.subtract)
             turn(v("y2t"), v("y2"))
             tt(sm(5), sm(4), sm(0), A.mult)
             tt(sm(6), PP, sm(4), A.subtract)
             scan(v("rs2"), v("m32"), v("y2t"), A.mult, A.max)
-            tt(gv(l + 1), gv(l), sm(5), A.subtract)
-            tt(PP, v("rs2", 31, None, 32), sm(6), A.max)
-            act(lv("w2", l + 1), gv(l + 1), 2.0, NI2)
+            tt(lv("gg", l + 1), lv("gg", l), sm(5), A.subtract)
+            tt(v("top", 0, 6), ends("rs2"), sm(6), A.max)
+            tt(PP, ends("rs2"), sm(6), A.max)
+            act(lv("w2", l + 1), lv("gg", l + 1), 2.0, NI2)
             spread(l + 1)
-            if t == 0 and l == 0:
-                for k in range(3):
-                    quant_t(k)
-                send_t()
-        same_piece(3)
+        act(v("cg", 0, 24), v("w2"), func=FN.Sign)
+        act(v("cg", 24, 48), v("cg", 0, 24), PI)
+        tt(v("cg", 48, 72), v("colc"), v("cg", 24, 48), A.subtract)
+        tt(v("cg", 96, 120), v("cg", 0, 24), v("call"), A.mult)
+        tt(v("cg", 72, 96), v("cg", 96, 120), v("cg", 48, 72), A.add)
+        for h in range(2):
+            for qq in range(2):
+                for qs in range(2):
+                    (copy if qs else act)(quad("cd", 2 * h + qq, 192 * qs, 192 * qs + 192, 16), quad("cg", 2 * qs + h, 72 + 12 * qq, 84 + 12 * qq))
+        scan(v("cbs"), v("m16"), v("cd"), A.mult, A.add)
+        turn(v("cf"), v("cbs"))
         scan(v("sbs"), v("mcl"), v("sd"), A.mult, A.add)
         turn(v("sf"), v("sbs"))
         act(v("sgn"), v("sf"), 1.0, PNB, FN.Sign, col("cnt", 0))
         act(col("cnt", 1), col("cnt", 0), 0.5, BASE + C / 2)
-        heavy(3)
         ts(v("eq1"), v("sf"), PCL, A.is_equal, 1.0, A.add)
-        turn(v("y1t"), v("y1"))
         turn(v("eqt"), v("eq1"))
-        scan(v("ks"), v("m32"), v("y1t"), A.mult, A.max)
-        ts(v("cg", 0, 24), v("w2"), 0.0, A.is_gt)
-        ts(lv("call", 3), END, MAGIC, A.add, MAGIC, A.subtract)
         scan(v("p2"), v("eq1"), v("ones"), A.add, A.subtract, col("cnt", 1))
-        ts(v("cg", 24, 48), v("call"), PI, A.subtract)
         turn(v("p2t"), v("p2"))
-        tt(v("cg", 48, 72), v("cg", 0, 24), v("cg", 24, 48), A.mult)
         scan(v("rs"), v("eqt"), v("p2t"), A.mult, A.min, BASE)
-        tt(v("cg", 72, 96), v("cg", 48, 72), v("colc"), A.add)
-        for h in range(2):
-            for qq in range(2):
-                for qs in range(2):
-                    act(quad("cd", 2 * h + qq, 192 * qs, 192 * qs + 192, 16), quad("cg", 2 * qs + h, 72 + 12 * qq, 84 + 12 * qq))
         copy(v("rr", 0, 12), v("rs", 31, C, 32))
         for h in range(2):
-            copy(quad("rr", 2 * h, 32, 44), quad("rs", 2 * h + 1, 16, C, 32))
+            act(quad("rr", 2 * h, 32, 44), quad("rs", 2 * h + 1, 16, C, 32))
             copy(quad("rr", 2 * h + 1, 32, 44), quad("rs", 2 * h + 1, 21, C, 32))
         turn(v("t1"), v("rr"))
         copy(v("t2"), ind(v("t1"), v("swp")))
         turn(v("t3"), v("t2"))
-        scan(v("cbs"), v("m16"), v("cd"), A.mult, A.add)
-        ts(v("opl", 0, None, 2), v("t3", 0, 12), -BASE - 0.75, A.add)
-        turn(v("cf"), v("cbs"))
-        ts(v("opl", 1, None, 2), v("t3", 32, 44), -BASE - 0.75, A.add)
+        for hi in range(2):
+            ts(v("opl", hi, None, 2), v("t3", 32 * hi, 32 * hi + 12), -BASE - 0.75, A.add)
         for b in range(4):
-            mm(bank(b), "e", b, v(ql), v(sl), waits=[("big%d" % t, 2 * ne)] if b == 0 else ())
+            mm(bank(b), "e", b, v(ql), v(sl), waits=[("big%d" % t, 2 * ne)], behind=[(tile_sent, TILE)])
             act(v("gall", C * b, C * b + C), bank(b), 1.0 / 32)
         for k in (1, 0):
             for b in range(4):
@@ -494,119 +480,151 @@ def rank_program(g, core, T, topo):
         copy(ind(v("cs"), v("opl")), v("cf"))
         scan(v("csw"), v("cs", 0, K), v("mw"), A.add, A.mult)
         ts(v(lo), v("csw", 15, None, 16), SMALL, A.mult, HC + 0.25, A.add)
-        send(v(li), v(lo), peer, "lst%d" % t)
+        list_sent = send(v(li), v(lo), peer, "lst%d" % t)
         for b in range(4):
             act(v("ee", K * b, K * b + K), ind(v("win", WIN * b, WIN * b + C), v(lo)), 0.5)
         for a in range(2):
-            copy(v("zz", 32 * a, 32 * a + 12), v("cd", 16 * a, None, 32))
-        ts(v("zz", 128, 192), v("rr"), C - HC - BASE - 1.0, A.add)
+            act(v("zz", 32 * a, 32 * a + 12), v("cd", 16 * a, None, 32))
+        act(v("zz", 128, 192), v("rr"), 1.0, C - HC - BASE - 1.0)
         ts(v("zz", 64, 128), v("rr"), BASE + K + 0.5, A.is_lt)
         tt(v("zz", 192, 256), v("zz", 128, 192), v("zz", 0, 64), A.subtract)
         tt(v("zz", 256, 320), v("zz", 192, 256), v("zz", 64, 128), A.mult)
-        tt(v("zz", 128, 192), v("zz", 256, 320), v("zz", 0, 64), A.add)
-        turn(v("z1"), v("zz", 128, 192))
+        tt(v("zz", 320, 384), v("zz", 256, 320), v("zz", 0, 64), A.add)
+        turn(v("z1"), v("zz", 320, 384))
         copy(v("z2"), ind(v("z1"), v("swp")))
         turn(v("z3"), v("z2"))
         for hi in range(2):
             ts(v("ozl", hi, None, 2), v("z3", 32 * hi, 32 * hi + 12), HC + 0.25, A.add)
         if t == 2:
-            ts(v("clo"), v("cf"), float(HC), A.add)
+            act(v("clo"), v("cf"), 1.0, float(HC))
             dma("Y", lambda: T.cl[:], lambda: T.clo[0:128:16, :], [v("clo")], [])
-            quant(v("qv"), v("sv"), v("vt"))
-
-        def zpart(b, k, eng):
-            o = v("zt", 4 * HC * k + b, 4 * HC * (k + 1), 4)
-            i = ind(v("win", WIN * b, WIN * b + WIN), v("ozl", 12 * k, 12 * k + 12))
-            if eng == "V":
-                ts(o, i, 0.5, A.mult)
-            else:
-                act(o, i, 0.5)
-
-        def xpart(b, k, eng):
-            o = v("xn", 4 * HC * k + b, 4 * HC * (k + 1), 4)
-            if eng == "V":
-                ts(o, bank(4 * k + b, HC), 1.0 / 32, A.mult)
-            else:
-                act(o, bank(4 * k + b, HC), 1.0 / 32)
-
-        def layer(k):
+        for b in range(4):
+            tt(v("win", WIN * b + C, WIN * b + WIN), ind(v("gall", C * b, C * b + C), v(li)), v("ee", K * b, K * b + K), A.add,
+               waits=[("lst%d" % t, ne)], behind=[(list_sent, LIST)])
+        for k in range(2):
+            for b in range(4):
+                o = v("zt", 4 * HC * k + b, 4 * HC * (k + 1), 4)
+                i = ind(v("win", WIN * b, WIN * b + WIN), v("ozl", 12 * k, 12 * k + 12))
+                if b == 3:
+                    ts(o, i, 0.5, A.mult)
+                else:
+                    act(o, i, 0.5)
             quant_half("qz", "sz", "zt", k)
             for b in range(4):
                 mm(bank(4 * k + b, HC), "w", b, half("qz", k), half("sz", k), False, True)
-
-        def after(k):
+        for k in range(2):
+            for b in range(4):
+                o = v("xn", 4 * HC * k + b, 4 * HC * (k + 1), 4)
+                if (b % 2 if k else b < 2):
+                    ts(o, bank(4 * k + b, HC), 1.0 / 32, A.mult)
+                else:
+                    act(o, bank(4 * k + b, HC), 1.0 / 32)
             quant_half("qx", "sx", "xn", k)
             if t < 2:
                 scores(k)
             else:
                 mm(bank(k, HC), "v", 0, half("qx", k), half("sx", k))
-                dma("Y", lambda: T.oc[:, 4 * HC * k:4 * HC * (k + 1)], lambda: T.qx[:, HC * k:HC * (k + 1)].bitcast(dt.uint8), [half("qx", k)], [])
+                dma("Y", lambda k=k: T.oc[:, 4 * HC * k:4 * HC * (k + 1)], lambda k=k: T.qx[:, HC * k:HC * (k + 1)].bitcast(dt.uint8), [half("qx", k)], [])
+                (copy if k else act)(half("yo", k), bank(k, HC))
+                dma("Y" if k else "S", lambda k=k: T.y[:, HC * k:HC * (k + 1)], lambda k=k: T.yo[:, HC * k:HC * (k + 1)], [half("yo", k)], [])
 
-        for b in range(4):
-            tt(v("win", WIN * b + C, WIN * b + WIN), ind(v("gall", C * b, C * b + C), v(li)), v("ee", K * b, K * b + K), A.add,
-               waits=[("lst%d" % t, ne)] if b == 0 else ())
-        for b in range(3):
-            zpart(b, 0, "S")
-        zpart(3, 0, "V")
-        layer(0)
-        for b in range(3):
-            zpart(b, 1, "S")
-        zpart(3, 1, "V")
-        xpart(0, 0, "V")
-        xpart(1, 0, "V")
-        layer(1)
-        xpart(2, 0, "S")
-        xpart(3, 0, "S")
-        after(0)
-        xpart(0, 1, "S")
-        xpart(1, 1, "V")
-        xpart(2, 1, "S")
-        xpart(3, 1, "V")
-        if t < 2:
-            act(v("ssb", 0, HC, 1, 0, 64), bank(0, HC, 0, 64))
-        else:
-            act(half("yo", 0), bank(0, HC))
-            dma("S", lambda: T.y[:, 0:HC], lambda: T.yo[:, 0:HC], [half("yo", 0)], [])
-        after(1)
-
-    copy(half("yo", 1), bank(1, HC))
     for k in range(4):
         dma("S" if k % 2 else "Y", lambda k=k: T.osc[4 * k:4 * k + 4, :], lambda k=k: T.sx[32 * k:32 * k + 4, :], [v("sx")], [])
-    dma("Y", lambda: T.y[:, HC:C], lambda: T.yo[:, HC:C], [half("yo", 1)], [])
 
     used = {}
-    seen = {}
-    need = set()
     deps = []
-    for n, (q, call, r, w, waits, kind) in enumerate(ops):
+    for n, op in enumerate(ops):
+        q, r, w = op[0], op[2], op[3]
         hits = set()
         for mine, writes in ((r, False), (w, True)):
             for a in mine:
                 for m, b, wrote in used.get(a[0], ()):
-                    q2 = ops[m][0]
-                    if (writes or wrote or (a[0] == "ps" and q2 != q)) and not (q == "P" and q2 == "P") and _meet(a, b):
+                    if (writes or wrote or a[0] == "ps") and _meet(a, b):
                         hits.add(m)
-        keep = []
-        for m in sorted(hits, reverse=True):
-            key = (q, ops[m][0]) if ops[m][5] == "c" else (q, m)
-            if seen.get(key, -1) < m:
-                seen[key] = m
-                keep.append(m)
-                need.add(m)
-        deps.append(keep)
-        if kind != "r":
+        deps.append(hits)
+        if op[5] != "r":
             for mine, writes in ((r, False), (w, True)):
                 for a in mine:
                     used.setdefault(a[0], []).append((n, a, writes))
+
+    for n in range(4):
+        lands[n] = LOAD
+
+    def gap(m, n):
+        if ops[m][5] == "d":
+            return lands[m]
+        return 0.0 if ops[m][0] == "P" and ops[n][0] == "P" else WAKE
+
+    edges = [[(m, gap(m, n)) for m in deps[n]] + ops[n][7] for n in range(len(ops))]
+    tail = [op[6] + (LOAD if op[5] == "d" else 0.0) for op in ops]
+    later = [[] for _ in ops]
+    for n in range(len(ops) - 1, -1, -1):
+        for m, d in edges[n]:
+            tail[m] = max(tail[m], ops[m][6] + d + tail[n])
+            later[m].append(n)
+    for n in range(loads):
+        tail[n] = 1e9 - n
+    left = [len(e) for e in edges]
+    ready = {q: [] for q in "VSPGY"}
+    at = {}
+    for n in range(len(ops)):
+        if not left[n]:
+            ready[ops[n][0]].append(n)
+            at[n] = 0.0
+    free = {q: 0.0 for q in ready}
+    end = {}
+    order = []
+    while len(order) < len(ops):
+        best = None
+        for q, c in ready.items():
+            if not c:
+                continue
+            first = max(c, key=lambda n: (tail[n], -n))
+            s = max(free[q], at[first])
+            fit = [n for n in c if max(free[q], at[n]) + ops[n][6] <= s + 40.0]
+            n = max(fit, key=lambda n: (tail[n], -n)) if fit and s > free[q] else first
+            s = max(free[q], at[n])
+            if best is None or s < best[0]:
+                best = (s, n)
+        s, n = best
+        q = ops[n][0]
+        ready[q].remove(n)
+        free[q] = end[n] = s + ops[n][6]
+        order.append(n)
+        for k in later[n]:
+            left[k] -= 1
+            if not left[k]:
+                at[k] = max(end[m] + d for m, d in edges[k])
+                ready[ops[k][0]].append(k)
+
+    place = {n: k for k, n in enumerate(order)}
+    seen = {}
+    need = set()
+    keep = {}
+    for n in order:
+        q = ops[n][0]
+        keep[n] = []
+        for m in sorted(deps[n], key=lambda m: -place[m]):
+            if q == "P" and ops[m][0] == "P":
+                continue
+            key = (q, ops[m][0]) if ops[m][5] == "c" else (q, m)
+            if seen.get(key, -1) < place[m]:
+                seen[key] = place[m]
+                keep[n].append(m)
+                need.add(m)
     queue = {"V": g.vector, "S": g.scalar, "P": g.tensor, "G": g, "Y": g.sync}
     count = {"V": 0, "S": 0, "P": 0, "G": 0}
     mark = {}
+    waited = set()
     ndma = 0
-    for n, (q, call, r, w, waits, kind) in enumerate(ops):
-        for m in deps[n]:
+    for n in order:
+        q, call, waits, kind = ops[n][0], ops[n][1], ops[n][4], ops[n][5]
+        for m in keep[n]:
             queue[q].wait_ge(T.sem[mark[m][0]], mark[m][1])
         for s, val in waits:
-            queue[q].wait_ge(T.sem[s], val)
+            if s not in waited:
+                waited.add(s)
+                queue[q].wait_ge(T.sem[s], val)
         done = call()
         if kind == "d":
             mark[n] = ("d%d" % ndma, 16)

@@ -3,12 +3,13 @@ from concourse.mybir import dt, AluOpType, ActivationFunctionType
 C, K, ROUNDS = 384, 160, (1, 2, 3)
 HC = C // 2
 F32, BF, HF, I32, U16, MX, U8 = "float32", "bfloat16", "float16", "int32", "uint16", "float8_e4m3fn_x4", "uint8"
-MAGIC = 12582912.0
-BIG = 1048576.0
-SMALL = 262144.0
+BIG = 2.0 ** 20
+SMALL = 2.0 ** 18
+TINY = 2.0 ** -60
 WIN = C + K
-BASE = 1024.0
-CY, WAKE, LOAD, LIST, TILE = 0.95, 170.0, 2500.0, 2600.0, 6000.0
+SG = 1.0 / 64
+EPS = SG / 64
+WAKE, LOAD, LIST, TILE = 170.0, 2200.0, 2300.0, 12000.0
 
 _SB = {
     "xt": (4 * C, BF), "xn": (4 * C, BF), "ut": (512, BF), "vt": (512, BF), "eye": (528, BF),
@@ -16,20 +17,20 @@ _SB = {
     "qv": (128, MX), "sv": (128, U8), "qw": (512, MX), "sw": (512, U8), "qe": (512, MX), "se": (512, U8),
     "qz": (C, MX), "sz": (C, U8), "tt": (4 * C, BF), "zt": (4 * C, BF),
     "win": (4 * WIN, F32), "gall": (4 * C, F32), "ee": (4 * K, F32), "yo": (C, F32), "clo": (C, F32),
-    "pr": (48, I32), "pi": (8, I32), "pj": (16, I32), "top": (8, I32), "fio": (192, F32), "p0f": (96, F32),
-    "dm": (K, F32), "eqm": (K, F32), "eqb": (K, F32), "gtm": (K, F32), "mw": (K, F32), "mwa": (96, F32), "m2": (192, F32),
-    "cd0": (192, F32), "cd1": (192, F32), "eqc": (96, F32), "tmp": (192, F32), "tmp2": (288, F32), "tmp3": (288, F32), "tmp4": (192, F32),
-    "m32": (192, BF), "m16": (C, BF), "mcl": (C, BF), "ones": (C, BF),
-    "ssb": (192, F32), "sb1": (96, F32), "sca": (192, F32),
-    "w0": (192, F32), "wa": (192, F32), "wb": (192, F32), "wc4": (192, F32), "wd": (192, F32), "x3": (96, F32),
-    "wf": (96, F32), "wg": (96, F32), "wft": (96, F32),
-    "bits": (96, F32), "bitt": (96, F32), "b2": (96, BF), "at": (192, BF), "am": (192, BF), "ua": (192, BF), "ws0": (192, BF),
-    "hd": (192, BF), "h1": (192, BF), "h2": (192, BF), "h3": (192, F32),
-    "pd": (192, HF), "kd": (192, HF), "bs": (192, HF), "pfree": (192, HF), "y1": (192, HF), "y1t": (192, HF), "ks": (192, HF),
-    "y2": (192, HF), "y2t": (192, HF), "rs2": (192, HF),
-    "sd": (C, BF), "sbs": (C, BF), "sf": (C, BF), "eq1": (C, BF), "eqt": (C, BF), "sgn": (C, BF),
-    "p2": (C, HF), "p2t": (C, HF), "rs": (C, F32),
-    "cd": (C, BF), "cbs": (C, BF), "cf": (C, BF), "cs": (C, F32), "csw": (K, F32), "zz": (384, F32),
+    "pr": (48, I32), "pi": (8, I32), "pj": (16, I32),
+    "ones": (C, BF), "m32": (192, BF), "m16": (C, BF), "mcl": (C, BF), "mx0": (192, BF), "rst": (192, BF),
+    "fi": (192, BF), "flo": (192, BF), "fb": (192, BF), "dm": (K, BF), "gtm": (96, BF),
+    "mw": (K, BF), "mo": (192, BF), "me": (192, BF), "tmp": (192, BF), "tmp2": (288, BF), "tmp3": (384, BF), "tmp4": (192, BF),
+    "cd0": (208, BF), "d1p": (192, BF), "d1b": (192, BF), "sr": (96, BF),
+    "ssb": (192, F32), "sb1": (96, F32), "sca": (192, BF),
+    "pa": (192, BF), "pb": (192, BF), "pc": (192, BF), "cv": (288, BF), "ba": (192, BF), "bb": (192, BF), "bc": (192, BF),
+    "vv": (192, BF), "bm": (192, BF), "se2": (192, BF), "so": (96, BF), "yb": (192, BF), "yrow": (192, BF), "ybs": (192, BF),
+    "pk": (192, BF), "ub": (192, BF), "utn": (192, BF), "gq": (192, HF),
+    "idr": (192, BF), "ids": (192, BF), "idb": (192, BF), "gr0": (192, HF), "gr1": (192, HF), "gd": (192, HF), "gb": (192, HF),
+    "cs": (192, BF), "cz": (192, BF), "ks": (192, HF), "dd": (192, BF), "sa": (192, HF), "sb": (192, BF), "pbc": (192, HF), "prow": (192, HF),
+    "y1": (192, BF), "yt": (192, BF),
+    "sd": (C, BF), "sbs": (C, BF), "sf": (C, BF), "eq2": (C, BF), "eqt": (C, BF), "sgn": (C, BF), "p2": (C, BF), "p2t": (C, BF), "rs": (1024, BF),
+    "cd": (C, BF), "cbs": (C, BF), "cf": (C, BF), "cw": (C, BF), "csw": (K, BF),
 }
 for _t in range(3):
     _SB["qt%d" % _t] = (C, MX)
@@ -40,17 +41,19 @@ for _t in range(3):
     _SB["li%d" % _t] = (10, U16)
 _PART = {}
 for _pool, _d, _names in (
-        ("fpool", F32, {"pf": 24, "aux": 16, "lpf": 16, "p1w": 8, "p1c": 8, "o1f": 8, "u1": 8, "up1": 8, "gg": 24, "w2": 24, "call": 24,
-                        "sm": 64, "cnt": 8, "rr": 64, "t1": 64, "t2": 64, "t3": 64, "cg": 120, "colc": 24, "z1": 64, "z2": 64, "z3": 64}),
-        ("upool", U16, {"uoff": 8, "sel": 8, "lp": 32, "o1": 8, "o4": 8, "o16": 8, "swp": 4, "opl": 24, "ozl": 24})):
+        ("fpool", F32, {"pf": 24, "aux": 8, "pcc": 6, "pc1": 6, "pc2": 6, "ws0": 12, "ws1": 12, "ws2": 12, "ws3": 12, "wd": 12, "xx": 6, "pp": 6,
+                        "cand": 6, "nn": 6, "n62": 6, "cg0": 48, "cg1": 48, "cg2": 48, "colc": 24, "cnt": 1, "kk": 44, "ky": 44, "km": 44, "kn": 44}),
+        ("bpool", BF, {"t1": 64, "t2": 64, "t3": 64, "zz": 64, "z1": 64, "z2": 64, "z3": 64,
+                       "b1": 96, "p4": 96, "p7": 96, "p10": 96, "b4": 96, "b7": 96, "b10": 96, "b13": 96, "b20": 96, "bx": 96}),
+        ("upool", U16, {"uoff": 8, "sel": 2, "lp": 32, "o1": 6, "o3": 6, "o7": 6, "o10": 6, "swp": 4, "opl": 24, "ozl": 24})):
     _at = 0
     for _k, _n in _names.items():
         _PART[_k] = (_pool, _at, _n)
-        _at += (_n + 7) // 8 * 8
+        _at += (_n + 15) // 16 * 16
     _SB[_pool] = (_at, _d)
 SCRATCH = {k: ("sbuf", [128, n], d) for k, (n, d) in _SB.items()}
 SCRATCH["ps"] = ("psum", [128, 4096], F32)
-NDMA = 20
+NDMA = 24
 SEMAPHORES = ["cV", "cS", "cP", "cG", "sent"] + ["d%d" % k for k in range(NDMA)] + ["big%d" % t for t in range(3)] + ["lst%d" % t for t in range(3)]
 
 A = AluOpType
@@ -70,28 +73,44 @@ def col(name, c):
     return v(name, c, c + 1)
 
 
+def back(a):
+    return a[:5] + (-a[5],)
+
+
+def on(a, q):
+    return (a[0], 32 * q, 32 * q + 32) + a[3:]
+
+
+def _len(a):
+    return 16 * _len(a[2]) if a[0] == "@" else len(range(a[3], a[4], abs(a[5])))
+
+
+_COLS = {}
+
+
+def _cols(a):
+    k = a[3:]
+    if k not in _COLS:
+        _COLS[k] = sum(1 << c for c in range(a[3], a[4], abs(a[5])))
+    return _COLS[k]
+
+
 def _meet(a, b):
     if a[0] == "ps":
         return a[3] // 512 == b[3] // 512
     if a[2] <= b[1] or b[2] <= a[1] or a[4] <= b[3] or b[4] <= a[3]:
         return False
-    if a[5] == b[5] and a[5] > 1 and (a[3] - b[3]) % a[5]:
-        return False
-    return True
+    return bool(_cols(a) & _cols(b))
 
 
-def _len(a):
-    return 16 * _len(a[2]) if a[0] == "@" else (a[4] - a[3] + a[5] - 1) // a[5]
-
-
-def _ns(o, i, rate=None):
+def _ns(o, ins, rate=None):
     if o[0] == "@":
-        return 50 + 3.2 * _len(o)
-    if i[0] == "@":
-        return 55 + 1.3 * _len(i)
+        return 50 + 3.5 * _len(o)
+    if ins[0][0] == "@":
+        return 55 + 1.5 * _len(o)
     if rate is None:
-        rate = 0.5 if all(a[0] != "ps" and _SB[a[0]][1] in (BF, HF) for a in (o, i)) else 1.0
-    return max(64, rate * _len(i)) * CY
+        rate = 0.5 if all(a[0] != "ps" and _SB[a[0]][1] in (BF, HF) for a in [o] + ins) else 1.0
+    return max(64, rate * _len(o))
 
 
 def rank_program(g, core, T, topo):
@@ -105,6 +124,8 @@ def rank_program(g, core, T, topo):
         if a[0] == "@":
             return real(a[1], cast).indirect(real(a[2]))
         name, p0, p1, c0, c1, step = a
+        if step < 0:
+            return T[name][p0:p1, range(c0, c1, -step)[-1]:(c0 - 1 if c0 else None):step]
         r = T[name][p0:p1, c0:c1] if step == 1 else T[name][p0:p1, c0:c1:step]
         return r.bitcast(cast) if cast is not None else r
 
@@ -130,41 +151,42 @@ def rank_program(g, core, T, topo):
         return len(ops) - 1
 
     def copy(o, i):
-        add("V", lambda: g.vector.tensor_copy(real(o), real(i)), [i], [o], _ns(o, i))
+        add("V", lambda: g.vector.tensor_copy(real(o), real(i)), [i], [o], _ns(o, [i]))
 
     def pick(o, i):
-        add("V", lambda: g.vector.tensor_copy(real(o, dt.uint32), real(i, dt.uint32)), [i], [o], _ns(o, i))
+        add("V", lambda: g.vector.tensor_copy(real(o, dt.uint32), real(i, dt.uint32)), [i], [o], _ns(o, [i]))
 
     def tt(o, a, b, op, waits=(), behind=()):
-        add("V", lambda: g.vector.tensor_tensor(real(o), real(a), real(b), op), [a, b], [o], _ns(o, a, 2.0), waits, "c", behind)
+        add("V", lambda: g.vector.tensor_tensor(real(o), real(a), real(b), op), [a, b], [o], _ns(o, [a], 2.0), waits, "c", behind)
 
     def ts(o, a, s1, op0, s2=None, op1=None):
         if op1 is None:
-            add("V", lambda: g.vector.tensor_scalar(real(o), real(a), arg(s1), None, op0), [a, s1], [o], _ns(o, a))
+            add("V", lambda: g.vector.tensor_scalar(real(o), real(a), arg(s1), None, op0), [a, s1], [o], _ns(o, [a]))
         else:
-            add("V", lambda: g.vector.tensor_scalar(real(o), real(a), arg(s1), arg(s2), op0, op1), [a, s1, s2], [o], _ns(o, a))
+            add("V", lambda: g.vector.tensor_scalar(real(o), real(a), arg(s1), arg(s2), op0, op1), [a, s1, s2], [o], _ns(o, [a]))
 
     def scan(o, d0, d1, op0, op1, init=0.0):
-        add("V", lambda: g.vector.tensor_tensor_scan(real(o), real(d0), real(d1), arg(init), op0, op1), [d0, d1, init], [o], _ns(o, d1))
+        add("V", lambda: g.vector.tensor_tensor_scan(real(o), real(d0), real(d1), arg(init), op0, op1), [d0, d1, init], [o], _ns(o, [d0, d1]))
 
     def turn(o, i):
-        add("V", lambda: g.vector.transpose(real(o), real(i)), [i], [o], _ns(o, i))
+        add("V", lambda: g.vector.transpose(real(o), real(i)), [i], [o], _ns(o, [i]))
 
     def fill(o, c):
-        add("V", lambda: g.vector.memset(real(o), c), [], [o], _ns(o, o))
+        add("V", lambda: g.vector.memset(real(o), c), [], [o], _ns(o, [o]))
 
     def quant(q, s, i):
-        add("V", lambda: g.vector.quantize_mx(real(q), real(s), real(i)), [i], [q, s], 15 + 0.25 * _len(i))
+        add("V", lambda: g.vector.quantize_mx(real(q), real(s), real(i)), [i], [q, s], 15 + 0.265 * _len(i))
 
     def act(o, i, scale=1.0, bias=0.0, func=None, acc=None):
         f = func if func is not None else (FN.Copy if not isinstance(bias, tuple) and bias == 0.0 else FN.Identity)
         if acc is None:
-            add("S", lambda: g.scalar.activation(real(o), real(i), f, bias=arg(bias), scale=arg(scale)), [i, scale, bias], [o], _ns(o, i, 1.0))
+            add("S", lambda: g.scalar.activation(real(o), real(i), f, bias=arg(bias), scale=arg(scale)), [i, scale, bias], [o], _ns(o, [i], 1.0))
         else:
-            add("S", lambda: g.scalar.activation(real(o), real(i), f, bias=arg(bias), scale=arg(scale), accum_out=real(acc)), [i, scale, bias], [o, acc], _ns(o, i, 1.0))
+            add("S", lambda: g.scalar.activation(real(o), real(i), f, bias=arg(bias), scale=arg(scale), accum_out=real(acc)), [i, scale, bias], [o, acc],
+                20 + _ns(o, [i], 1.0))
 
-    def zero(o, n):
-        act(o, v("ones", 0, n), 0.0)
+    def const(o, c):
+        act(o, (("ones",) + o[1:3] + (0, _len(o), 1)), c)
 
     def mm(o, l, b, rq, rs, start=True, stop=True, waits=(), behind=()):
         lq, ls = v("q" + l, 128 * b, 128 * b + 128), v("s" + l, 128 * b, 128 * b + 128)
@@ -173,12 +195,12 @@ def rank_program(g, core, T, topo):
 
     def iota(o, pattern, base, cm):
         if _SB[o[0]][1] == I32:
-            add("G", lambda: g.iota(real(o), pattern, base, cm), [], [o], 130 + 2 * CY * _len(o))
+            add("G", lambda: g.iota(real(o), pattern, base, cm), [], [o], 130 + 2 * _len(o))
         else:
-            add("G", lambda: g.iota(real(o), pattern, base, cm, allow_small_or_imprecise_dtypes=True), [], [o], 130 + 2 * CY * _len(o))
+            add("G", lambda: g.iota(real(o), pattern, base, cm, allow_small_or_imprecise_dtypes=True), [], [o], 130 + 2 * _len(o))
 
     def select(o, i, pattern, op, base, cm):
-        add("G", lambda: g.affine_select(real(o), real(i), pattern, op, 0.0, base, cm), [i], [o], 170 + 2 * CY * _len(o))
+        add("G", lambda: g.affine_select(real(o), real(i), pattern, op, 0.0, base, cm), [i], [o], 170 + 2 * _len(o))
 
     def dma(q, mk_out, mk_in, ins, outs, ns=LOAD):
         e = g.sync if q == "Y" else g.scalar
@@ -190,13 +212,10 @@ def rank_program(g, core, T, topo):
         rid, pid, _ = topo.addr(peer)
         m = topo.mask(core, peer)
         sent[0] += len(topo.engines(core, peer))
-        return add("G", lambda: g.remote_dma(real(o, cast), real(i, cast), T.sem[sem], T.sem.sent, pid, rid, m), [i], [], 400.0, (), "r")
+        return add("G", lambda: g.remote_dma(real(o, cast), real(i, cast), T.sem[sem], T.sem.sent, pid, rid, m), [i], [], 300.0, (), "r")
 
     def bank(b, n=C, p0=0, p1=128):
         return ("ps", p0, p1, 512 * b, 512 * b + n, 1)
-
-    def quad(name, q, c0, c1, step=1):
-        return v(name, c0, c1, step, 32 * q, 32 * q + 32)
 
     def half(name, k):
         return v(name, HC * k, HC * k + HC)
@@ -216,77 +235,56 @@ def rank_program(g, core, T, topo):
     def starts(name):
         return v(name, 0, None, 32)
 
+    def slot(name, s, first=0):
+        return v(name, 32 * s + first, 32 * s + 32)
+
+    dma("S", lambda: T.ut[:], lambda: T.u[:], [], [v("ut")], LOAD + 500)
     for k in range(2):
-        dma("Y", lambda k=k: T.pr[16 * k:16 * k + 16, 0:24], lambda: T.p0[:], [], [v("pr", 0, 24, 1, 16 * k, 16 * k + 16)], LOAD + 3000)
-        dma("S", lambda k=k: T.pr[16 * k:16 * k + 16, 24:48], lambda: T.p1[:], [], [v("pr", 24, 48, 1, 16 * k, 16 * k + 16)], LOAD + 3000)
-    dma("S", lambda: T.ut[:], lambda: T.u[:], [], [v("ut")], LOAD + 300)
+        dma("Y", lambda k=k: T.pr[16 * k:16 * k + 16, 0:24], lambda: T.p0[:], [], [v("pr", 0, 24, 1, 16 * k, 16 * k + 16)])
+        dma("S", lambda k=k: T.pr[16 * k:16 * k + 16, 24:48], lambda: T.p1[:], [], [v("pr", 24, 48, 1, 16 * k, 16 * k + 16)])
     for k in range(2):
         dma("Y", lambda k=k: T.xt[:, 4 * HC * k:4 * HC * (k + 1)], lambda k=k: T.x[:, 4 * HC * k:4 * HC * (k + 1)], [], [v("xt", 4 * HC * k, 4 * HC * (k + 1))],
-            LOAD + 1200 + 800 * k)
-    dma("Y", lambda: T.qw[:].bitcast(dt.uint8), lambda: T.wc[:], [], [v("qw")])
-    dma("Y", lambda: T.sw[:], lambda: T.ws[:], [], [v("sw")])
-    dma("Y", lambda: T.vt[:], lambda: T.v[:], [], [v("vt")], 10 * LOAD)
-    loads = len(ops)
+            LOAD + 900)
 
     fill(v("ones"), 1.0)
     fill(v("eye"), 32.0)
+    loads = len(ops)
     iota(col("pi", 0), [[0, 1]], 0, 1)
     iota(v("pj", 0, 8), [[0, 2], [64, 2], [0, 2]], 0, 0)
-    iota(v("dm"), [[0, K // 16], [1, 16]], 0, 0)
-    iota(v("tmp", 0, 96), [[0, 3], [1, 32]], 0, 0)
-    iota(v("tmp", 96, 192), [[64, 3], [1, 32]], 0, 0)
-    iota(v("p1c", 0, 6), [[32, 3], [0, 2]], 0, 0)
-    iota(v("fio"), [[1, 192]], 0, 0)
     select(v("eye"), v("eye"), [[-1, 528]], A.is_equal, 3, 4)
-    select(v("m32"), v("ones", 0, 192), [[0, 6], [1, 32]], A.is_gt, 0, 0)
     iota(v("pj", 8, 12), [[16, 2], [32, 2]], 0, 0)
     iota(v("colc"), [[0, 2], [32, 6], [0, 2]], -HC, 0)
-    select(v("mcl"), v("ones"), [[0, 12], [1, 32]], A.is_gt, 0, 0)
-    select(v("m16"), v("ones"), [[0, 24], [1, 16]], A.is_gt, 0, 0)
-    for name in ("cd0", "wa", "wb", "hd"):
-        zero(v(name), 192)
+    for name, n, w in (("m32", 32, 192), ("m16", 16, K)):
+        fill(v(name, 0, w), 1.0)
+        fill(v(name, 0, w, n), 0.0)
+    const(v("m16", K), 1.0)
+    const(v("m16", K, None, 16), 0.0)
+    scan(v("fi"), v("m32"), v("m32"), A.mult, A.add)
+    scan(v("dm"), v("m16", 0, K), v("m16", 0, K), A.mult, A.add)
+    for b in range(3):
+        act(v("flo", 64 * b, 64 * b + 64), v("fi", 64 * b, 64 * b + 64), 1.0, 32.0 * b)
     for k, (c, op) in enumerate(((15, A.bitwise_and), (31, A.bitwise_and), (6, A.logical_shift_right), (16, A.bitwise_and),
-                                 (1, A.bitwise_and), (14, A.bitwise_and), (63, A.bitwise_and))):
+                                 (1, A.bitwise_and), (14, A.bitwise_and))):
         ts(col("pi", k + 1), col("pi", 0), c, op)
     copy(v("uoff"), v("pj", 0, 8))
-    copy(v("pf", 0, 8), v("pi", 0, 8))
-    PR, PI, PQ, PSB, PX, P2B, P64 = [col("pf", k) for k in range(1, 8)]
-    R2, R21, I1, SB32, PCL, PNB, Q192, ROOT, I162, NI162, NI2 = [col("pf", k) for k in range(8, 19)]
+    copy(v("pf", 0, 7), v("pi", 0, 7))
+    PR, PI, PQ, PSB, PX, P2B = [col("pf", k) for k in range(1, 7)]
+    R2, R21, Q192, ROOT, GE, GO, IDH, F31 = [col("pf", k) for k in range(8, 16)]
     ts(col("aux", 0), P2B, 4.0, A.min, 2.0, A.mult)
     ts(col("aux", 1), PQ, 12.0, A.mult, PX, A.add)
     ts(Q192, PQ, -192.0, A.mult)
     ts(col("aux", 2), PSB, 0.125, A.mult, col("aux", 0), A.add)
+    ts(col("sel", 0), col("aux", 1), col("aux", 2), A.add)
     act(R2, PR, 2.0)
     act(R21, PR, 2.0, 1.0)
-    act(SB32, PSB, 2.0)
-    ts(v("eqm"), v("dm"), PR, A.is_equal)
-    ts(col("sel", 0), col("aux", 1), col("aux", 2), A.add)
-    ts(v("gtm"), v("dm"), PR, A.is_gt)
-    act(v("eqb"), v("eqm"), BIG)
-    ts(v("tmp2", 0, 96), v("tmp", 0, 96), R2, A.is_equal, 1.0 / 16, A.mult)
-    ts(v("tmp2", 96, 192), v("tmp", 0, 96), R21, A.is_equal, 2.0 / 16, A.mult)
-    act(v("tmp3", 0, 96), v("tmp", 96, 192), 1.0, SB32)
-    for name in ("eqb", "gtm"):
-        act(v(name, 15, None, 16), v(name, 15, None, 16), 1.0 / BIG / SMALL)
-    act(v("eqc"), v("eqb", 0, 96), -2.0)
-    fill(v("tmp2", 0, 96, 32), 0.0)
-    copy(v("pr", 0, 48, 1, 32, 64), v("pr", 0, 48, 1, 0, 32))
-    copy(v("pr", 0, 48, 1, 64, 96), v("pr", 0, 48, 1, 0, 32))
-    copy(v("pr", 0, 48, 1, 96, 128), v("pr", 0, 48, 1, 0, 32))
-    tt(v("tmp3", 96, 192), v("tmp3", 0, 96), v("tmp2", 96, 192), A.add)
-    tt(v("tmp3", 192, 288), v("tmp3", 96, 192), v("tmp2", 0, 96), A.add)
+    for q in range(1, 4):
+        copy(on(v("pr"), q), on(v("pr"), 0))
     for k in range(2):
         ts(v("lp", 16 * k, 16 * k + 16), ind(v("pr", 24 * k, 24 * k + 24), col("sel", 0)), Q192, A.add)
-    ts(v("lpf"), ind(v("pr", 24, 48), col("sel", 0)), Q192, A.add)
+    LP0, LP1 = v("lp", 0, 6), v("lp", 16, 22)
     quant(v("qu"), v("su"), v("ut"))
     pick(v("qup"), ind(v("qu"), v("uoff")))
-    copy(v("sup"), ind(v("su"), v("uoff")))
-    LP0, LP1 = v("lp", 0, 6), v("lp", 16, 22)
-    act(v("p0f"), ind(v("fio"), LP0))
-    ts(v("p1c", 0, 6), v("p1c", 0, 6), SB32, A.add, -0.625, A.add)
-    quant_half("qx", "sx", "xt", 0)
-    quant_half("qx", "sx", "xt", 1)
-    tt(v("tmp4", 96, 192), ind(v("fio"), LP1), v("tmp3", 192, 288), A.subtract)
+    add("S", lambda: g.scalar.activation(real(v("sup")), real(ind(v("su"), v("uoff"))), FN.Copy), [ind(v("su"), v("uoff"))], [v("sup")], 260.0)
 
     def scores(k):
         mm(bank(k, HC), "up", 0, half("qx", k), half("sx", k))
@@ -296,66 +294,89 @@ def rank_program(g, core, T, topo):
             act(v("ssb", 0, HC, 1, 0, 64), bank(0, HC, 0, 64))
 
     for k in range(2):
+        quant_half("qx", "sx", "xt", k)
         scores(k)
-    tt(v("tmp4", 0, 96), ind(v("fio"), LP1), v("p0f"), A.subtract)
-    act(odd("cd1"), v("tmp4", 96, 192), -16.0)
-    act(even("cd1"), v("tmp4", 0, 96), 16.0)
-    tt(v("p1w", 0, 6), v("lpf", 0, 6), v("p1c", 0, 6), A.subtract)
-    tt(v("tmp2", 192, 288), v("tmp4", 0, 96), v("eqc"), A.mult)
-    act(v("p1w", 0, 6), v("p1w", 0, 6), 2.0 / SMALL)
-    tt(v("mwa"), v("tmp2", 192, 288), v("gtm", 0, 96), A.add)
-    for name in ("wc4", "wd"):
-        act(even(name), v("fio", 0, 96), -16.0, -8 * 1.45)
-    act(I1, PI, 1.0, 1.0)
-    act(I162, PI, 16.0, 2.0)
-    act(NI162, PI, -16.0, -2.0)
-    act(NI2, PI, -2.0)
-    ts(even("m2"), v("dm", 0, 96), PR, A.is_ge)
-    tt(odd("m2"), v("gtm", 0, 96), v("eqb", 0, 96), A.subtract)
-    ts(ROOT, PR, 0.0, A.is_equal)
+    dma("Y", lambda: T.qw[:].bitcast(dt.uint8), lambda: T.wc[:], [v("xt")], [v("qw")])
+    dma("Y", lambda: T.sw[:], lambda: T.ws[:], [v("xt")], [v("sw")])
+    dma("Y", lambda: T.vt[:], lambda: T.v[:], [v("xt")], [v("vt")])
+    ts(v("tmp", 0, 96), v("fi", 0, 96), R2, A.is_equal, 64.0, A.mult)
+    ts(v("tmp", 96, 192), v("fi", 0, 96), R21, A.is_equal, 128.0, A.mult)
+    fill(v("tmp", 0, 96, 32), 0.0)
+    tt(v("fb", 0, 96), v("tmp", 0, 96), v("tmp", 96, 192), A.add)
+    act(v("fb", 96, 192), v("fb", 0, 96))
+    ts(ROOT, PR, 0.0, A.is_equal, 64.0, A.mult)
+    act(v("sr"), v("fb", 0, 96), 1.0, ROOT)
+    act(v("tmp2", 0, 96), ind(v("flo"), LP1))
+    act(odd("d1p"), v("tmp2", 0, 96))
+    act(odd("d1b"), ind(v("fb"), LP1))
+    tt(even("d1p"), ind(v("flo"), LP0), v("tmp2", 0, 96), A.subtract)
+    tt(even("d1b"), ind(v("fb"), LP0), odd("d1b"), A.subtract)
+    ts(v("gtm"), v("dm", 0, 96), PR, A.is_gt)
+    ts(v("tmp3", 0, K), v("dm"), PR, A.is_equal, BIG, A.mult)
+    scan(v("mw"), v("m16", 0, K), v("tmp3", 0, K), A.min, A.max)
+    act(v("mw", 15, None, 16), v("mw", 15, None, 16), 1.0 / BIG / SMALL)
+    act(v("tmp3", 192, 288), v("tmp3", 0, 96), 1.0 / TINY)
+    scan(odd("mo"), v("m16", 0, 96), v("tmp3", 192, 288), A.min, A.max)
+    act(ends("mo"), ends("mo"), 1.0 / BIG / SMALL)
+    act(v("tmp3", 288, 384), v("tmp3", 0, 96), 2.0 * TINY / BIG)
+    tt(v("tmp2", 96, 192), even("d1p"), v("tmp3", 288, 384), A.mult)
+    tt(even("mo"), v("tmp2", 96, 192), v("gtm", 0, 96), A.add)
+    fill(col("cd0", 0), 0.0)
+    act(v("tmp2", 192, 288), v("tmp2", 0, 96), 1.0, 0.5)
+    tt(v("cd0", 2, 194, 2), v("tmp2", 192, 288), v("tmp3", 288, 384), A.mult)
+    for name in ("pb", "pc", "bb", "bc"):
+        const(even(name), 0.0)
     for b in range(4):
         quant(v("qe", 128 * b, 128 * b + 128), v("se", 128 * b, 128 * b + 128), v("eye", 3 - b, 515 - b))
-    for name in ("pd", "kd"):
-        ts(v(name), v("ones", 0, 192), 0.0, A.mult)
-    zero(v("sd"), C)
-    zero(v("cd"), C)
-    zero(v("rr"), 64)
-    zero(v("zz", 0, 64), 64)
-    ts(col("aux", 3), P64, 32.0, A.is_ge, 16.0, A.mult)
-    ts(col("aux", 4), P64, 49.0, A.is_ge, 5.0, A.mult)
-    ts(col("aux", 5), P64, 55.0, A.is_ge, 10.0, A.mult)
+    for e, r in enumerate((R2, R21)):
+        ts(v("tmp4", 96 * e, 96 * e + 96), v("fi", 0, 96), r, A.is_equal, BIG, A.mult)
+    scan(v("me"), v("m32"), v("tmp4"), A.min, A.max)
+    act(ends("me"), ends("me"), 1.0 / BIG / SMALL)
+    for b in range(3):
+        const(v("pcc", b, 6, 3), -(32.0 + 32 * b) / 64)
+    const(v("mx0"), -4096.0)
+    const(v("mx0", 0, None, 64), 1024.0)
+    const(v("rst"), 0.0)
+    const(starts("rst"), 4096.0)
+    act(GE, R2, -SG, 31 * SG + 1.0 / 128)
+    act(GO, R21, -SG, 31 * SG + 1.0 / 128)
+    act(IDH, PI, -SG, 31 * SG - EPS / 2)
+    act(F31, PI, 1.0, -31.0)
+    act(v("idr"), v("fi"), -1.0, 31.0)
+    act(v("ids"), v("fi"), -SG, 31 * SG)
+    act(v("idb"), v("fi"), -SG, 31 * SG)
+    const(starts("dd"), 0.0)
+    fill(v("gd"), 0.0)
+    const(even("wd"), 0.0)
+    const(even("cg0"), 0.0)
+    ts(odd("cg1"), v("colc"), Q192, A.subtract, PI, A.add)
+    const(v("sd"), 1.0)
+    const(v("mcl"), 1.0)
+    const(starts("mcl"), 0.0)
     for h in range(2):
-        fill(quad("mcl", 2 * h + 1, 17, C, 32), 0.0)
-        fill(quad("mcl", 2 * h + 1, 23, C, 32), 0.0)
-    ts(col("aux", 6), P64, col("aux", 3), A.subtract, col("aux", 4), A.subtract)
-    act(col("aux", 7), col("aux", 5), 1.0 / 32, 1.0)
-    ts(v("colc"), v("colc"), Q192, A.subtract, PI, A.add)
+        for c in (17, 23):
+            const(on(v("mcl", c, None, 32), 2 * h + 1), 0.0)
+    const(v("cd"), 0.0)
+    const(v("zz"), 0.0)
     ts(v("swp"), v("pj", 8, 12), PR, A.add)
-    tt(v("mw"), v("eqb"), v("gtm"), A.add)
-    act(PCL, col("aux", 6), -1.0 / 32, col("aux", 7))
-    act(PNB, PCL, -1.0, -1.0 / 64)
     quant(v("qv"), v("sv"), v("vt"))
+    iota(v("rs", C), [[0, 1024 - C]], 0, 0)
 
-    def lv(name, l):
-        return v(name, 12 * (l // 2) + l % 2, 12 * (l // 2) + 12, 2)
+    def lv(name, l, c):
+        c0 = 2 * (12 * (l // 2) + l % 2) + c
+        return v(name, c0, c0 + 21, 4)
 
-    def lvc(name, l, s):
-        return col(name, 12 * (l // 2) + l % 2 + 2 * s)
-
-    def sm(k):
-        return v("sm", 8 * k, 8 * k + 6)
-
-    def slot(name, s):
-        return v(name, 32 * s, 32 * s + 32)
+    def across(l, c):
+        return [(lambda name, h=h, qs=qs: on(v(name, 192 * qs + c, 192 * qs + 192, 32), 2 * h + (l > 0)), 2 * qs + h) for h in range(2) for qs in range(2)]
 
     def spread(l):
-        c0, c1, off = lv("gg", l)[3], lv("gg", l)[4], (0, 0, 23, 17)[l]
-        for h in range(2):
-            for qs in range(2):
-                act(quad("sd", 2 * h + (l > 0), 192 * qs + off, 192 * qs + 192, 32), quad("fpool", 2 * qs + h, c0, c1, 2), 2.0,
-                    quad("fpool", 2 * qs + h, NI2[3], NI2[4]))
+        c, top = ((0, 32), (0, 16), (23, 8))[l]
+        for to, q in across(l, c):
+            act(to("sd"), on(odd("ws%d" % l), q), 1024.0, -0.25 - top)
 
-    PP = starts("pd")
+    def wrap(off, row, k):
+        scan(v("cv", 96 * k, 96 * k + 96), row, v("mw", 0, 96), A.add, A.mult)
+        ts(v(off), v("cv", 96 * k + 15, 96 * k + 96, 16), SMALL, A.mult, 0.25, A.add)
 
     for t, mask in enumerate(ROUNDS):
         peer = T.cores[rank ^ mask]
@@ -363,149 +384,163 @@ def rank_program(g, core, T, topo):
         qt, st, ql, sl, lo, li = ["%s%d" % (n, t) for n in ("qt", "st", "ql", "sl", "lo", "li")]
         for b in range(4):
             mm(bank(4 + b), "e", b, v("qx"), v("sx"))
-            act(v("tt", b, None, 4), bank(4 + b), 1.0 / 32)
+            for k in range(2):
+                act(v("tt", 4 * HC * k + b, 4 * HC * (k + 1), 4), ("ps", 0, 128, 512 * (4 + b) + HC * k, 512 * (4 + b) + HC * (k + 1), 1), 1.0 / 32)
         for k in range(3):
             quant(v(qt, 128 * k, 128 * k + 128), v(st, 128 * k, 128 * k + 128), v("tt", 512 * k, 512 * k + 512))
         send(v(ql), v(qt), peer, "big%d" % t, dt.uint8)
         tile_sent = send(v(sl), v(st), peer, "big%d" % t)
         for b in range(4):
-            act(v("win", WIN * b, WIN * b + C), bank(4 + b), 1.0 / 16)
+            for k in range(2):
+                act(v("win", WIN * b + K + HC * k, WIN * b + K + HC * (k + 1)), ("ps", 0, 128, 512 * (4 + b) + HC * k, 512 * (4 + b) + HC * (k + 1), 1), 1.0 / 16)
         act(v("sb1"), ind(v("ssb"), LP1))
-        tt(odd("cd0"), ind(v("ssb"), LP0), v("sb1"), A.is_ge)
-        scan(v("sca", 0, 96), odd("cd0"), v("mwa"), A.add, A.mult)
-        scan(v("w0"), v("cd0"), v("cd1"), A.mult, A.add)
-        act(v("wf"), odd("w0"))
-        tt(v("o1f", 0, 6), v("sca", 15, 96, 16), v("p1w", 0, 6), A.add)
-        ts(v("o1", 0, 6), v("o1f", 0, 6), SMALL, A.mult)
-        turn(v("wft"), v("wf"))
-        act(v("u1", 0, 6), v("wft", 0, None, 16), -1.0 / 16, MAGIC)
-        ts(v("up1", 0, 6), v("u1", 0, 6), MAGIC, A.subtract, I1, A.add)
-        for src, base, off, last, nxt in (("w0", "wf", "o1", "wc4", "o4"), ("wc4", "wg", "o4", "wd", "o16")):
-            for dst in ("wa", "wb", last):
-                tt(odd(dst), ind(v(src), v(off, 0, 6)), v(base), A.add)
-                src = dst
-            if last == "wd":
-                act(v("x3"), odd("wd"), 1.0, ROOT)
-            else:
-                act(v("wg"), odd("wc4"))
-            scan(v("sca"), v(last), v("m2"), A.add, A.mult)
-            ts(v(nxt, 0, 6), v("sca", 31, None, 32), SMALL / 8, A.mult)
-        tt(v("bits"), ind(v("wd"), v("o16", 0, 6)), v("x3"), A.add)
-        turn(v("bitt"), v("bits"))
-        act(v("b2"), v("bitt"), 1.0, NI162, FN.Abs)
-        ts(odd("at"), v("bitt"), I162, A.is_ge)
-        ts(even("at"), v("b2"), 1.0, A.is_equal)
-        turn(v("am"), v("at"))
-        for s in range(6):
-            act(slot("ua", s), slot("am", s), col("up1", s), -1.0)
-        scan(v("ws0"), v("m32"), v("am"), A.mult, A.add)
-        W0 = ends("ws0")
-        ts(starts("hd"), W0, 16.0, A.is_ge, PI, A.mult)
-        scan(v("h1"), v("m32"), v("hd"), A.mult, A.add)
-        turn(v("h2"), v("h1"))
-        scan(v("h3"), v("m32"), v("h2"), A.mult, A.max)
-        ts(lv("gg", 0), W0, 1.0 / 64, A.mult, PI, A.add)
-        ts(sm(0), W0, 16.0, A.is_ge)
-        act(lv("w2", 0), W0, 1.0 / 32)
-        tt(starts("kd"), sm(0), lv("gg", 0), A.mult)
-        ts(PP, W0, 0.0, A.mult, 0.5, A.add)
-        scan(v("y1"), v("m32"), v("kd"), A.mult, A.add)
-        act(lv("call", 0), ends("h3"))
-        spread(0)
+        tt(v("cd0", 1, 193, 2), ind(v("ssb"), LP0), v("sb1"), A.is_ge)
+        scan(v("sca"), v("cd0", 1, 193), v("mo"), A.add, A.mult)
+        ts(v("o1"), ends("sca"), SMALL, A.mult, 0.25, A.add)
+        scan(v("pa"), v("cd0", 0, 192), v("d1p"), A.mult, A.add)
+        scan(v("ba"), v("cd0", 0, 192), v("d1b"), A.mult, A.add)
+        act(v("b1"), odd("ba"))
+        act(odd("pb"), ind(v("pa"), v("o1")))
+        act(odd("pc"), ind(v("pb"), v("o1")))
+        act(v("p4"), ind(v("pc"), v("o1")))
+        wrap("o3", odd("pc"), 0)
+        act(v("p7"), ind(v("p4"), v("o3")))
+        act(v("p10"), ind(v("p7"), v("o3")))
+        wrap("o7", v("p7"), 1)
+        wrap("o10", v("p10"), 2)
+        for o, w, off, base in ((odd("bb"), "ba", "o1", v("b1")), (odd("bc"), "bb", "o1", odd("ba")), (v("b4"), "bc", "o1", odd("ba")),
+                                (v("b7"), "b4", "o3", odd("bc")), (v("b10"), "b7", "o3", odd("bc")), (v("b13"), "b10", "o3", odd("bc")),
+                                (v("b20"), "b13", "o7", v("b7"))):
+            tt(o, ind(v(w), v(off)), base, A.add)
+        tt(v("bx"), v("b10"), v("sr"), A.add)
+        tt(odd("vv"), ind(v("b20"), v("o10")), v("bx"), A.add)
+        for e in range(2):
+            scan(v("pk", 96 * e, 96 * e + 96), odd("pa"), v("me", 96 * e, 96 * e + 96), A.add, A.mult)
+        act(v("pc1"), ends("pk"), SMALL / 64)
+        tt(v("pc2"), v("pc1"), v("pcc"), A.add)
+        ts(even("vv"), odd("vv"), 96.0, A.is_ge, -128.0, A.mult)
+        ts(v("bm", 96), odd("vv"), 96.0, A.is_ge, 64.0, A.mult)
+        scan(v("se2"), v("mx0"), v("vv"), A.max, A.subtract)
+        scan(v("so"), even("mx0"), v("bm", 96), A.max, A.subtract)
+        tt(v("bm", 0, 96), odd("vv"), even("vv"), A.add)
+        for e, (src, gc) in enumerate(((odd("se2"), GE), (v("so"), GO))):
+            part = v("yb", 96 * e, 96 * e + 96)
+            scan(back(part), v("rst", 0, 96), back(src), A.add, A.min)
+            turn(v("yrow", e, None, 2), part)
+            ts(v("gq", 96 * e, 96 * e + 96), part, -1.0 / 131072, A.mult, gc, A.add)
+            turn(v("gr0", e, None, 2), v("gq", 96 * e, 96 * e + 96))
+            for b in range(3):
+                act(slot("ub", 3 * e + b), slot("bm", 3 * e + b), col("pc2", 3 * e + b), 1.0)
+            turn(v("utn", e, None, 2), v("ub", 96 * e, 96 * e + 96))
+        turn(v("ybs"), v("yrow"))
+        act(odd("ws0"), starts("ybs"), -1.0 / 65536, 1.0 / 64 + EPS)
+        ts(odd("wd"), starts("ybs"), 0.0, A.is_le, 2.0, A.mult)
         for l in range(4):
+            ws, gr = "ws%d" % l, "gr%d" % (l % 2)
             if l:
-                scan(v("bs"), v("m32"), v("pd"), A.mult, A.add)
-                tt(sm(2), lv("w2", l), v("top", 0, 6), A.add)
-                turn(v("pfree"), v("bs"))
-                tt(sm(3), sm(2), PP, A.min)
-                if l < 3:
-                    tt(sm(0), sm(2), PP, A.is_ge)
+                scan(back(v("pbc")), v("rst"), back(v("sa")), A.add, A.min)
+                turn(v("prow"), v("pbc"))
+                tt(v("xx"), ends("sb"), odd(ws), A.add)
+                copy(v("pp"), ends("sa"))
                 for s in range(6):
-                    ts(slot("y1", s), slot("pfree", s), col("sm", 24 + s), A.is_equal, lvc("gg", l, s), A.mult)
-            for c in (0, 96):
-                turn(v("y1t", c, c + 96), v("y1", c, c + 96))
-                scan(v("ks", c, c + 96), v("m32", c, c + 96), v("y1t", c, c + 96), A.mult, A.max)
-                if l:
-                    c0 = 12 * (l // 2) + l % 2 + c // 16
-                    ts(v("call", c0, c0 + 5, 2), v("ks", c + 31, c + 96, 32), MAGIC, A.add, MAGIC, A.subtract)
+                    ts(slot("y1", s), slot("prow", s), col("xx", s), A.min, col("pp", s), A.not_equal)
+                turn(v("yt"), v("y1"))
+                if l < 3:
+                    tt(v("cand"), v("xx"), v("pp"), A.is_gt)
+                    act(odd("wd"), v("cand"), 2.0)
+                    tt(v("nn"), v("pp"), ends("sb"), A.subtract)
+                    act(v("n62"), v("nn"), 1.0, 62 * SG)
+            hit, op = (v("yt"), A.mult) if l else (v("yrow"), A.min)
+            scan(v("cs"), hit, v("idr"), op, A.max)
+            act(lv("cg1", l, 0), ends("cs"), 1.0, F31)
+            act(lv("cg0", l, 1), odd(ws), -1.0, EPS, FN.Sign)
             if l == 3:
                 break
+            spread(l)
+            scan(v("ks"), hit, v(gr), op, A.max)
+            scan(v("cz"), hit, v("ids"), op, A.max)
+            if l == 2:
+                for to, q in across(3, 18):
+                    act(to("sd"), on(odd(ws), q), 1024.0, -4.25)
+                    act(to("mcl"), on(v("cand"), q), 2048.0)
+                for to, q in across(3, 17):
+                    tt(to("sd"), on(ends("cz"), q), on(ends("ks"), q), A.subtract)
             for s in range(6):
-                ts(slot("y2", s), slot("ua", s), lvc("call", l, s) if l else col("h3", 32 * s + 31), A.is_equal, lvc("gg", l, s), A.mult)
-            tt(sm(4), ends("ks"), lv("call", l) if l else ends("h3"), A.subtract)
-            turn(v("y2t"), v("y2"))
-            tt(sm(5), sm(4), sm(0), A.mult)
-            tt(sm(6), PP, sm(4), A.subtract)
-            scan(v("rs2"), v("m32"), v("y2t"), A.mult, A.max)
-            tt(lv("gg", l + 1), lv("gg", l), sm(5), A.subtract)
-            tt(v("top", 0, 6), ends("rs2"), sm(6), A.max)
-            tt(PP, ends("rs2"), sm(6), A.max)
-            act(lv("w2", l + 1), lv("gg", l + 1), 2.0, NI2)
-            spread(l + 1)
-        act(v("cg", 0, 24), v("w2"), func=FN.Sign)
-        act(v("cg", 24, 48), v("cg", 0, 24), PI)
-        tt(v("cg", 48, 72), v("colc"), v("cg", 24, 48), A.subtract)
-        tt(v("cg", 96, 120), v("cg", 0, 24), v("call"), A.mult)
-        tt(v("cg", 72, 96), v("cg", 96, 120), v("cg", 48, 72), A.add)
-        for h in range(2):
-            for qq in range(2):
+                if s < 3:
+                    ts(slot("dd", s, 1), slot("utn", s, 1), col("cs", 32 * s + 31), A.add, 0.0, A.not_equal)
+                else:
+                    act(slot("dd", s, 1), slot("utn", s, 1), 1.0, col("cs", 32 * s + 31), FN.Abs)
+            if l:
+                tt(starts(gr), v("n62"), ends("ks"), A.subtract)
+            else:
+                ts(starts(gr), ends("ks"), -1.0, A.mult, 63 * SG, A.add)
+            act(starts("idb"), ends("cs"), -SG, 62 * SG)
+            tt(even(ws), ends("cz"), ends("ks"), A.subtract)
+            scan(v("sa"), v("dd"), v(gr), A.min, A.max)
+            scan(v("sb"), v("dd"), v("idb"), A.min, A.max)
+            scan(v("ws%d" % (l + 1)), v("wd"), v(ws), A.mult, A.add)
+            if l < 2:
+                ts(starts("gd"), odd("ws%d" % (l + 1)), 0.5, A.mult, IDH, A.add)
+                scan(v("gb"), v("m32"), v("gd"), A.mult, A.add)
+                turn(v("gr%d" % (1 - l % 2)), v("gb"))
+        for a in range(2):
+            scan(v("cg2", 24 * a, 24 * a + 24), v("cg0", 24 * a, 24 * a + 24), v("cg1", 24 * a, 24 * a + 24), A.mult, A.add)
+            for h in range(2):
                 for qs in range(2):
-                    (copy if qs else act)(quad("cd", 2 * h + qq, 192 * qs, 192 * qs + 192, 16), quad("cg", 2 * qs + h, 72 + 12 * qq, 84 + 12 * qq))
+                    (copy if qs and a else act)(on(v("cd", 192 * qs, 192 * qs + 192, 16), 2 * h + a), on(v("cg2", 24 * a + 1, 24 * a + 24, 2), 2 * qs + h))
         scan(v("cbs"), v("m16"), v("cd"), A.mult, A.add)
         turn(v("cf"), v("cbs"))
         scan(v("sbs"), v("mcl"), v("sd"), A.mult, A.add)
         turn(v("sf"), v("sbs"))
-        act(v("sgn"), v("sf"), 1.0, PNB, FN.Sign, col("cnt", 0))
-        act(col("cnt", 1), col("cnt", 0), 0.5, BASE + C / 2)
-        ts(v("eq1"), v("sf"), PCL, A.is_equal, 1.0, A.add)
-        turn(v("eqt"), v("eq1"))
-        scan(v("p2"), v("eq1"), v("ones"), A.add, A.subtract, col("cnt", 1))
+        ts(v("eqt"), v("sbs"), 0.0, A.is_equal, 1024.0, A.mult)
+        act(v("sgn"), v("sf"), 1.0, -0.5, FN.Sign, col("cnt", 0))
+        ts(v("eq2"), v("sf"), 0.0, A.is_equal, 2.0, A.mult)
+        scan(v("p2"), v("eq2"), v("ones"), A.add, A.mult, col("cnt", 0))
         turn(v("p2t"), v("p2"))
-        scan(v("rs"), v("eqt"), v("p2t"), A.mult, A.min, BASE)
-        copy(v("rr", 0, 12), v("rs", 31, C, 32))
+        scan(v("rs", 0, C), v("eqt"), v("p2t"), A.add, A.min)
+        turn(v("t1", 0, 32), ends("rs"))
         for h in range(2):
-            act(quad("rr", 2 * h, 32, 44), quad("rs", 2 * h + 1, 16, C, 32))
-            copy(quad("rr", 2 * h + 1, 32, 44), quad("rs", 2 * h + 1, 21, C, 32))
-        turn(v("t1"), v("rr"))
+            turn(on(v("t1", 32, 64), 2 * h + 1), on(v("rs", 22, None, 32), 2 * h + 1))
+            turn(on(v("t1", 32, 64), 2 * h), on(v("rs", 16, None, 32), 2 * h + 1))
         copy(v("t2"), ind(v("t1"), v("swp")))
         turn(v("t3"), v("t2"))
-        for hi in range(2):
-            ts(v("opl", hi, None, 2), v("t3", 32 * hi, 32 * hi + 12), -BASE - 0.75, A.add)
+        for u in range(2):
+            ts(v("opl", u, None, 2), v("t3", 32 * u, 32 * u + 12), 0.5, A.mult, 191.25, A.add)
         for b in range(4):
             mm(bank(b), "e", b, v(ql), v(sl), waits=[("big%d" % t, 2 * ne)], behind=[(tile_sent, TILE)])
-            act(v("gall", C * b, C * b + C), bank(b), 1.0 / 32)
+            for k in range(2):
+                act(v("gall", C * b + HC * k, C * b + HC * (k + 1)), ("ps", 0, 128, 512 * b + HC * k, 512 * b + HC * (k + 1), 1), 1.0 / 32)
         for k in (1, 0):
             for b in range(4):
                 mm(bank(4 * k + b, HC), "e", b, half("qx", k), half("sx", k), True, False)
-        copy(ind(v("cs"), v("opl")), v("cf"))
-        scan(v("csw"), v("cs", 0, K), v("mw"), A.add, A.mult)
+        copy(ind(v("cw"), v("opl")), v("cf"))
+        scan(v("csw"), v("cw", 0, K), v("mw"), A.add, A.mult)
         ts(v(lo), v("csw", 15, None, 16), SMALL, A.mult, HC + 0.25, A.add)
         list_sent = send(v(li), v(lo), peer, "lst%d" % t)
         for b in range(4):
-            act(v("ee", K * b, K * b + K), ind(v("win", WIN * b, WIN * b + C), v(lo)), 0.5)
+            act(v("ee", K * b, K * b + K), ind(v("win", WIN * b + K, WIN * b + WIN), v(lo)), 0.5)
         for a in range(2):
             act(v("zz", 32 * a, 32 * a + 12), v("cd", 16 * a, None, 32))
-        act(v("zz", 128, 192), v("rr"), 1.0, C - HC - BASE - 1.0)
-        ts(v("zz", 64, 128), v("rr"), BASE + K + 0.5, A.is_lt)
-        tt(v("zz", 192, 256), v("zz", 128, 192), v("zz", 0, 64), A.subtract)
-        tt(v("zz", 256, 320), v("zz", 192, 256), v("zz", 64, 128), A.mult)
-        tt(v("zz", 320, 384), v("zz", 256, 320), v("zz", 0, 64), A.add)
-        turn(v("z1"), v("zz", 320, 384))
-        copy(v("z2"), ind(v("z1"), v("swp")))
+        turn(v("z1"), v("zz"))
+        act(v("z2"), ind(v("z1"), v("swp")))
         turn(v("z3"), v("z2"))
-        for hi in range(2):
-            ts(v("ozl", hi, None, 2), v("z3", 32 * hi, 32 * hi + 12), HC + 0.25, A.add)
+        act(v("kk"), v("t3", 0, 44), 0.5, 191.0 - K - HC)
+        act(v("ky"), v("t3", 0, 44), 800.0, 1600.0 * (191.5 - K) - K - HC)
+        tt(v("km"), v("kk"), v("ky"), A.max)
+        tt(v("kn"), v("km"), v("z3", 0, 44), A.min)
+        for u in range(2):
+            ts(v("ozl", u, None, 2), v("kn", 32 * u, 32 * u + 12), K + HC + 0.25, A.add)
         if t == 2:
             act(v("clo"), v("cf"), 1.0, float(HC))
             dma("Y", lambda: T.cl[:], lambda: T.clo[0:128:16, :], [v("clo")], [])
         for b in range(4):
-            tt(v("win", WIN * b + C, WIN * b + WIN), ind(v("gall", C * b, C * b + C), v(li)), v("ee", K * b, K * b + K), A.add,
+            tt(v("win", WIN * b, WIN * b + K), ind(v("gall", C * b, C * b + C), v(li)), v("ee", K * b, K * b + K), A.add,
                waits=[("lst%d" % t, ne)], behind=[(list_sent, LIST)])
         for k in range(2):
             for b in range(4):
                 o = v("zt", 4 * HC * k + b, 4 * HC * (k + 1), 4)
                 i = ind(v("win", WIN * b, WIN * b + WIN), v("ozl", 12 * k, 12 * k + 12))
-                if b == 3:
+                if b == 3 or (b == 2 and k):
                     ts(o, i, 0.5, A.mult)
                 else:
                     act(o, i, 0.5)
@@ -515,7 +550,7 @@ def rank_program(g, core, T, topo):
         for k in range(2):
             for b in range(4):
                 o = v("xn", 4 * HC * k + b, 4 * HC * (k + 1), 4)
-                if (b % 2 if k else b < 2):
+                if b % 2 if k else b == 3:
                     ts(o, bank(4 * k + b, HC), 1.0 / 32, A.mult)
                 else:
                     act(o, bank(4 * k + b, HC), 1.0 / 32)
@@ -547,9 +582,6 @@ def rank_program(g, core, T, topo):
                 for a in mine:
                     used.setdefault(a[0], []).append((n, a, writes))
 
-    for n in range(4):
-        lands[n] = LOAD
-
     def gap(m, n):
         if ops[m][5] == "d":
             return lands[m]
@@ -579,10 +611,12 @@ def rank_program(g, core, T, topo):
         for q, c in ready.items():
             if not c:
                 continue
-            first = max(c, key=lambda n: (tail[n], -n))
-            s = max(free[q], at[first])
-            fit = [n for n in c if max(free[q], at[n]) + ops[n][6] <= s + 40.0]
-            n = max(fit, key=lambda n: (tail[n], -n)) if fit and s > free[q] else first
+            n = max(c, key=lambda n: (tail[n], -n))
+            while at[n] > free[q]:
+                fit = [k for k in c if k != n and max(free[q], at[k]) + ops[k][6] <= at[n] + 40.0 and at[k] < at[n]]
+                if not fit:
+                    break
+                n = max(fit, key=lambda n: (tail[n], -n))
             s = max(free[q], at[n])
             if best is None or s < best[0]:
                 best = (s, n)
@@ -594,7 +628,7 @@ def rank_program(g, core, T, topo):
         for k in later[n]:
             left[k] -= 1
             if not left[k]:
-                at[k] = max(end[m] + d for m, d in edges[k])
+                at[k] = max(end[m] + (min(d, 6000.0) if d == TILE else d) for m, d in edges[k])
                 ready[ops[k][0]].append(k)
 
     place = {n: k for k, n in enumerate(order)}

@@ -6,26 +6,26 @@ F32, BF, HF, I32, U16, MX, U8 = "float32", "bfloat16", "float16", "int32", "uint
 BIG = 2.0 ** 20
 SMALL = 2.0 ** 18
 TINY = 2.0 ** -60
-WIN = C + K
+WIN = K + C + 16
 SG = 1.0 / 64
 EPS = SG / 64
-WAKE, LOAD, LIST, TILE = 170.0, 2200.0, 2300.0, 12000.0
+WAKE, LOAD, LIST, TILE = 170.0, 2200.0, 1500.0, 6000.0
 
 _SB = {
     "xt": (4 * C, BF), "xn": (4 * C, BF), "ut": (512, BF), "vt": (512, BF), "eye": (528, BF),
     "qx": (C, MX), "sx": (C, U8), "qu": (128, MX), "su": (128, U8), "qup": (128, MX), "sup": (128, U8),
     "qv": (128, MX), "sv": (128, U8), "qw": (512, MX), "sw": (512, U8), "qe": (512, MX), "se": (512, U8),
     "qz": (C, MX), "sz": (C, U8), "tt": (4 * C, BF), "zt": (4 * C, BF),
-    "win": (4 * WIN, F32), "gall": (4 * C, F32), "ee": (4 * K, F32), "yo": (C, F32), "clo": (C, F32),
+    "win": (4 * WIN, F32), "gall": (4 * C, F32), "ee": (4 * K, F32), "fm": (2 * C, F32), "yo": (C, F32), "clo": (C, F32),
     "pr": (48, I32), "pi": (8, I32), "pj": (16, I32),
     "ones": (C, BF), "m32": (192, BF), "m16": (C, BF), "mcl": (C, BF), "mx0": (192, BF), "rst": (192, BF),
-    "fi": (192, BF), "flo": (192, BF), "fb": (192, BF), "dm": (K, BF), "gtm": (96, BF),
-    "mw": (K, BF), "mo": (192, BF), "me": (192, BF), "tmp": (192, BF), "tmp2": (288, BF), "tmp3": (384, BF), "tmp4": (192, BF),
-    "cd0": (208, BF), "d1p": (192, BF), "d1b": (192, BF), "sr": (96, BF),
+    "fi": (192, BF), "flo": (192, BF), "fb": (192, BF), "dm": (K, BF),
+    "mw": (K, BF), "mo": (192, BF), "me": (192, BF), "tmp2": (288, BF), "tmp3": (384, BF), "tmp4": (192, BF),
+    "cd0": (208, BF), "d1p": (192, BF), "d1b": (192, BF), "pd": (192, BF), "m01": (192, BF), "b0": (192, BF), "df": (192, BF), "eqa": (C, BF),
     "ssb": (192, F32), "sb1": (96, F32), "sca": (192, BF),
-    "pa": (192, BF), "pb": (192, BF), "pc": (192, BF), "cv": (288, BF), "ba": (192, BF), "bb": (192, BF), "bc": (192, BF),
-    "vv": (192, BF), "bm": (192, BF), "se2": (192, BF), "so": (96, BF), "yb": (192, BF), "yrow": (192, BF), "ybs": (192, BF),
-    "pk": (192, BF), "ub": (192, BF), "utn": (192, BF), "gq": (192, HF),
+    "pa": (192, BF), "pb": (192, BF), "pc": (192, BF), "cv": (384, BF), "ba": (192, BF), "bb": (192, BF), "bc": (192, BF),
+    "vv": (192, BF), "se2": (192, BF), "yb": (192, BF), "yrow": (192, BF), "ybs": (192, BF),
+    "pk": (192, BF), "ub": (192, BF), "utn": (192, BF), "gq": (192, HF), "gs": (288, HF),
     "idr": (192, BF), "ids": (192, BF), "idb": (192, BF), "gr0": (192, HF), "gr1": (192, HF), "gd": (192, HF), "gb": (192, HF),
     "cs": (192, BF), "cz": (192, BF), "ks": (192, HF), "dd": (192, BF), "sa": (192, HF), "sb": (192, BF), "pbc": (192, HF), "prow": (192, HF),
     "y1": (192, BF), "yt": (192, BF),
@@ -42,10 +42,11 @@ for _t in range(3):
 _PART = {}
 for _pool, _d, _names in (
         ("fpool", F32, {"pf": 24, "aux": 8, "pcc": 6, "pc1": 6, "pc2": 6, "ws0": 12, "ws1": 12, "ws2": 12, "ws3": 12, "wd": 12, "xx": 6, "pp": 6,
-                        "cand": 6, "nn": 6, "n62": 6, "cg0": 48, "cg1": 48, "cg2": 48, "colc": 24, "cnt": 1, "kk": 44, "ky": 44, "km": 44, "kn": 44}),
-        ("bpool", BF, {"t1": 64, "t2": 64, "t3": 64, "zz": 64, "z1": 64, "z2": 64, "z3": 64,
-                       "b1": 96, "p4": 96, "p7": 96, "p10": 96, "b4": 96, "b7": 96, "b10": 96, "b13": 96, "b20": 96, "bx": 96}),
-        ("upool", U16, {"uoff": 8, "sel": 2, "lp": 32, "o1": 6, "o3": 6, "o7": 6, "o10": 6, "swp": 4, "opl": 24, "ozl": 24})):
+                        "cb6": 6, "keep": 6, "cand": 6, "nn": 6, "n62": 6, "cg0": 48, "cg1": 48, "cg2": 48, "colc": 24, "cnt": 1, "kk": 32, "ky": 32, "km": 32, "kn": 32, "kl": 32,
+                        "sw0": 32, "sw1": 32}),
+        ("bpool", BF, {"t1": 64, "t2": 96, "zz": 64, "z1": 64, "z2": 96,
+                       "p3": 96, "b4": 96, "b6": 96, "b9": 96, "p5": 96, "p8": 96, "p11": 96, "b5": 96, "b8": 96, "b11": 96, "b14": 96, "b22": 96, "mx1": 96, "vg": 288, "mxg": 288, "gtm": 96, "tmp": 192, "fc": 96, "tmp5": 96, "b1": 96, "so": 96, "fmi": 32}),
+        ("upool", U16, {"uoff": 8, "sel": 2, "lp": 32, "o1": 6, "o2": 6, "o3": 6, "o8": 6, "o11": 6, "swp": 2, "opl": 32, "ozl": 24, "ofl": 24})):
     _at = 0
     for _k, _n in _names.items():
         _PART[_k] = (_pool, _at, _n)
@@ -56,6 +57,9 @@ SCRATCH["ps"] = ("psum", [128, 4096], F32)
 NDMA = 24
 SEMAPHORES = ["cV", "cS", "cP", "cG", "sent"] + ["d%d" % k for k in range(NDMA)] + ["big%d" % t for t in range(3)] + ["lst%d" % t for t in range(3)]
 
+OPT = {"dd": (3, 3, 0), "cz": 0, "c3": 10, "eqt": 1, "t2": 0, "cut": 192, "late": (2, 3), "ee": (1,), "z": (), "order": ((0, 0), (0, 1), (0, 2), (0, 3), (1, 2), (0, 4), (1, 0), (1, 1), (1, 3), (1, 4)), "x": (3, 7), "passes": 2, "tile": 1.6, "anc": 1, "gg": 0, "tries": 100, "many": 12, "amp": 300,
+       "cy": 0.87, "sfix": 0, "wake": 210.0, "n": 2, "back": 0.7}
+_ORDER = []
 A = AluOpType
 FN = ActivationFunctionType
 
@@ -103,20 +107,22 @@ def _meet(a, b):
     return bool(_cols(a) & _cols(b))
 
 
-def _ns(o, ins, rate=None):
+def _ns(o, ins, rate=None, more=0.0):
     if o[0] == "@":
-        return 50 + 3.5 * _len(o)
+        return 50 + 3.5 * OPT["cy"] * _len(o)
     if ins[0][0] == "@":
-        return 55 + 1.5 * _len(o)
+        return 55 + 1.5 * OPT["cy"] * _len(o)
     if rate is None:
         rate = 0.5 if all(a[0] != "ps" and _SB[a[0]][1] in (BF, HF) for a in [o] + ins) else 1.0
-    return max(64, rate * _len(o))
+    return max(64, rate * _len(o)) * OPT["cy"] + more
 
 
 def rank_program(g, core, T, topo):
     rank = T.rank_of(core)
     if rank is None:
         return
+    CUT, LATE = (0, OPT["cut"], C), OPT["late"]
+    W3 = C // OPT["n"]
     ops = []
     lands = {}
 
@@ -175,15 +181,16 @@ def rank_program(g, core, T, topo):
         add("V", lambda: g.vector.memset(real(o), c), [], [o], _ns(o, [o]))
 
     def quant(q, s, i):
-        add("V", lambda: g.vector.quantize_mx(real(q), real(s), real(i)), [i], [q, s], 15 + 0.265 * _len(i))
+        add("V", lambda: g.vector.quantize_mx(real(q), real(s), real(i)), [i], [q, s], (15 + 0.265 * _len(i)) * OPT["cy"])
 
-    def act(o, i, scale=1.0, bias=0.0, func=None, acc=None):
+    def act(o, i, scale=1.0, bias=0.0, func=None, acc=None, waits=(), behind=()):
         f = func if func is not None else (FN.Copy if not isinstance(bias, tuple) and bias == 0.0 else FN.Identity)
         if acc is None:
-            add("S", lambda: g.scalar.activation(real(o), real(i), f, bias=arg(bias), scale=arg(scale)), [i, scale, bias], [o], _ns(o, [i], 1.0))
+            add("S", lambda: g.scalar.activation(real(o), real(i), f, bias=arg(bias), scale=arg(scale)), [i, scale, bias], [o], _ns(o, [i], 1.0, OPT["sfix"]),
+                waits, "c", behind)
         else:
             add("S", lambda: g.scalar.activation(real(o), real(i), f, bias=arg(bias), scale=arg(scale), accum_out=real(acc)), [i, scale, bias], [o, acc],
-                20 + _ns(o, [i], 1.0))
+                20 + _ns(o, [i], 1.0, OPT["sfix"]))
 
     def const(o, c):
         act(o, (("ones",) + o[1:3] + (0, _len(o), 1)), c)
@@ -217,11 +224,14 @@ def rank_program(g, core, T, topo):
     def bank(b, n=C, p0=0, p1=128):
         return ("ps", p0, p1, 512 * b, 512 * b + n, 1)
 
+    def third(b, k):
+        return ("ps", 0, 128, 512 * b + W3 * k, 512 * b + W3 * k + W3, 1)
+
     def half(name, k):
-        return v(name, HC * k, HC * k + HC)
+        return v(name, CUT[k], CUT[k + 1])
 
     def quant_half(q, s, i, k):
-        quant(half(q, k), half(s, k), v(i, 4 * HC * k, 4 * HC * (k + 1)))
+        quant(half(q, k), half(s, k), v(i, 4 * CUT[k], 4 * CUT[k + 1]))
 
     def odd(name):
         return v(name, 1, None, 2)
@@ -243,7 +253,7 @@ def rank_program(g, core, T, topo):
         dma("Y", lambda k=k: T.pr[16 * k:16 * k + 16, 0:24], lambda: T.p0[:], [], [v("pr", 0, 24, 1, 16 * k, 16 * k + 16)])
         dma("S", lambda k=k: T.pr[16 * k:16 * k + 16, 24:48], lambda: T.p1[:], [], [v("pr", 24, 48, 1, 16 * k, 16 * k + 16)])
     for k in range(2):
-        dma("Y", lambda k=k: T.xt[:, 4 * HC * k:4 * HC * (k + 1)], lambda k=k: T.x[:, 4 * HC * k:4 * HC * (k + 1)], [], [v("xt", 4 * HC * k, 4 * HC * (k + 1))],
+        dma("Y", lambda k=k: T.xt[:, 4 * CUT[k]:4 * CUT[k + 1]], lambda k=k: T.x[:, 4 * CUT[k]:4 * CUT[k + 1]], [], [v("xt", 4 * CUT[k], 4 * CUT[k + 1])],
             LOAD + 900)
 
     fill(v("ones"), 1.0)
@@ -252,7 +262,6 @@ def rank_program(g, core, T, topo):
     iota(col("pi", 0), [[0, 1]], 0, 1)
     iota(v("pj", 0, 8), [[0, 2], [64, 2], [0, 2]], 0, 0)
     select(v("eye"), v("eye"), [[-1, 528]], A.is_equal, 3, 4)
-    iota(v("pj", 8, 12), [[16, 2], [32, 2]], 0, 0)
     iota(v("colc"), [[0, 2], [32, 6], [0, 2]], -HC, 0)
     for name, n, w in (("m32", 32, 192), ("m16", 16, K)):
         fill(v(name, 0, w), 1.0)
@@ -269,7 +278,7 @@ def rank_program(g, core, T, topo):
     copy(v("uoff"), v("pj", 0, 8))
     copy(v("pf", 0, 7), v("pi", 0, 7))
     PR, PI, PQ, PSB, PX, P2B = [col("pf", k) for k in range(1, 7)]
-    R2, R21, Q192, ROOT, GE, GO, IDH, F31 = [col("pf", k) for k in range(8, 16)]
+    R2, R21, Q192, ROOT, GE, GO, IDH, F31, F192 = [col("pf", k) for k in range(8, 17)]
     ts(col("aux", 0), P2B, 4.0, A.min, 2.0, A.mult)
     ts(col("aux", 1), PQ, 12.0, A.mult, PX, A.add)
     ts(Q192, PQ, -192.0, A.mult)
@@ -287,11 +296,12 @@ def rank_program(g, core, T, topo):
     add("S", lambda: g.scalar.activation(real(v("sup")), real(ind(v("su"), v("uoff"))), FN.Copy), [ind(v("su"), v("uoff"))], [v("sup")], 260.0)
 
     def scores(k):
-        mm(bank(k, HC), "up", 0, half("qx", k), half("sx", k))
-        if k:
-            copy(v("ssb", 0, HC, 1, 64, 128), bank(1, HC, 64, 128))
-        else:
-            act(v("ssb", 0, HC, 1, 0, 64), bank(0, HC, 0, 64))
+        mm(bank(k, CUT[k + 1] - CUT[k]), "up", 0, half("qx", k), half("sx", k))
+        for qs in range(2):
+            c0, c1 = max(CUT[k], HC * qs), min(CUT[k + 1], HC * qs + HC)
+            if c0 < c1:
+                (copy if k else act)(v("ssb", c0 - HC * qs, c1 - HC * qs, 1, 64 * qs, 64 * qs + 64),
+                                     ("ps", 64 * qs, 64 * qs + 64, 512 * k + c0 - CUT[k], 512 * k + c1 - CUT[k], 1))
 
     for k in range(2):
         quant_half("qx", "sx", "xt", k)
@@ -304,13 +314,14 @@ def rank_program(g, core, T, topo):
     fill(v("tmp", 0, 96, 32), 0.0)
     tt(v("fb", 0, 96), v("tmp", 0, 96), v("tmp", 96, 192), A.add)
     act(v("fb", 96, 192), v("fb", 0, 96))
-    ts(ROOT, PR, 0.0, A.is_equal, 64.0, A.mult)
-    act(v("sr"), v("fb", 0, 96), 1.0, ROOT)
+    ts(ROOT, PR, 0.0, A.is_equal, -2048.0, A.mult)
     act(v("tmp2", 0, 96), ind(v("flo"), LP1))
     act(odd("d1p"), v("tmp2", 0, 96))
-    act(odd("d1b"), ind(v("fb"), LP1))
+    act(v("tmp5"), ind(v("fb"), LP1))
     tt(even("d1p"), ind(v("flo"), LP0), v("tmp2", 0, 96), A.subtract)
-    tt(even("d1b"), ind(v("fb"), LP0), odd("d1b"), A.subtract)
+    tt(even("d1b"), ind(v("fb"), LP0), v("tmp5"), A.subtract)
+    act(v("fc"), v("fb", 0, 96))
+    tt(odd("d1b"), ind(v("fb"), LP1), v("fc"), A.add)
     ts(v("gtm"), v("dm", 0, 96), PR, A.is_gt)
     ts(v("tmp3", 0, K), v("dm"), PR, A.is_equal, BIG, A.mult)
     scan(v("mw"), v("m16", 0, K), v("tmp3", 0, K), A.min, A.max)
@@ -324,7 +335,7 @@ def rank_program(g, core, T, topo):
     fill(col("cd0", 0), 0.0)
     act(v("tmp2", 192, 288), v("tmp2", 0, 96), 1.0, 0.5)
     tt(v("cd0", 2, 194, 2), v("tmp2", 192, 288), v("tmp3", 288, 384), A.mult)
-    for name in ("pb", "pc", "bb", "bc"):
+    for name in ("pb", "pc", "pd", "bb", "bc"):
         const(even(name), 0.0)
     for b in range(4):
         quant(v("qe", 128 * b, 128 * b + 128), v("se", 128 * b, 128 * b + 128), v("eye", 3 - b, 515 - b))
@@ -334,12 +345,24 @@ def rank_program(g, core, T, topo):
     act(ends("me"), ends("me"), 1.0 / BIG / SMALL)
     for b in range(3):
         const(v("pcc", b, 6, 3), -(32.0 + 32 * b) / 64)
+    act(F192, PI, -1.0, float(HC))
     const(v("mx0"), -4096.0)
-    const(v("mx0", 0, None, 64), 1024.0)
+    act(v("mx0", 0, None, 64), v("ones", 0, 3), 1024.0, ROOT)
+    const(v("mx1"), -4096.0)
+    const(v("mx1", 0, None, 32), 1024.0)
+    const(odd("m01"), 1.0)
+    const(even("m01"), 0.0)
+    act(v("fmi"), v("fi", 0, 32), -1.0, PI)
+    act(v("cb6"), v("fi", 0, 6), -32.0, F192)
     const(v("rst"), 0.0)
     const(starts("rst"), 4096.0)
     act(GE, R2, -SG, 31 * SG + 1.0 / 128)
     act(GO, R21, -SG, 31 * SG + 1.0 / 128)
+    if OPT["gg"]:
+        const(v("mxg"), 4096.0)
+        act(col("aux", 7), ROOT, -1.0 / 131072, GE)
+        act(v("mxg", 0, 192, 64), v("ones", 0, 3), -1.0 / 128, col("aux", 7))
+        act(v("mxg", 192, 288, 32), v("ones", 0, 3), -1.0 / 128, GO)
     act(IDH, PI, -SG, 31 * SG - EPS / 2)
     act(F31, PI, 1.0, -31.0)
     act(v("idr"), v("fi"), -1.0, 31.0)
@@ -348,7 +371,8 @@ def rank_program(g, core, T, topo):
     const(starts("dd"), 0.0)
     fill(v("gd"), 0.0)
     const(even("wd"), 0.0)
-    const(even("cg0"), 0.0)
+    const(v("cg0"), 0.0)
+    const(even("cg1"), 0.0)
     ts(odd("cg1"), v("colc"), Q192, A.subtract, PI, A.add)
     const(v("sd"), 1.0)
     const(v("mcl"), 1.0)
@@ -358,9 +382,16 @@ def rank_program(g, core, T, topo):
             const(on(v("mcl", c, None, 32), 2 * h + 1), 0.0)
     const(v("cd"), 0.0)
     const(v("zz"), 0.0)
-    ts(v("swp"), v("pj", 8, 12), PR, A.add)
+    act(col("aux", 3), P2B, 0.5)
+    ts(col("aux", 4), PSB, -6.0, A.mult, 64.0, A.add)
+    ts(col("aux", 5), PSB, 4.0, A.mult, col("aux", 3), A.add)
+    ts(col("aux", 6), PX, col("aux", 4), A.mult, col("aux", 5), A.add)
+    ts(v("swp"), v("fi", 0, 16, 8), col("aux", 6), A.add)
     quant(v("qv"), v("sv"), v("vt"))
     iota(v("rs", C), [[0, 1024 - C]], 0, 0)
+    for b in range(4):
+        const(v("win", WIN * b + K + C, WIN * b + WIN), 0.0)
+        const(v("win", WIN * b, WIN * b + K), 0.0)
 
     def lv(name, l, c):
         c0 = 2 * (12 * (l // 2) + l % 2) + c
@@ -378,59 +409,78 @@ def rank_program(g, core, T, topo):
         scan(v("cv", 96 * k, 96 * k + 96), row, v("mw", 0, 96), A.add, A.mult)
         ts(v(off), v("cv", 96 * k + 15, 96 * k + 96, 16), SMALL, A.mult, 0.25, A.add)
 
+    begins = []
     for t, mask in enumerate(ROUNDS):
+        begins.append(len(ops))
         peer = T.cores[rank ^ mask]
         ne = len(topo.engines(peer, core))
         qt, st, ql, sl, lo, li = ["%s%d" % (n, t) for n in ("qt", "st", "ql", "sl", "lo", "li")]
         for b in range(4):
             mm(bank(4 + b), "e", b, v("qx"), v("sx"))
-            for k in range(2):
-                act(v("tt", 4 * HC * k + b, 4 * HC * (k + 1), 4), ("ps", 0, 128, 512 * (4 + b) + HC * k, 512 * (4 + b) + HC * (k + 1), 1), 1.0 / 32)
+            for k in range(OPT["n"]):
+                act(v("tt", 4 * W3 * k + b, 4 * W3 * k + 4 * W3, 4), third(4 + b, k), 1.0 / 32)
         for k in range(3):
             quant(v(qt, 128 * k, 128 * k + 128), v(st, 128 * k, 128 * k + 128), v("tt", 512 * k, 512 * k + 512))
-        send(v(ql), v(qt), peer, "big%d" % t, dt.uint8)
-        tile_sent = send(v(sl), v(st), peer, "big%d" % t)
+        tile_sent = [(send(v(ql), v(qt), peer, "big%d" % t, dt.uint8), TILE), (send(v(sl), v(st), peer, "big%d" % t), TILE)]
         for b in range(4):
-            for k in range(2):
-                act(v("win", WIN * b + K + HC * k, WIN * b + K + HC * (k + 1)), ("ps", 0, 128, 512 * (4 + b) + HC * k, 512 * (4 + b) + HC * (k + 1), 1), 1.0 / 16)
+            for k in range(OPT["n"]):
+                act(v("win", WIN * b + K + W3 * k, WIN * b + K + W3 * k + W3), third(4 + b, k), 1.0 / 32)
         act(v("sb1"), ind(v("ssb"), LP1))
         tt(v("cd0", 1, 193, 2), ind(v("ssb"), LP0), v("sb1"), A.is_ge)
         scan(v("sca"), v("cd0", 1, 193), v("mo"), A.add, A.mult)
         ts(v("o1"), ends("sca"), SMALL, A.mult, 0.25, A.add)
         scan(v("pa"), v("cd0", 0, 192), v("d1p"), A.mult, A.add)
         scan(v("ba"), v("cd0", 0, 192), v("d1b"), A.mult, A.add)
-        act(v("b1"), odd("ba"))
         act(odd("pb"), ind(v("pa"), v("o1")))
-        act(odd("pc"), ind(v("pb"), v("o1")))
-        act(v("p4"), ind(v("pc"), v("o1")))
-        wrap("o3", odd("pc"), 0)
-        act(v("p7"), ind(v("p4"), v("o3")))
-        act(v("p10"), ind(v("p7"), v("o3")))
-        wrap("o7", v("p7"), 1)
-        wrap("o10", v("p10"), 2)
-        for o, w, off, base in ((odd("bb"), "ba", "o1", v("b1")), (odd("bc"), "bb", "o1", odd("ba")), (v("b4"), "bc", "o1", odd("ba")),
-                                (v("b7"), "b4", "o3", odd("bc")), (v("b10"), "b7", "o3", odd("bc")), (v("b13"), "b10", "o3", odd("bc")),
-                                (v("b20"), "b13", "o7", v("b7"))):
+        own = v("fb", 0, 96)
+        if OPT["anc"]:
+            act(v("p3"), ind(v("pb"), v("o1")))
+            wrap("o2", odd("pb"), 3)
+            wrap("o3", v("p3"), 0)
+            act(v("p5"), ind(v("p3"), v("o2")))
+            steps = ((odd("bb"), "ba", "o1", own), (v("b4"), "bb", "o1", own), (v("b6"), "b4", "o2", odd("ba")), (v("b8"), "b6", "o2", odd("ba")),
+                     (v("b9"), "b6", "o3", odd("bb")), (v("b11"), "b8", "o3", odd("bb")), (v("b14"), "b9", "o3", odd("bb")),
+                     (v("b22"), "b14", "o8", v("b8")), (odd("vv"), "b22", "o11", v("b11")))
+        else:
+            act(odd("pc"), ind(v("pb"), v("o1")))
+            act(odd("pd"), ind(v("pc"), v("o1")))
+            act(v("p5"), ind(v("pd"), v("o1")))
+            wrap("o3", odd("pc"), 0)
+            steps = ((odd("bb"), "ba", "o1", own), (odd("bc"), "bb", "o1", own), (v("b5"), "bc", "o1", own),
+                     (v("b8"), "b5", "o3", odd("bb")), (v("b11"), "b8", "o3", odd("bb")), (v("b14"), "b11", "o3", odd("bb")),
+                     (v("b22"), "b14", "o8", v("b8")), (odd("vv"), "b22", "o11", v("b11")))
+        act(v("p8"), ind(v("p5"), v("o3")))
+        act(v("p11"), ind(v("p8"), v("o3")))
+        wrap("o8", v("p8"), 1)
+        wrap("o11", v("p11"), 2)
+        for o, w, off, base in steps:
             tt(o, ind(v(w), v(off)), base, A.add)
-        tt(v("bx"), v("b10"), v("sr"), A.add)
-        tt(odd("vv"), ind(v("b20"), v("o10")), v("bx"), A.add)
         for e in range(2):
             scan(v("pk", 96 * e, 96 * e + 96), odd("pa"), v("me", 96 * e, 96 * e + 96), A.add, A.mult)
         act(v("pc1"), ends("pk"), SMALL / 64)
         tt(v("pc2"), v("pc1"), v("pcc"), A.add)
         ts(even("vv"), odd("vv"), 96.0, A.is_ge, -128.0, A.mult)
-        ts(v("bm", 96), odd("vv"), 96.0, A.is_ge, 64.0, A.mult)
-        scan(v("se2"), v("mx0"), v("vv"), A.max, A.subtract)
-        scan(v("so"), even("mx0"), v("bm", 96), A.max, A.subtract)
-        tt(v("bm", 0, 96), odd("vv"), even("vv"), A.add)
+        ts(v("b1"), odd("vv"), 96.0, A.is_ge, 64.0, A.mult)
+        scan(v("se2"), v("mx0"), v("vv"), A.max, A.subtract, -4096.0)
+        scan(v("so"), v("mx1"), v("b1"), A.max, A.subtract)
+        if OPT["gg"]:
+            act(v("vg", 1, 192, 2), odd("vv"), 1.0 / 131072)
+            ts(v("vg", 0, 192, 2), odd("vv"), 96.0, A.is_ge, -1.0 / 1024, A.mult)
+            ts(v("vg", 192), odd("vv"), 96.0, A.is_ge, 1.0 / 2048, A.mult)
+            scan(v("gs", 0, 192), v("mxg", 0, 192), v("vg", 0, 192), A.min, A.add, 4096.0)
+            scan(v("gs", 192), v("mxg", 192), v("vg", 192), A.min, A.add, 4096.0)
+        scan(v("b0"), v("m01"), v("vv"), A.mult, A.add)
         for e, (src, gc) in enumerate(((odd("se2"), GE), (v("so"), GO))):
             part = v("yb", 96 * e, 96 * e + 96)
             scan(back(part), v("rst", 0, 96), back(src), A.add, A.min)
             turn(v("yrow", e, None, 2), part)
-            ts(v("gq", 96 * e, 96 * e + 96), part, -1.0 / 131072, A.mult, gc, A.add)
+            if not OPT["gg"]:
+                ts(v("gq", 96 * e, 96 * e + 96), part, -1.0 / 131072, A.mult, gc, A.add)
+            else:
+                scan(back(v("gq", 96 * e, 96 * e + 96)), v("m32", 0, 96), back(v("gs", 192) if e else v("gs", 1, 192, 2)), A.mult, A.max)
             turn(v("gr0", e, None, 2), v("gq", 96 * e, 96 * e + 96))
             for b in range(3):
-                act(slot("ub", 3 * e + b), slot("bm", 3 * e + b), col("pc2", 3 * e + b), 1.0)
+                act(slot("ub", 3 * e + b), slot("b1", b) if e else v("b0", 64 * b + 1, 64 * b + 64, 2), col("pc2", 3 * e + b), 1.0)
             turn(v("utn", e, None, 2), v("ub", 96 * e, 96 * e + 96))
         turn(v("ybs"), v("yrow"))
         act(odd("ws0"), starts("ybs"), -1.0 / 65536, 1.0 / 64 + EPS)
@@ -451,14 +501,30 @@ def rank_program(g, core, T, topo):
                     tt(v("nn"), v("pp"), ends("sb"), A.subtract)
                     act(v("n62"), v("nn"), 1.0, 62 * SG)
             hit, op = (v("yt"), A.mult) if l else (v("yrow"), A.min)
+            if l == 3:
+                act(v("keep"), odd(ws), 1.0, -EPS, FN.Sign)
+                for s in range(6):
+                    act(slot("df", s), v("fmi"), col("keep", s), col("cb6", s))
+                scan(v("cs"), hit, v("df"), op, A.max)
+                for h in range(2):
+                    for qs in range(2):
+                        o, i = on(v("cd", 192 * qs + 16, 192 * qs + 192, 32), 2 * h + 1), on(ends("cs"), 2 * qs + h)
+                        if not OPT["c3"] & 1 << 2 * h + qs:
+                            act(o, i, -1.0, 192.0 * qs)
+                        elif qs:
+                            ts(o, i, -1.0, A.mult, 192.0, A.add)
+                        else:
+                            act(o, i, -1.0)
+                break
             scan(v("cs"), hit, v("idr"), op, A.max)
             act(lv("cg1", l, 0), ends("cs"), 1.0, F31)
             act(lv("cg0", l, 1), odd(ws), -1.0, EPS, FN.Sign)
-            if l == 3:
-                break
             spread(l)
             scan(v("ks"), hit, v(gr), op, A.max)
-            scan(v("cz"), hit, v("ids"), op, A.max)
+            if l >= OPT["cz"]:
+                scan(v("cz"), hit, v("ids"), op, A.max)
+            else:
+                act(ends("cz"), ends("cs"), SG)
             if l == 2:
                 for to, q in across(3, 18):
                     act(to("sd"), on(odd(ws), q), 1024.0, -4.25)
@@ -466,7 +532,7 @@ def rank_program(g, core, T, topo):
                 for to, q in across(3, 17):
                     tt(to("sd"), on(ends("cz"), q), on(ends("ks"), q), A.subtract)
             for s in range(6):
-                if s < 3:
+                if s < OPT["dd"][l]:
                     ts(slot("dd", s, 1), slot("utn", s, 1), col("cs", 32 * s + 31), A.add, 0.0, A.not_equal)
                 else:
                     act(slot("dd", s, 1), slot("utn", s, 1), 1.0, col("cs", 32 * s + 31), FN.Abs)
@@ -487,12 +553,16 @@ def rank_program(g, core, T, topo):
             scan(v("cg2", 24 * a, 24 * a + 24), v("cg0", 24 * a, 24 * a + 24), v("cg1", 24 * a, 24 * a + 24), A.mult, A.add)
             for h in range(2):
                 for qs in range(2):
-                    (copy if qs and a else act)(on(v("cd", 192 * qs, 192 * qs + 192, 16), 2 * h + a), on(v("cg2", 24 * a + 1, 24 * a + 24, 2), 2 * qs + h))
+                    act(on(v("cd", 192 * qs, 192 * qs + 192, 16 << a), 2 * h + a), on(v("cg2", 24 * a + 1, 24 * a + 24, 2 << a), 2 * qs + h))
         scan(v("cbs"), v("m16"), v("cd"), A.mult, A.add)
         turn(v("cf"), v("cbs"))
         scan(v("sbs"), v("mcl"), v("sd"), A.mult, A.add)
         turn(v("sf"), v("sbs"))
-        ts(v("eqt"), v("sbs"), 0.0, A.is_equal, 1024.0, A.mult)
+        if OPT["eqt"]:
+            act(v("eqa"), v("sbs"), 1024.0, 0.0, FN.Abs)
+            act(v("eqt"), v("eqa"), -1.0, 1024.0, FN.Relu)
+        else:
+            ts(v("eqt"), v("sbs"), 0.0, A.is_equal, 1024.0, A.mult)
         act(v("sgn"), v("sf"), 1.0, -0.5, FN.Sign, col("cnt", 0))
         ts(v("eq2"), v("sf"), 0.0, A.is_equal, 2.0, A.mult)
         scan(v("p2"), v("eq2"), v("ones"), A.add, A.mult, col("cnt", 0))
@@ -502,67 +572,93 @@ def rank_program(g, core, T, topo):
         for h in range(2):
             turn(on(v("t1", 32, 64), 2 * h + 1), on(v("rs", 22, None, 32), 2 * h + 1))
             turn(on(v("t1", 32, 64), 2 * h), on(v("rs", 16, None, 32), 2 * h + 1))
-        copy(v("t2"), ind(v("t1"), v("swp")))
-        turn(v("t3"), v("t2"))
-        for u in range(2):
-            ts(v("opl", u, None, 2), v("t3", 32 * u, 32 * u + 12), 0.5, A.mult, 191.25, A.add)
+        turn(v("t2", 64, 96), v("t1", 16, 48))
+        turn(v("t2", 0, 64), v("t1"))
+        ts(v("opl"), ind(v("t2"), v("swp")), 0.5, A.mult, 191.25, A.add)
         for b in range(4):
-            mm(bank(b), "e", b, v(ql), v(sl), waits=[("big%d" % t, 2 * ne)], behind=[(tile_sent, TILE)])
-            for k in range(2):
-                act(v("gall", C * b + HC * k, C * b + HC * (k + 1)), ("ps", 0, 128, 512 * b + HC * k, 512 * b + HC * (k + 1), 1), 1.0 / 32)
+            mm(bank(b), "e", b, v(ql), v(sl), waits=[("big%d" % t, 2 * ne)], behind=tile_sent)
+            for k in range(OPT["n"]):
+                act(v("gall", C * b + W3 * k, C * b + W3 * k + W3), third(b, k), 1.0 / 64)
         for k in (1, 0):
             for b in range(4):
-                mm(bank(4 * k + b, HC), "e", b, half("qx", k), half("sx", k), True, False)
-        copy(ind(v("cw"), v("opl")), v("cf"))
+                mm(bank(4 * k + b, CUT[k + 1] - CUT[k]), "e", b, half("qx", k), half("sx", k), True, False)
+        copy(ind(v("cw"), v("opl", 0, 24)), v("cf"))
         scan(v("csw"), v("cw", 0, K), v("mw"), A.add, A.mult)
         ts(v(lo), v("csw", 15, None, 16), SMALL, A.mult, HC + 0.25, A.add)
         list_sent = send(v(li), v(lo), peer, "lst%d" % t)
         for b in range(4):
-            act(v("ee", K * b, K * b + K), ind(v("win", WIN * b + K, WIN * b + WIN), v(lo)), 0.5)
+            o, i = v("ee", K * b, K * b + K), ind(v("win", WIN * b + K, WIN * b + WIN), v(lo))
+            if b in LATE:
+                continue
+            if b in OPT["ee"]:
+                ts(o, i, 0.5, A.mult)
+            else:
+                act(o, i, 0.5)
         for a in range(2):
             act(v("zz", 32 * a, 32 * a + 12), v("cd", 16 * a, None, 32))
         turn(v("z1"), v("zz"))
-        act(v("z2"), ind(v("z1"), v("swp")))
-        turn(v("z3"), v("z2"))
-        act(v("kk"), v("t3", 0, 44), 0.5, 191.0 - K - HC)
-        act(v("ky"), v("t3", 0, 44), 800.0, 1600.0 * (191.5 - K) - K - HC)
+        turn(v("z2", 64, 96), v("z1", 16, 48))
+        turn(v("z2", 0, 64), v("z1"))
+        act(v("kk"), ind(v("t2"), v("swp")), 0.5, 191.0 - K - HC)
+        act(v("ky"), ind(v("t2"), v("swp")), 800.0, 1600.0 * (191.5 - K) - K - HC)
         tt(v("km"), v("kk"), v("ky"), A.max)
-        tt(v("kn"), v("km"), v("z3", 0, 44), A.min)
-        for u in range(2):
-            ts(v("ozl", u, None, 2), v("kn", 32 * u, 32 * u + 12), K + HC + 0.25, A.add)
-        if t == 2:
-            act(v("clo"), v("cf"), 1.0, float(HC))
-            dma("Y", lambda: T.cl[:], lambda: T.clo[0:128:16, :], [v("clo")], [])
+        tt(v("kn"), ind(v("z2"), v("swp")), v("km"), A.min)
+        ts(v("ozl"), v("kn", 0, 24), K + HC + 0.25, A.add)
+        if LATE:
+            tt(v("kl"), ind(v("z2"), v("swp")), v("ky"), A.max)
+            ts(v("ofl"), v("kl", 0, 24), float(HC), A.min, K + HC + 0.25, A.add)
+        def places(k):
+            return v("ozl", CUT[k] // 16, CUT[k + 1] // 16)
+
+        for b in LATE:
+            act(v("fm", C * (b - LATE[0]), C * (b - LATE[0]) + C), ind(v("win", WIN * b, WIN * b + WIN), v("ofl")), 0.5)
+        arrival = {"waits": [("lst%d" % t, ne)], "behind": [(list_sent, LIST)]}
+        last = {"V": [], "S": []}
+
+        def in_turn():
+            ops[-1][7].extend(last[ops[-1][0]])
+            last[ops[-1][0]] = [(len(ops) - 1, 0.0)]
+
         for b in range(4):
-            tt(v("win", WIN * b, WIN * b + K), ind(v("gall", C * b, C * b + C), v(li)), v("ee", K * b, K * b + K), A.add,
-               waits=[("lst%d" % t, ne)], behind=[(list_sent, LIST)])
-        for k in range(2):
-            for b in range(4):
-                o = v("zt", 4 * HC * k + b, 4 * HC * (k + 1), 4)
-                i = ind(v("win", WIN * b, WIN * b + WIN), v("ozl", 12 * k, 12 * k + 12))
-                if b == 3 or (b == 2 and k):
-                    ts(o, i, 0.5, A.mult)
+            o, i = v("win", WIN * b, WIN * b + K), ind(v("gall", C * b, C * b + C), v(li))
+            if b in LATE:
+                act(o, i, **arrival)
+            else:
+                tt(o, i, v("ee", K * b, K * b + K), A.add, **arrival)
+            in_turn()
+        for k, b in OPT["order"]:
+            if b < 4:
+                o = v("zt", 4 * CUT[k] + b, 4 * CUT[k + 1], 4)
+                i = ind(v("win", WIN * b, WIN * b + WIN), places(k))
+                if b in LATE:
+                    tt(o, i, v("fm", C * (b - LATE[0]) + CUT[k], C * (b - LATE[0]) + CUT[k + 1]), A.add)
                 else:
-                    act(o, i, 0.5)
-            quant_half("qz", "sz", "zt", k)
-            for b in range(4):
-                mm(bank(4 * k + b, HC), "w", b, half("qz", k), half("sz", k), False, True)
+                    (copy if 4 * k + b in OPT["z"] else act)(o, i)
+            else:
+                quant_half("qz", "sz", "zt", k)
+            in_turn()
+            if b == 4:
+                for c in range(4):
+                    mm(bank(4 * k + c, CUT[k + 1] - CUT[k]), "w", c, half("qz", k), half("sz", k), False, True)
         for k in range(2):
+            c0, c1 = CUT[k], CUT[k + 1]
             for b in range(4):
-                o = v("xn", 4 * HC * k + b, 4 * HC * (k + 1), 4)
-                if b % 2 if k else b == 3:
-                    ts(o, bank(4 * k + b, HC), 1.0 / 32, A.mult)
+                o = v("xn", 4 * c0 + b, 4 * c1, 4)
+                if 4 * k + b in OPT["x"]:
+                    ts(o, bank(4 * k + b, c1 - c0), 1.0 / 32, A.mult)
                 else:
-                    act(o, bank(4 * k + b, HC), 1.0 / 32)
+                    act(o, bank(4 * k + b, c1 - c0), 1.0 / 32)
             quant_half("qx", "sx", "xn", k)
             if t < 2:
                 scores(k)
             else:
-                mm(bank(k, HC), "v", 0, half("qx", k), half("sx", k))
-                dma("Y", lambda k=k: T.oc[:, 4 * HC * k:4 * HC * (k + 1)], lambda k=k: T.qx[:, HC * k:HC * (k + 1)].bitcast(dt.uint8), [half("qx", k)], [])
-                (copy if k else act)(half("yo", k), bank(k, HC))
-                dma("Y" if k else "S", lambda k=k: T.y[:, HC * k:HC * (k + 1)], lambda k=k: T.yo[:, HC * k:HC * (k + 1)], [half("yo", k)], [])
+                mm(bank(k, c1 - c0), "v", 0, half("qx", k), half("sx", k))
+                dma("Y", lambda c0=c0, c1=c1: T.oc[:, 4 * c0:4 * c1], lambda c0=c0, c1=c1: T.qx[:, c0:c1].bitcast(dt.uint8), [half("qx", k)], [])
+                (copy if k else act)(half("yo", k), bank(k, c1 - c0))
+                dma("Y" if k else "S", lambda c0=c0, c1=c1: T.y[:, c0:c1], lambda c0=c0, c1=c1: T.yo[:, c0:c1], [half("yo", k)], [])
 
+    act(v("clo"), v("cf"), 1.0, float(HC))
+    dma("Y", lambda: T.cl[:], lambda: T.clo[0:128:16, :], [v("clo")], [])
     for k in range(4):
         dma("S" if k % 2 else "Y", lambda k=k: T.osc[4 * k:4 * k + 4, :], lambda k=k: T.sx[32 * k:32 * k + 4, :], [v("sx")], [])
 
@@ -585,51 +681,72 @@ def rank_program(g, core, T, topo):
     def gap(m, n):
         if ops[m][5] == "d":
             return lands[m]
-        return 0.0 if ops[m][0] == "P" and ops[n][0] == "P" else WAKE
+        return 0.0 if ops[m][0] == "P" and ops[n][0] == "P" else OPT["wake"]
 
     edges = [[(m, gap(m, n)) for m in deps[n]] + ops[n][7] for n in range(len(ops))]
-    tail = [op[6] + (LOAD if op[5] == "d" else 0.0) for op in ops]
-    later = [[] for _ in ops]
-    for n in range(len(ops) - 1, -1, -1):
-        for m, d in edges[n]:
-            tail[m] = max(tail[m], ops[m][6] + d + tail[n])
-            later[m].append(n)
-    for n in range(loads):
-        tail[n] = 1e9 - n
-    left = [len(e) for e in edges]
-    ready = {q: [] for q in "VSPGY"}
-    at = {}
-    for n in range(len(ops)):
-        if not left[n]:
-            ready[ops[n][0]].append(n)
-            at[n] = 0.0
-    free = {q: 0.0 for q in ready}
-    end = {}
-    order = []
-    while len(order) < len(ops):
-        best = None
-        for q, c in ready.items():
-            if not c:
-                continue
-            n = max(c, key=lambda n: (tail[n], -n))
-            while at[n] > free[q]:
-                fit = [k for k in c if k != n and max(free[q], at[k]) + ops[k][6] <= at[n] + 40.0 and at[k] < at[n]]
-                if not fit:
-                    break
-                n = max(fit, key=lambda n: (tail[n], -n))
-            s = max(free[q], at[n])
-            if best is None or s < best[0]:
-                best = (s, n)
-        s, n = best
-        q = ops[n][0]
-        ready[q].remove(n)
-        free[q] = end[n] = s + ops[n][6]
-        order.append(n)
-        for k in later[n]:
-            left[k] -= 1
-            if not left[k]:
-                at[k] = max(end[m] + (min(d, 6000.0) if d == TILE else d) for m, d in edges[k])
-                ready[ops[k][0]].append(k)
+    after = [LOAD if op[5] == "d" else 0.0 for op in ops]
+
+    def turned(tile):
+        later = [[] for _ in ops]
+        for n in range(len(ops)):
+            for m, d in edges[n]:
+                later[m].append((n, {TILE: tile * TILE, LIST: LIST * OPT["back"]}.get(d, d)))
+        return later
+
+    def play(order, far, slow):
+        free, end = {q: 0.0 for q in "VSPGY"}, {}
+        for n in order:
+            s = max([free[ops[n][0]]] + [end[m] + {TILE: far * TILE, LIST: far * LIST * 0.85}.get(d, d) for m, d in edges[n]])
+            free[ops[n][0]] = end[n] = s + slow * ops[n][6]
+        return max(end[n] + after[n] for n in end)
+
+    def lay(turns, links, least):
+        busy = {q: [] for q in "VSPGY"}
+        end = {}
+        for n in turns:
+            s = max([least[n]] + [end[m] + d for m, d in links[n]])
+            row = busy[ops[n][0]]
+            k, hi = 0, len(row)
+            while k < hi:
+                if row[(k + hi) // 2][1] <= s:
+                    k = (k + hi) // 2 + 1
+                else:
+                    hi = (k + hi) // 2
+            while k < len(row) and row[k][0] < s + ops[n][6] - 1e-6:
+                s = max(s, row[k][1])
+                k += 1
+            end[n] = s + ops[n][6]
+            row.insert(k, (s, end[n]))
+        return end
+
+    if not _ORDER:
+        later = turned(OPT["tile"])
+        kin = [n - max([r for r in begins if r <= n] or [-len(ops)]) for n in range(len(ops))]
+
+        def arrange(urge):
+            tail = [0.0] * len(ops)
+            for n in range(len(ops) - 1, -1, -1):
+                tail[n] = ops[n][6] + urge.get(kin[n], 0.0) + max([after[n]] + [d + tail[k] for k, d in later[n]])
+            found = []
+            for _ in range(OPT["passes"]):
+                end = lay(sorted(range(len(ops)), key=lambda n: (n >= loads, -tail[n] if n >= loads else n, n)), edges, [0.0] * len(ops))
+                order = sorted(range(len(ops)), key=lambda n: (end[n] - ops[n][6], n))
+                found.append((play(order, 1.0, 1.0) + play(order, 1.5, 1.1) + play(order, 0.8, 1.3), order))
+                tail = lay(sorted(range(len(ops)), key=lambda n: (-end[n], -n)), later, after)
+            return min(found)
+
+        urge, seed = {}, 1
+        best = arrange(urge)
+        for _ in range(OPT["tries"]):
+            trial = dict(urge)
+            for _ in range(OPT["many"]):
+                seed = seed * 48271 % 2147483647
+                trial[kin[seed % len(ops)]] = float(seed // len(ops) % OPT["amp"])
+            found = arrange(trial)
+            if found[0] < best[0]:
+                best, urge = found, trial
+        _ORDER.extend(best[1])
+    order = list(_ORDER)
 
     place = {n: k for k, n in enumerate(order)}
     seen = {}
@@ -656,8 +773,8 @@ def rank_program(g, core, T, topo):
         for m in keep[n]:
             queue[q].wait_ge(T.sem[mark[m][0]], mark[m][1])
         for s, val in waits:
-            if s not in waited:
-                waited.add(s)
+            if (q, s) not in waited:
+                waited.add((q, s))
                 queue[q].wait_ge(T.sem[s], val)
         done = call()
         if kind == "d":

from concourse.mybir import dt, AluOpType, ActivationFunctionType

C, K, ROUNDS = 384, 160, (1, 2, 3)
HC = C // 2
F32, BF, HF, I32, U16, MX, U8 = "float32", "bfloat16", "float16", "int32", "uint16", "float8_e4m3fn_x4", "uint8"
BIG = 2.0 ** 20
SMALL = 2.0 ** 18
TINY = 2.0 ** -60
WIN = K + C + 16
SG = 1.0 / 64
EPS = SG / 64
WAKE, LOAD, LIST, TILE = 170.0, 2200.0, 1500.0, 6000.0

_SB = {
    "xt": (4 * C, BF), "xn": (4 * C, BF), "ut": (512, BF), "vt": (512, BF), "eye": (528, BF),
    "qx": (C, MX), "sx": (C, U8), "qu": (128, MX), "su": (128, U8), "qup": (128, MX), "sup": (128, U8),
    "qv": (128, MX), "sv": (128, U8), "qw": (512, MX), "sw": (512, U8), "qe": (512, MX), "se": (512, U8),
    "qz": (C, MX), "sz": (C, U8), "tt": (4 * C, BF), "zt": (4 * C, BF),
    "win": (4 * WIN, F32), "gall": (4 * C, F32), "ee": (4 * K, F32), "fm": (2 * C, F32), "yo": (C, F32), "clo": (C, F32),
    "pr": (48, I32), "pi": (8, I32), "pj": (16, I32),
    "ones": (C, BF), "m32": (192, BF), "m16": (C, BF), "mcl": (C, BF), "mx0": (192, BF), "rst": (192, BF),
    "fi": (192, BF), "flo": (192, BF), "fb": (192, BF), "dm": (K, BF),
    "mw": (K, BF), "mo": (192, BF), "me": (192, BF), "tmp2": (288, BF), "tmp3": (384, BF), "tmp4": (192, BF),
    "cd0": (208, BF), "d1p": (192, BF), "d1b": (192, BF), "pd": (192, BF), "m01": (192, BF), "b0": (192, BF), "df": (192, BF), "eqa": (C, BF),
    "ssb": (192, F32), "sb1": (96, F32), "sca": (192, BF),
    "pa": (192, BF), "pb": (192, BF), "pc": (192, BF), "cv": (384, BF), "ba": (192, BF), "bb": (192, BF), "bc": (192, BF),
    "vv": (192, BF), "se2": (192, BF), "yb": (192, BF), "yrow": (192, BF), "ybs": (192, BF),
    "pk": (192, BF), "ub": (192, BF), "utn": (192, BF), "gq": (192, HF), "gs": (288, HF),
    "idr": (192, BF), "ids": (192, BF), "idb": (192, BF), "gr0": (192, HF), "gr1": (192, HF), "gd": (192, HF), "gb": (192, HF),
    "cs": (192, BF), "cz": (192, BF), "ks": (192, HF), "dd": (192, BF), "sa": (192, HF), "sb": (192, BF), "pbc": (192, HF), "prow": (192, HF),
    "y1": (192, BF), "yt": (192, BF),
    "sd": (C, BF), "sbs": (C, BF), "sf": (C, BF), "eq2": (C, BF), "eqt": (C, BF), "sgn": (C, BF), "p2": (C, BF), "p2t": (C, BF), "rs": (1024, BF),
    "cd": (C, BF), "cbs": (C, BF), "cf": (C, BF), "cw": (C, BF), "csw": (K, BF),
}
for _t in range(3):
    _SB["qt%d" % _t] = (C, MX)
    _SB["st%d" % _t] = (C, U8)
    _SB["ql%d" % _t] = (C, MX)
    _SB["sl%d" % _t] = (C, U8)
    _SB["lo%d" % _t] = (10, U16)
    _SB["li%d" % _t] = (10, U16)
_PART = {}
for _pool, _d, _names in (
        ("fpool", F32, {"pf": 24, "aux": 8, "pcc": 6, "pc1": 6, "pc2": 6, "ws0": 12, "ws1": 12, "ws2": 12, "ws3": 12, "wd": 12, "xx": 6, "pp": 6,
                        "cb6": 6, "keep": 6, "cand": 6, "nn": 6, "n62": 6, "cg0": 48, "cg1": 48, "cg2": 48, "colc": 24, "cnt": 1, "kk": 32, "ky": 32, "km": 32, "kn": 32, "kl": 32,
                        "sw0": 32, "sw1": 32}),
        ("bpool", BF, {"t1": 64, "t2": 96, "zz": 64, "z1": 64, "z2": 96,
                       "p3": 96, "b4": 96, "b6": 96, "b9": 96, "p5": 96, "p8": 96, "p11": 96, "b5": 96, "b8": 96, "b11": 96, "b14": 96, "b22": 96, "mx1": 96, "vg": 288, "mxg": 288, "gtm": 96, "tmp": 192, "fc": 96, "tmp5": 96, "b1": 96, "so": 96, "fmi": 32}),
        ("upool", U16, {"uoff": 8, "sel": 2, "lp": 32, "o1": 6, "o2": 6, "o3": 6, "o8": 6, "o11": 6, "swp": 2, "opl": 32, "ozl": 24, "ofl": 24})):
    _at = 0
    for _k, _n in _names.items():
        _PART[_k] = (_pool, _at, _n)
        _at += (_n + 15) // 16 * 16
    _SB[_pool] = (_at, _d)
SCRATCH = {k: ("sbuf", [128, n], d) for k, (n, d) in _SB.items()}
SCRATCH["ps"] = ("psum", [128, 4096], F32)
NDMA = 24
SEMAPHORES = ["cV", "cS", "cP", "cG", "sent"] + ["d%d" % k for k in range(NDMA)] + ["big%d" % t for t in range(3)] + ["lst%d" % t for t in range(3)]

OPT = {"dd": (3, 3, 0), "cz": 0, "c3": 10, "eqt": 1, "t2": 0, "cut": 192, "late": (2, 3), "ee": (1,), "z": (), "order": ((0, 0), (0, 1), (0, 2), (0, 3), (1, 2), (0, 4), (1, 0), (1, 1), (1, 3), (1, 4)), "x": (3, 7), "passes": 2, "tile": 1.6, "anc": 1, "gg": 0, "tries": 100, "many": 12, "amp": 300,
       "cy": 0.87, "sfix": 0, "wake": 210.0, "n": 2, "back": 0.7}
_ORDER = []
A = AluOpType
FN = ActivationFunctionType


def v(name, c0=0, c1=None, step=1, p0=0, p1=128):
    name, at, n = _PART[name] if name in _PART else (name, 0, _SB[name][0])
    return (name, p0, p1, at + c0, at + (n if c1 is None else c1), step)


def ind(win, off):
    return ("@", win, off)


def col(name, c):
    return v(name, c, c + 1)


def back(a):
    return a[:5] + (-a[5],)


def on(a, q):
    return (a[0], 32 * q, 32 * q + 32) + a[3:]


def _len(a):
    return 16 * _len(a[2]) if a[0] == "@" else len(range(a[3], a[4], abs(a[5])))


_COLS = {}


def _cols(a):
    k = a[3:]
    if k not in _COLS:
        _COLS[k] = sum(1 << c for c in range(a[3], a[4], abs(a[5])))
    return _COLS[k]


def _meet(a, b):
    if a[0] == "ps":
        return a[3] // 512 == b[3] // 512
    if a[2] <= b[1] or b[2] <= a[1] or a[4] <= b[3] or b[4] <= a[3]:
        return False
    return bool(_cols(a) & _cols(b))


def _ns(o, ins, rate=None, more=0.0):
    if o[0] == "@":
        return 50 + 3.5 * OPT["cy"] * _len(o)
    if ins[0][0] == "@":
        return 55 + 1.5 * OPT["cy"] * _len(o)
    if rate is None:
        rate = 0.5 if all(a[0] != "ps" and _SB[a[0]][1] in (BF, HF) for a in [o] + ins) else 1.0
    return max(64, rate * _len(o)) * OPT["cy"] + more


def rank_program(g, core, T, topo):
    rank = T.rank_of(core)
    if rank is None:
        return
    CUT, LATE = (0, OPT["cut"], C), OPT["late"]
    W3 = C // OPT["n"]
    ops = []
    lands = {}

    def real(a, cast=None):
        if a[0] == "@":
            return real(a[1], cast).indirect(real(a[2]))
        name, p0, p1, c0, c1, step = a
        if step < 0:
            return T[name][p0:p1, range(c0, c1, -step)[-1]:(c0 - 1 if c0 else None):step]
        r = T[name][p0:p1, c0:c1] if step == 1 else T[name][p0:p1, c0:c1:step]
        return r.bitcast(cast) if cast is not None else r

    def parts(a):
        if isinstance(a, tuple):
            return [a[1], a[2]] if a[0] == "@" else [a]
        return []

    def arg(a):
        return real(a) if isinstance(a, tuple) else a

    def add(q, call, ins, outs, ns, waits=(), kind="c", behind=()):
        r, w = [], []
        for a in ins:
            r += parts(a)
        for a in outs:
            if a[0] == "@":
                w.append(a[1])
                r.append(a[2])
            else:
                w.append(a)
        ops.append((q, call, r, w, list(waits), kind, ns, list(behind)))
        return len(ops) - 1

    def copy(o, i):
        add("V", lambda: g.vector.tensor_copy(real(o), real(i)), [i], [o], _ns(o, [i]))

    def pick(o, i):
        add("V", lambda: g.vector.tensor_copy(real(o, dt.uint32), real(i, dt.uint32)), [i], [o], _ns(o, [i]))

    def tt(o, a, b, op, waits=(), behind=()):
        add("V", lambda: g.vector.tensor_tensor(real(o), real(a), real(b), op), [a, b], [o], _ns(o, [a], 2.0), waits, "c", behind)

    def ts(o, a, s1, op0, s2=None, op1=None):
        if op1 is None:
            add("V", lambda: g.vector.tensor_scalar(real(o), real(a), arg(s1), None, op0), [a, s1], [o], _ns(o, [a]))
        else:
            add("V", lambda: g.vector.tensor_scalar(real(o), real(a), arg(s1), arg(s2), op0, op1), [a, s1, s2], [o], _ns(o, [a]))

    def scan(o, d0, d1, op0, op1, init=0.0):
        add("V", lambda: g.vector.tensor_tensor_scan(real(o), real(d0), real(d1), arg(init), op0, op1), [d0, d1, init], [o], _ns(o, [d0, d1]))

    def turn(o, i):
        add("V", lambda: g.vector.transpose(real(o), real(i)), [i], [o], _ns(o, [i]))

    def fill(o, c):
        add("V", lambda: g.vector.memset(real(o), c), [], [o], _ns(o, [o]))

    def quant(q, s, i):
        add("V", lambda: g.vector.quantize_mx(real(q), real(s), real(i)), [i], [q, s], (15 + 0.265 * _len(i)) * OPT["cy"])

    def act(o, i, scale=1.0, bias=0.0, func=None, acc=None, waits=(), behind=()):
        f = func if func is not None else (FN.Copy if not isinstance(bias, tuple) and bias == 0.0 else FN.Identity)
        if acc is None:
            add("S", lambda: g.scalar.activation(real(o), real(i), f, bias=arg(bias), scale=arg(scale)), [i, scale, bias], [o], _ns(o, [i], 1.0, OPT["sfix"]),
                waits, "c", behind)
        else:
            add("S", lambda: g.scalar.activation(real(o), real(i), f, bias=arg(bias), scale=arg(scale), accum_out=real(acc)), [i, scale, bias], [o, acc],
                20 + _ns(o, [i], 1.0, OPT["sfix"]))

    def const(o, c):
        act(o, (("ones",) + o[1:3] + (0, _len(o), 1)), c)

    def mm(o, l, b, rq, rs, start=True, stop=True, waits=(), behind=()):
        lq, ls = v("q" + l, 128 * b, 128 * b + 128), v("s" + l, 128 * b, 128 * b + 128)
        add("P", lambda: g.tensor.matmul_mx(real(o), real(lq), real(ls), real(rq), real(rs), start, stop), [lq, ls, rq, rs], [o], 0.6 * (_len(rq) + 16),
            waits, "c", behind)

    def iota(o, pattern, base, cm):
        if _SB[o[0]][1] == I32:
            add("G", lambda: g.iota(real(o), pattern, base, cm), [], [o], 130 + 2 * _len(o))
        else:
            add("G", lambda: g.iota(real(o), pattern, base, cm, allow_small_or_imprecise_dtypes=True), [], [o], 130 + 2 * _len(o))

    def select(o, i, pattern, op, base, cm):
        add("G", lambda: g.affine_select(real(o), real(i), pattern, op, 0.0, base, cm), [i], [o], 170 + 2 * _len(o))

    def dma(q, mk_out, mk_in, ins, outs, ns=LOAD):
        e = g.sync if q == "Y" else g.scalar
        lands[add(q, lambda: e.dma_start(mk_out(), mk_in()), ins, outs, 60.0, (), "d")] = ns

    sent = [0]

    def send(o, i, peer, sem, cast=None):
        rid, pid, _ = topo.addr(peer)
        m = topo.mask(core, peer)
        sent[0] += len(topo.engines(core, peer))
        return add("G", lambda: g.remote_dma(real(o, cast), real(i, cast), T.sem[sem], T.sem.sent, pid, rid, m), [i], [], 300.0, (), "r")

    def bank(b, n=C, p0=0, p1=128):
        return ("ps", p0, p1, 512 * b, 512 * b + n, 1)

    def third(b, k):
        return ("ps", 0, 128, 512 * b + W3 * k, 512 * b + W3 * k + W3, 1)

    def half(name, k):
        return v(name, CUT[k], CUT[k + 1])

    def quant_half(q, s, i, k):
        quant(half(q, k), half(s, k), v(i, 4 * CUT[k], 4 * CUT[k + 1]))

    def odd(name):
        return v(name, 1, None, 2)

    def even(name):
        return v(name, 0, None, 2)

    def ends(name):
        return v(name, 31, None, 32)

    def starts(name):
        return v(name, 0, None, 32)

    def slot(name, s, first=0):
        return v(name, 32 * s + first, 32 * s + 32)

    dma("S", lambda: T.ut[:], lambda: T.u[:], [], [v("ut")], LOAD + 500)
    for k in range(2):
        dma("Y", lambda k=k: T.pr[16 * k:16 * k + 16, 0:24], lambda: T.p0[:], [], [v("pr", 0, 24, 1, 16 * k, 16 * k + 16)])
        dma("S", lambda k=k: T.pr[16 * k:16 * k + 16, 24:48], lambda: T.p1[:], [], [v("pr", 24, 48, 1, 16 * k, 16 * k + 16)])
    for k in range(2):
        dma("Y", lambda k=k: T.xt[:, 4 * CUT[k]:4 * CUT[k + 1]], lambda k=k: T.x[:, 4 * CUT[k]:4 * CUT[k + 1]], [], [v("xt", 4 * CUT[k], 4 * CUT[k + 1])],
            LOAD + 900)

    fill(v("ones"), 1.0)
    fill(v("eye"), 32.0)
    loads = len(ops)
    iota(col("pi", 0), [[0, 1]], 0, 1)
    iota(v("pj", 0, 8), [[0, 2], [64, 2], [0, 2]], 0, 0)
    select(v("eye"), v("eye"), [[-1, 528]], A.is_equal, 3, 4)
    iota(v("colc"), [[0, 2], [32, 6], [0, 2]], -HC, 0)
    for name, n, w in (("m32", 32, 192), ("m16", 16, K)):
        fill(v(name, 0, w), 1.0)
        fill(v(name, 0, w, n), 0.0)
    const(v("m16", K), 1.0)
    const(v("m16", K, None, 16), 0.0)
    scan(v("fi"), v("m32"), v("m32"), A.mult, A.add)
    scan(v("dm"), v("m16", 0, K), v("m16", 0, K), A.mult, A.add)
    for b in range(3):
        act(v("flo", 64 * b, 64 * b + 64), v("fi", 64 * b, 64 * b + 64), 1.0, 32.0 * b)
    for k, (c, op) in enumerate(((15, A.bitwise_and), (31, A.bitwise_and), (6, A.logical_shift_right), (16, A.bitwise_and),
                                 (1, A.bitwise_and), (14, A.bitwise_and))):
        ts(col("pi", k + 1), col("pi", 0), c, op)
    copy(v("uoff"), v("pj", 0, 8))
    copy(v("pf", 0, 7), v("pi", 0, 7))
    PR, PI, PQ, PSB, PX, P2B = [col("pf", k) for k in range(1, 7)]
    R2, R21, Q192, ROOT, GE, GO, IDH, F31, F192 = [col("pf", k) for k in range(8, 17)]
    ts(col("aux", 0), P2B, 4.0, A.min, 2.0, A.mult)
    ts(col("aux", 1), PQ, 12.0, A.mult, PX, A.add)
    ts(Q192, PQ, -192.0, A.mult)
    ts(col("aux", 2), PSB, 0.125, A.mult, col("aux", 0), A.add)
    ts(col("sel", 0), col("aux", 1), col("aux", 2), A.add)
    act(R2, PR, 2.0)
    act(R21, PR, 2.0, 1.0)
    for q in range(1, 4):
        copy(on(v("pr"), q), on(v("pr"), 0))
    for k in range(2):
        ts(v("lp", 16 * k, 16 * k + 16), ind(v("pr", 24 * k, 24 * k + 24), col("sel", 0)), Q192, A.add)
    LP0, LP1 = v("lp", 0, 6), v("lp", 16, 22)
    quant(v("qu"), v("su"), v("ut"))
    pick(v("qup"), ind(v("qu"), v("uoff")))
    add("S", lambda: g.scalar.activation(real(v("sup")), real(ind(v("su"), v("uoff"))), FN.Copy), [ind(v("su"), v("uoff"))], [v("sup")], 260.0)

    def scores(k):
        mm(bank(k, CUT[k + 1] - CUT[k]), "up", 0, half("qx", k), half("sx", k))
        for qs in range(2):
            c0, c1 = max(CUT[k], HC * qs), min(CUT[k + 1], HC * qs + HC)
            if c0 < c1:
                (copy if k else act)(v("ssb", c0 - HC * qs, c1 - HC * qs, 1, 64 * qs, 64 * qs + 64),
                                     ("ps", 64 * qs, 64 * qs + 64, 512 * k + c0 - CUT[k], 512 * k + c1 - CUT[k], 1))

    for k in range(2):
        quant_half("qx", "sx", "xt", k)
        scores(k)
    dma("Y", lambda: T.qw[:].bitcast(dt.uint8), lambda: T.wc[:], [v("xt")], [v("qw")])
    dma("Y", lambda: T.sw[:], lambda: T.ws[:], [v("xt")], [v("sw")])
    dma("Y", lambda: T.vt[:], lambda: T.v[:], [v("xt")], [v("vt")])
    ts(v("tmp", 0, 96), v("fi", 0, 96), R2, A.is_equal, 64.0, A.mult)
    ts(v("tmp", 96, 192), v("fi", 0, 96), R21, A.is_equal, 128.0, A.mult)
    fill(v("tmp", 0, 96, 32), 0.0)
    tt(v("fb", 0, 96), v("tmp", 0, 96), v("tmp", 96, 192), A.add)
    act(v("fb", 96, 192), v("fb", 0, 96))
    ts(ROOT, PR, 0.0, A.is_equal, -2048.0, A.mult)
    act(v("tmp2", 0, 96), ind(v("flo"), LP1))
    act(odd("d1p"), v("tmp2", 0, 96))
    act(v("tmp5"), ind(v("fb"), LP1))
    tt(even("d1p"), ind(v("flo"), LP0), v("tmp2", 0, 96), A.subtract)
    tt(even("d1b"), ind(v("fb"), LP0), v("tmp5"), A.subtract)
    act(v("fc"), v("fb", 0, 96))
    tt(odd("d1b"), ind(v("fb"), LP1), v("fc"), A.add)
    ts(v("gtm"), v("dm", 0, 96), PR, A.is_gt)
    ts(v("tmp3", 0, K), v("dm"), PR, A.is_equal, BIG, A.mult)
    scan(v("mw"), v("m16", 0, K), v("tmp3", 0, K), A.min, A.max)
    act(v("mw", 15, None, 16), v("mw", 15, None, 16), 1.0 / BIG / SMALL)
    act(v("tmp3", 192, 288), v("tmp3", 0, 96), 1.0 / TINY)
    scan(odd("mo"), v("m16", 0, 96), v("tmp3", 192, 288), A.min, A.max)
    act(ends("mo"), ends("mo"), 1.0 / BIG / SMALL)
    act(v("tmp3", 288, 384), v("tmp3", 0, 96), 2.0 * TINY / BIG)
    tt(v("tmp2", 96, 192), even("d1p"), v("tmp3", 288, 384), A.mult)
    tt(even("mo"), v("tmp2", 96, 192), v("gtm", 0, 96), A.add)
    fill(col("cd0", 0), 0.0)
    act(v("tmp2", 192, 288), v("tmp2", 0, 96), 1.0, 0.5)
    tt(v("cd0", 2, 194, 2), v("tmp2", 192, 288), v("tmp3", 288, 384), A.mult)
    for name in ("pb", "pc", "pd", "bb", "bc"):
        const(even(name), 0.0)
    for b in range(4):
        quant(v("qe", 128 * b, 128 * b + 128), v("se", 128 * b, 128 * b + 128), v("eye", 3 - b, 515 - b))
    for e, r in enumerate((R2, R21)):
        ts(v("tmp4", 96 * e, 96 * e + 96), v("fi", 0, 96), r, A.is_equal, BIG, A.mult)
    scan(v("me"), v("m32"), v("tmp4"), A.min, A.max)
    act(ends("me"), ends("me"), 1.0 / BIG / SMALL)
    for b in range(3):
        const(v("pcc", b, 6, 3), -(32.0 + 32 * b) / 64)
    act(F192, PI, -1.0, float(HC))
    const(v("mx0"), -4096.0)
    act(v("mx0", 0, None, 64), v("ones", 0, 3), 1024.0, ROOT)
    const(v("mx1"), -4096.0)
    const(v("mx1", 0, None, 32), 1024.0)
    const(odd("m01"), 1.0)
    const(even("m01"), 0.0)
    act(v("fmi"), v("fi", 0, 32), -1.0, PI)
    act(v("cb6"), v("fi", 0, 6), -32.0, F192)
    const(v("rst"), 0.0)
    const(starts("rst"), 4096.0)
    act(GE, R2, -SG, 31 * SG + 1.0 / 128)
    act(GO, R21, -SG, 31 * SG + 1.0 / 128)
    if OPT["gg"]:
        const(v("mxg"), 4096.0)
        act(col("aux", 7), ROOT, -1.0 / 131072, GE)
        act(v("mxg", 0, 192, 64), v("ones", 0, 3), -1.0 / 128, col("aux", 7))
        act(v("mxg", 192, 288, 32), v("ones", 0, 3), -1.0 / 128, GO)
    act(IDH, PI, -SG, 31 * SG - EPS / 2)
    act(F31, PI, 1.0, -31.0)
    act(v("idr"), v("fi"), -1.0, 31.0)
    act(v("ids"), v("fi"), -SG, 31 * SG)
    act(v("idb"), v("fi"), -SG, 31 * SG)
    const(starts("dd"), 0.0)
    fill(v("gd"), 0.0)
    const(even("wd"), 0.0)
    const(v("cg0"), 0.0)
    const(even("cg1"), 0.0)
    ts(odd("cg1"), v("colc"), Q192, A.subtract, PI, A.add)
    const(v("sd"), 1.0)
    const(v("mcl"), 1.0)
    const(starts("mcl"), 0.0)
    for h in range(2):
        for c in (17, 23):
            const(on(v("mcl", c, None, 32), 2 * h + 1), 0.0)
    const(v("cd"), 0.0)
    const(v("zz"), 0.0)
    act(col("aux", 3), P2B, 0.5)
    ts(col("aux", 4), PSB, -6.0, A.mult, 64.0, A.add)
    ts(col("aux", 5), PSB, 4.0, A.mult, col("aux", 3), A.add)
    ts(col("aux", 6), PX, col("aux", 4), A.mult, col("aux", 5), A.add)
    ts(v("swp"), v("fi", 0, 16, 8), col("aux", 6), A.add)
    quant(v("qv"), v("sv"), v("vt"))
    iota(v("rs", C), [[0, 1024 - C]], 0, 0)
    for b in range(4):
        const(v("win", WIN * b + K + C, WIN * b + WIN), 0.0)
        const(v("win", WIN * b, WIN * b + K), 0.0)

    def lv(name, l, c):
        c0 = 2 * (12 * (l // 2) + l % 2) + c
        return v(name, c0, c0 + 21, 4)

    def across(l, c):
        return [(lambda name, h=h, qs=qs: on(v(name, 192 * qs + c, 192 * qs + 192, 32), 2 * h + (l > 0)), 2 * qs + h) for h in range(2) for qs in range(2)]

    def spread(l):
        c, top = ((0, 32), (0, 16), (23, 8))[l]
        for to, q in across(l, c):
            act(to("sd"), on(odd("ws%d" % l), q), 1024.0, -0.25 - top)

    def wrap(off, row, k):
        scan(v("cv", 96 * k, 96 * k + 96), row, v("mw", 0, 96), A.add, A.mult)
        ts(v(off), v("cv", 96 * k + 15, 96 * k + 96, 16), SMALL, A.mult, 0.25, A.add)

    begins = []
    for t, mask in enumerate(ROUNDS):
        begins.append(len(ops))
        peer = T.cores[rank ^ mask]
        ne = len(topo.engines(peer, core))
        qt, st, ql, sl, lo, li = ["%s%d" % (n, t) for n in ("qt", "st", "ql", "sl", "lo", "li")]
        for b in range(4):
            mm(bank(4 + b), "e", b, v("qx"), v("sx"))
            for k in range(OPT["n"]):
                act(v("tt", 4 * W3 * k + b, 4 * W3 * k + 4 * W3, 4), third(4 + b, k), 1.0 / 32)
        for k in range(3):
            quant(v(qt, 128 * k, 128 * k + 128), v(st, 128 * k, 128 * k + 128), v("tt", 512 * k, 512 * k + 512))
        tile_sent = [(send(v(ql), v(qt), peer, "big%d" % t, dt.uint8), TILE), (send(v(sl), v(st), peer, "big%d" % t), TILE)]
        for b in range(4):
            for k in range(OPT["n"]):
                act(v("win", WIN * b + K + W3 * k, WIN * b + K + W3 * k + W3), third(4 + b, k), 1.0 / 32)
        act(v("sb1"), ind(v("ssb"), LP1))
        tt(v("cd0", 1, 193, 2), ind(v("ssb"), LP0), v("sb1"), A.is_ge)
        scan(v("sca"), v("cd0", 1, 193), v("mo"), A.add, A.mult)
        ts(v("o1"), ends("sca"), SMALL, A.mult, 0.25, A.add)
        scan(v("pa"), v("cd0", 0, 192), v("d1p"), A.mult, A.add)
        scan(v("ba"), v("cd0", 0, 192), v("d1b"), A.mult, A.add)
        act(odd("pb"), ind(v("pa"), v("o1")))
        own = v("fb", 0, 96)
        if OPT["anc"]:
            act(v("p3"), ind(v("pb"), v("o1")))
            wrap("o2", odd("pb"), 3)
            wrap("o3", v("p3"), 0)
            act(v("p5"), ind(v("p3"), v("o2")))
            steps = ((odd("bb"), "ba", "o1", own), (v("b4"), "bb", "o1", own), (v("b6"), "b4", "o2", odd("ba")), (v("b8"), "b6", "o2", odd("ba")),
                     (v("b9"), "b6", "o3", odd("bb")), (v("b11"), "b8", "o3", odd("bb")), (v("b14"), "b9", "o3", odd("bb")),
                     (v("b22"), "b14", "o8", v("b8")), (odd("vv"), "b22", "o11", v("b11")))
        else:
            act(odd("pc"), ind(v("pb"), v("o1")))
            act(odd("pd"), ind(v("pc"), v("o1")))
            act(v("p5"), ind(v("pd"), v("o1")))
            wrap("o3", odd("pc"), 0)
            steps = ((odd("bb"), "ba", "o1", own), (odd("bc"), "bb", "o1", own), (v("b5"), "bc", "o1", own),
                     (v("b8"), "b5", "o3", odd("bb")), (v("b11"), "b8", "o3", odd("bb")), (v("b14"), "b11", "o3", odd("bb")),
                     (v("b22"), "b14", "o8", v("b8")), (odd("vv"), "b22", "o11", v("b11")))
        act(v("p8"), ind(v("p5"), v("o3")))
        act(v("p11"), ind(v("p8"), v("o3")))
        wrap("o8", v("p8"), 1)
        wrap("o11", v("p11"), 2)
        for o, w, off, base in steps:
            tt(o, ind(v(w), v(off)), base, A.add)
        for e in range(2):
            scan(v("pk", 96 * e, 96 * e + 96), odd("pa"), v("me", 96 * e, 96 * e + 96), A.add, A.mult)
        act(v("pc1"), ends("pk"), SMALL / 64)
        tt(v("pc2"), v("pc1"), v("pcc"), A.add)
        ts(even("vv"), odd("vv"), 96.0, A.is_ge, -128.0, A.mult)
        ts(v("b1"), odd("vv"), 96.0, A.is_ge, 64.0, A.mult)
        scan(v("se2"), v("mx0"), v("vv"), A.max, A.subtract, -4096.0)
        scan(v("so"), v("mx1"), v("b1"), A.max, A.subtract)
        if OPT["gg"]:
            act(v("vg", 1, 192, 2), odd("vv"), 1.0 / 131072)
            ts(v("vg", 0, 192, 2), odd("vv"), 96.0, A.is_ge, -1.0 / 1024, A.mult)
            ts(v("vg", 192), odd("vv"), 96.0, A.is_ge, 1.0 / 2048, A.mult)
            scan(v("gs", 0, 192), v("mxg", 0, 192), v("vg", 0, 192), A.min, A.add, 4096.0)
            scan(v("gs", 192), v("mxg", 192), v("vg", 192), A.min, A.add, 4096.0)
        scan(v("b0"), v("m01"), v("vv"), A.mult, A.add)
        for e, (src, gc) in enumerate(((odd("se2"), GE), (v("so"), GO))):
            part = v("yb", 96 * e, 96 * e + 96)
            scan(back(part), v("rst", 0, 96), back(src), A.add, A.min)
            turn(v("yrow", e, None, 2), part)
            if not OPT["gg"]:
                ts(v("gq", 96 * e, 96 * e + 96), part, -1.0 / 131072, A.mult, gc, A.add)
            else:
                scan(back(v("gq", 96 * e, 96 * e + 96)), v("m32", 0, 96), back(v("gs", 192) if e else v("gs", 1, 192, 2)), A.mult, A.max)
            turn(v("gr0", e, None, 2), v("gq", 96 * e, 96 * e + 96))
            for b in range(3):
                act(slot("ub", 3 * e + b), slot("b1", b) if e else v("b0", 64 * b + 1, 64 * b + 64, 2), col("pc2", 3 * e + b), 1.0)
            turn(v("utn", e, None, 2), v("ub", 96 * e, 96 * e + 96))
        turn(v("ybs"), v("yrow"))
        act(odd("ws0"), starts("ybs"), -1.0 / 65536, 1.0 / 64 + EPS)
        ts(odd("wd"), starts("ybs"), 0.0, A.is_le, 2.0, A.mult)
        for l in range(4):
            ws, gr = "ws%d" % l, "gr%d" % (l % 2)
            if l:
                scan(back(v("pbc")), v("rst"), back(v("sa")), A.add, A.min)
                turn(v("prow"), v("pbc"))
                tt(v("xx"), ends("sb"), odd(ws), A.add)
                copy(v("pp"), ends("sa"))
                for s in range(6):
                    ts(slot("y1", s), slot("prow", s), col("xx", s), A.min, col("pp", s), A.not_equal)
                turn(v("yt"), v("y1"))
                if l < 3:
                    tt(v("cand"), v("xx"), v("pp"), A.is_gt)
                    act(odd("wd"), v("cand"), 2.0)
                    tt(v("nn"), v("pp"), ends("sb"), A.subtract)
                    act(v("n62"), v("nn"), 1.0, 62 * SG)
            hit, op = (v("yt"), A.mult) if l else (v("yrow"), A.min)
            if l == 3:
                act(v("keep"), odd(ws), 1.0, -EPS, FN.Sign)
                for s in range(6):
                    act(slot("df", s), v("fmi"), col("keep", s), col("cb6", s))
                scan(v("cs"), hit, v("df"), op, A.max)
                for h in range(2):
                    for qs in range(2):
                        o, i = on(v("cd", 192 * qs + 16, 192 * qs + 192, 32), 2 * h + 1), on(ends("cs"), 2 * qs + h)
                        if not OPT["c3"] & 1 << 2 * h + qs:
                            act(o, i, -1.0, 192.0 * qs)
                        elif qs:
                            ts(o, i, -1.0, A.mult, 192.0, A.add)
                        else:
                            act(o, i, -1.0)
                break
            scan(v("cs"), hit, v("idr"), op, A.max)
            act(lv("cg1", l, 0), ends("cs"), 1.0, F31)
            act(lv("cg0", l, 1), odd(ws), -1.0, EPS, FN.Sign)
            spread(l)
            scan(v("ks"), hit, v(gr), op, A.max)
            if l >= OPT["cz"]:
                scan(v("cz"), hit, v("ids"), op, A.max)
            else:
                act(ends("cz"), ends("cs"), SG)
            if l == 2:
                for to, q in across(3, 18):
                    act(to("sd"), on(odd(ws), q), 1024.0, -4.25)
                    act(to("mcl"), on(v("cand"), q), 2048.0)
                for to, q in across(3, 17):
                    tt(to("sd"), on(ends("cz"), q), on(ends("ks"), q), A.subtract)
            for s in range(6):
                if s < OPT["dd"][l]:
                    ts(slot("dd", s, 1), slot("utn", s, 1), col("cs", 32 * s + 31), A.add, 0.0, A.not_equal)
                else:
                    act(slot("dd", s, 1), slot("utn", s, 1), 1.0, col("cs", 32 * s + 31), FN.Abs)
            if l:
                tt(starts(gr), v("n62"), ends("ks"), A.subtract)
            else:
                ts(starts(gr), ends("ks"), -1.0, A.mult, 63 * SG, A.add)
            act(starts("idb"), ends("cs"), -SG, 62 * SG)
            tt(even(ws), ends("cz"), ends("ks"), A.subtract)
            scan(v("sa"), v("dd"), v(gr), A.min, A.max)
            scan(v("sb"), v("dd"), v("idb"), A.min, A.max)
            scan(v("ws%d" % (l + 1)), v("wd"), v(ws), A.mult, A.add)
            if l < 2:
                ts(starts("gd"), odd("ws%d" % (l + 1)), 0.5, A.mult, IDH, A.add)
                scan(v("gb"), v("m32"), v("gd"), A.mult, A.add)
                turn(v("gr%d" % (1 - l % 2)), v("gb"))
        for a in range(2):
            scan(v("cg2", 24 * a, 24 * a + 24), v("cg0", 24 * a, 24 * a + 24), v("cg1", 24 * a, 24 * a + 24), A.mult, A.add)
            for h in range(2):
                for qs in range(2):
                    act(on(v("cd", 192 * qs, 192 * qs + 192, 16 << a), 2 * h + a), on(v("cg2", 24 * a + 1, 24 * a + 24, 2 << a), 2 * qs + h))
        scan(v("cbs"), v("m16"), v("cd"), A.mult, A.add)
        turn(v("cf"), v("cbs"))
        scan(v("sbs"), v("mcl"), v("sd"), A.mult, A.add)
        turn(v("sf"), v("sbs"))
        if OPT["eqt"]:
            act(v("eqa"), v("sbs"), 1024.0, 0.0, FN.Abs)
            act(v("eqt"), v("eqa"), -1.0, 1024.0, FN.Relu)
        else:
            ts(v("eqt"), v("sbs"), 0.0, A.is_equal, 1024.0, A.mult)
        act(v("sgn"), v("sf"), 1.0, -0.5, FN.Sign, col("cnt", 0))
        ts(v("eq2"), v("sf"), 0.0, A.is_equal, 2.0, A.mult)
        scan(v("p2"), v("eq2"), v("ones"), A.add, A.mult, col("cnt", 0))
        turn(v("p2t"), v("p2"))
        scan(v("rs", 0, C), v("eqt"), v("p2t"), A.add, A.min)
        turn(v("t1", 0, 32), ends("rs"))
        for h in range(2):
            turn(on(v("t1", 32, 64), 2 * h + 1), on(v("rs", 22, None, 32), 2 * h + 1))
            turn(on(v("t1", 32, 64), 2 * h), on(v("rs", 16, None, 32), 2 * h + 1))
        turn(v("t2", 64, 96), v("t1", 16, 48))
        turn(v("t2", 0, 64), v("t1"))
        ts(v("opl"), ind(v("t2"), v("swp")), 0.5, A.mult, 191.25, A.add)
        for b in range(4):
            mm(bank(b), "e", b, v(ql), v(sl), waits=[("big%d" % t, 2 * ne)], behind=tile_sent)
            for k in range(OPT["n"]):
                act(v("gall", C * b + W3 * k, C * b + W3 * k + W3), third(b, k), 1.0 / 64)
        for k in (1, 0):
            for b in range(4):
                mm(bank(4 * k + b, CUT[k + 1] - CUT[k]), "e", b, half("qx", k), half("sx", k), True, False)
        copy(ind(v("cw"), v("opl", 0, 24)), v("cf"))
        scan(v("csw"), v("cw", 0, K), v("mw"), A.add, A.mult)
        ts(v(lo), v("csw", 15, None, 16), SMALL, A.mult, HC + 0.25, A.add)
        list_sent = send(v(li), v(lo), peer, "lst%d" % t)
        for b in range(4):
            o, i = v("ee", K * b, K * b + K), ind(v("win", WIN * b + K, WIN * b + WIN), v(lo))
            if b in LATE:
                continue
            if b in OPT["ee"]:
                ts(o, i, 0.5, A.mult)
            else:
                act(o, i, 0.5)
        for a in range(2):
            act(v("zz", 32 * a, 32 * a + 12), v("cd", 16 * a, None, 32))
        turn(v("z1"), v("zz"))
        turn(v("z2", 64, 96), v("z1", 16, 48))
        turn(v("z2", 0, 64), v("z1"))
        act(v("kk"), ind(v("t2"), v("swp")), 0.5, 191.0 - K - HC)
        act(v("ky"), ind(v("t2"), v("swp")), 800.0, 1600.0 * (191.5 - K) - K - HC)
        tt(v("km"), v("kk"), v("ky"), A.max)
        tt(v("kn"), ind(v("z2"), v("swp")), v("km"), A.min)
        ts(v("ozl"), v("kn", 0, 24), K + HC + 0.25, A.add)
        if LATE:
            tt(v("kl"), ind(v("z2"), v("swp")), v("ky"), A.max)
            ts(v("ofl"), v("kl", 0, 24), float(HC), A.min, K + HC + 0.25, A.add)
        def places(k):
            return v("ozl", CUT[k] // 16, CUT[k + 1] // 16)

        for b in LATE:
            act(v("fm", C * (b - LATE[0]), C * (b - LATE[0]) + C), ind(v("win", WIN * b, WIN * b + WIN), v("ofl")), 0.5)
        arrival = {"waits": [("lst%d" % t, ne)], "behind": [(list_sent, LIST)]}
        last = {"V": [], "S": []}

        def in_turn():
            ops[-1][7].extend(last[ops[-1][0]])
            last[ops[-1][0]] = [(len(ops) - 1, 0.0)]

        for b in range(4):
            o, i = v("win", WIN * b, WIN * b + K), ind(v("gall", C * b, C * b + C), v(li))
            if b in LATE:
                act(o, i, **arrival)
            else:
                tt(o, i, v("ee", K * b, K * b + K), A.add, **arrival)
            in_turn()
        for k, b in OPT["order"]:
            if b < 4:
                o = v("zt", 4 * CUT[k] + b, 4 * CUT[k + 1], 4)
                i = ind(v("win", WIN * b, WIN * b + WIN), places(k))
                if b in LATE:
                    tt(o, i, v("fm", C * (b - LATE[0]) + CUT[k], C * (b - LATE[0]) + CUT[k + 1]), A.add)
                else:
                    (copy if 4 * k + b in OPT["z"] else act)(o, i)
            else:
                quant_half("qz", "sz", "zt", k)
            in_turn()
            if b == 4:
                for c in range(4):
                    mm(bank(4 * k + c, CUT[k + 1] - CUT[k]), "w", c, half("qz", k), half("sz", k), False, True)
        for k in range(2):
            c0, c1 = CUT[k], CUT[k + 1]
            for b in range(4):
                o = v("xn", 4 * c0 + b, 4 * c1, 4)
                if 4 * k + b in OPT["x"]:
                    ts(o, bank(4 * k + b, c1 - c0), 1.0 / 32, A.mult)
                else:
                    act(o, bank(4 * k + b, c1 - c0), 1.0 / 32)
            quant_half("qx", "sx", "xn", k)
            if t < 2:
                scores(k)
            else:
                mm(bank(k, c1 - c0), "v", 0, half("qx", k), half("sx", k))
                dma("Y", lambda c0=c0, c1=c1: T.oc[:, 4 * c0:4 * c1], lambda c0=c0, c1=c1: T.qx[:, c0:c1].bitcast(dt.uint8), [half("qx", k)], [])
                (copy if k else act)(half("yo", k), bank(k, c1 - c0))
                dma("Y" if k else "S", lambda c0=c0, c1=c1: T.y[:, c0:c1], lambda c0=c0, c1=c1: T.yo[:, c0:c1], [half("yo", k)], [])

    act(v("clo"), v("cf"), 1.0, float(HC))
    dma("Y", lambda: T.cl[:], lambda: T.clo[0:128:16, :], [v("clo")], [])
    for k in range(4):
        dma("S" if k % 2 else "Y", lambda k=k: T.osc[4 * k:4 * k + 4, :], lambda k=k: T.sx[32 * k:32 * k + 4, :], [v("sx")], [])

    used = {}
    deps = []
    for n, op in enumerate(ops):
        q, r, w = op[0], op[2], op[3]
        hits = set()
        for mine, writes in ((r, False), (w, True)):
            for a in mine:
                for m, b, wrote in used.get(a[0], ()):
                    if (writes or wrote or a[0] == "ps") and _meet(a, b):
                        hits.add(m)
        deps.append(hits)
        if op[5] != "r":
            for mine, writes in ((r, False), (w, True)):
                for a in mine:
                    used.setdefault(a[0], []).append((n, a, writes))

    def gap(m, n):
        if ops[m][5] == "d":
            return lands[m]
        return 0.0 if ops[m][0] == "P" and ops[n][0] == "P" else OPT["wake"]

    edges = [[(m, gap(m, n)) for m in deps[n]] + ops[n][7] for n in range(len(ops))]
    after = [LOAD if op[5] == "d" else 0.0 for op in ops]

    def turned(tile):
        later = [[] for _ in ops]
        for n in range(len(ops)):
            for m, d in edges[n]:
                later[m].append((n, {TILE: tile * TILE, LIST: LIST * OPT["back"]}.get(d, d)))
        return later

    def play(order, far, slow):
        free, end = {q: 0.0 for q in "VSPGY"}, {}
        for n in order:
            s = max([free[ops[n][0]]] + [end[m] + {TILE: far * TILE, LIST: far * LIST * 0.85}.get(d, d) for m, d in edges[n]])
            free[ops[n][0]] = end[n] = s + slow * ops[n][6]
        return max(end[n] + after[n] for n in end)

    def lay(turns, links, least):
        busy = {q: [] for q in "VSPGY"}
        end = {}
        for n in turns:
            s = max([least[n]] + [end[m] + d for m, d in links[n]])
            row = busy[ops[n][0]]
            k, hi = 0, len(row)
            while k < hi:
                if row[(k + hi) // 2][1] <= s:
                    k = (k + hi) // 2 + 1
                else:
                    hi = (k + hi) // 2
            while k < len(row) and row[k][0] < s + ops[n][6] - 1e-6:
                s = max(s, row[k][1])
                k += 1
            end[n] = s + ops[n][6]
            row.insert(k, (s, end[n]))
        return end

    if not _ORDER:
        later = turned(OPT["tile"])
        kin = [n - max([r for r in begins if r <= n] or [-len(ops)]) for n in range(len(ops))]

        def arrange(urge):
            tail = [0.0] * len(ops)
            for n in range(len(ops) - 1, -1, -1):
                tail[n] = ops[n][6] + urge.get(kin[n], 0.0) + max([after[n]] + [d + tail[k] for k, d in later[n]])
            found = []
            for _ in range(OPT["passes"]):
                end = lay(sorted(range(len(ops)), key=lambda n: (n >= loads, -tail[n] if n >= loads else n, n)), edges, [0.0] * len(ops))
                order = sorted(range(len(ops)), key=lambda n: (end[n] - ops[n][6], n))
                found.append((play(order, 1.0, 1.0) + play(order, 1.5, 1.1) + play(order, 0.8, 1.3), order))
                tail = lay(sorted(range(len(ops)), key=lambda n: (-end[n], -n)), later, after)
            return min(found)

        urge, seed = {}, 1
        best = arrange(urge)
        for _ in range(OPT["tries"]):
            trial = dict(urge)
            for _ in range(OPT["many"]):
                seed = seed * 48271 % 2147483647
                trial[kin[seed % len(ops)]] = float(seed // len(ops) % OPT["amp"])
            found = arrange(trial)
            if found[0] < best[0]:
                best, urge = found, trial
        _ORDER.extend(best[1])
    order = list(_ORDER)

    place = {n: k for k, n in enumerate(order)}
    seen = {}
    need = set()
    keep = {}
    for n in order:
        q = ops[n][0]
        keep[n] = []
        for m in sorted(deps[n], key=lambda m: -place[m]):
            if q == "P" and ops[m][0] == "P":
                continue
            key = (q, ops[m][0]) if ops[m][5] == "c" else (q, m)
            if seen.get(key, -1) < place[m]:
                seen[key] = place[m]
                keep[n].append(m)
                need.add(m)
    queue = {"V": g.vector, "S": g.scalar, "P": g.tensor, "G": g, "Y": g.sync}
    count = {"V": 0, "S": 0, "P": 0, "G": 0}
    mark = {}
    waited = set()
    ndma = 0
    for n in order:
        q, call, waits, kind = ops[n][0], ops[n][1], ops[n][4], ops[n][5]
        for m in keep[n]:
            queue[q].wait_ge(T.sem[mark[m][0]], mark[m][1])
        for s, val in waits:
            if (q, s) not in waited:
                waited.add((q, s))
                queue[q].wait_ge(T.sem[s], val)
        done = call()
        if kind == "d":
            mark[n] = ("d%d" % ndma, 16)
            ndma += 1
            done.then_inc(T.sem[mark[n][0]], 16)
        elif kind == "c" and n in need:
            count[q] += 1
            mark[n] = ("c" + q, count[q])
            done.then_inc(T.sem["c" + q], 1)
    for k in range(ndma):
        g.sync.wait_ge(T.sem["d%d" % k], 16)
    g.wait_ge(T.sem.sent, sent[0])
